import numpy as np
import ml_dtypes


def mxq(x, axis, fmt="e4m3"):
    dtype, down = {"e4m3": (ml_dtypes.float8_e4m3fn, 7), "e5m2": (ml_dtypes.float8_e5m2, 14)}[fmt]
    v = np.moveaxis(np.asarray(x, np.float32).astype(ml_dtypes.bfloat16).astype(np.float64), axis, -1)
    blocks = v.reshape(v.shape[:-1] + (-1, 32))
    amax = np.abs(blocks).max(-1, keepdims=True)
    byte = np.maximum(np.where(amax > 0, np.frexp(amax)[1] - 1 + 127, 0) - down, 1)
    scale = np.exp2(byte - 127.0)
    codes = (blocks / scale).astype(np.float32).astype(dtype).astype(np.float64)
    return np.moveaxis((codes * scale).reshape(v.shape), -1, axis)


WIDE = False


def mx_kscale(k):
    if not WIDE:
        return np.ones(k)
    levels = np.array([10, -10, 5, -5, 0])
    if k % 512:
        return np.exp2(np.random.permutation(np.resize(levels, k // 32))).repeat(32)
    a = np.empty((k // 512, 16))
    for p in range(k // 512):
        a[p, :8] = np.random.permutation(np.resize(levels, 8))
        for g in range(8):
            far = levels[np.abs(levels - a[p, g]) >= 10]
            a[p, g + 8] = far[np.random.randint(len(far))]
    return np.exp2(a.ravel()).repeat(32)


def f64(x):
    return np.asarray(x).astype(np.float64)


def striped(idx):
    return np.tile(idx.reshape(-1, 16).T, (8, 1)).astype(np.uint16)


def unstriped(offs):
    return offs[:16].T.reshape(-1).astype(np.int64)


E2M1 = np.array([0.0, 0.5, 1.0, 1.5, 2.0, 3.0, 4.0, 6.0, -0.0, -0.5, -1.0, -1.5, -2.0, -3.0, -4.0, -6.0])


def pack_weight(w, fmt):
    k, n = w.shape
    w = f64(np.asarray(w, np.float32).astype(ml_dtypes.bfloat16)).reshape(k // 32, 32, n)
    amax = np.abs(w).max(1)
    if fmt == "e4m3":
        byte = np.frexp(amax)[1] - 1 + 127 - 7
    else:
        mant, ex = np.frexp(amax / 6.0)
        byte = np.where(mant > 0.5, ex, ex - 1) + 127
    byte = np.clip(np.where(amax > 0, byte, 1), 1, 254)
    scaled = (w * np.exp2(127.0 - byte)[:, None, :]).reshape(k, n).astype(np.float32)
    by_word = np.ascontiguousarray(scaled.reshape(k // 512, 128, 4, n).transpose(0, 1, 3, 2))
    if fmt == "e4m3":
        words = by_word.astype(ml_dtypes.float8_e4m3fn).view(np.uint8)
    else:
        c = by_word.astype(ml_dtypes.float4_e2m1fn).view(np.uint8) & 0xF
        words = (c[..., 0::2] | (c[..., 1::2] << 4)).reshape(k // 512, 128, 2 * n)
    return np.ascontiguousarray(words), np.ascontiguousarray(byte.astype(np.uint8).reshape(k // 512, 16, n))


def unpack_weight(words, scales, fmt):
    g, _, n = scales.shape
    words = np.ascontiguousarray(words).reshape(g, 128, n, -1)
    if fmt == "e4m3":
        vals = words.view(ml_dtypes.float8_e4m3fn).astype(np.float64)
    else:
        nib = np.empty((g, 128, n, 4), np.uint8)
        nib[..., 0::2] = words & 0xF
        nib[..., 1::2] = words >> 4
        vals = E2M1[nib]
    vals = vals * np.repeat(np.exp2(scales.astype(np.float64) - 127.0), 8, axis=1)[..., None]
    return vals.transpose(0, 1, 3, 2).reshape(g * 512, n)


def gelu(v):
    return 0.5 * v * (1.0 + np.tanh(np.sqrt(2.0 / np.pi) * (v + 0.044715 * v**3)))


K, H, T, S, P = 1024, 1024, 4096, 1024, 512

def setup_inputs():
    n = np.random.standard_normal
    s = mx_kscale(K)[:, None]
    u = mx_kscale(H)[:, None]
    tab_words, tab_scales = pack_weight(n((K, T)) * s, "e4m3")
    c4_words, c4_scales = pack_weight(0.6 * n((H, K)) / np.sqrt(H) * u / s.T, "e2m1")
    return {
        "tab_words": tab_words, "tab_scales": tab_scales,
        "w": (n((K, H)) / np.sqrt(K) * u.T / s).astype(np.float32),
        "c4_words": c4_words, "c4_scales": c4_scales,
        "fade": (-0.3 * np.exp(0.3 * n(H)) / u[:, 0]).astype(np.float32),
        "lift": (np.exp(0.3 * n(H)) / u[:, 0] ** 2).astype(np.float32),
        "back": (np.exp(0.3 * n(K)) * s[:, 0]).astype(np.float32),
        "offs": striped(np.random.permutation(T)[:S]),
        "pos1": striped(np.random.permutation(S)[:P]),
        "pos2": striped(np.random.permutation(S)[:P]),
        "pos3": striped(np.random.permutation(S)[:P]),
    }

def reference(tab_words, tab_scales, w, c4_words, c4_scales, fade, lift, back, offs, pos1, pos2, pos3):
    v = unpack_weight(tab_words, tab_scales, "e4m3")[:, unstriped(offs)]
    c4 = unpack_weight(c4_words, c4_scales, "e2m1")
    h = mxq(f64(w), 0, "e4m3").T @ v
    want = h[:, unstriped(pos1)]
    repl = h[:, unstriped(pos2)]
    carr = h[:, unstriped(pos3)]
    damp = np.exp(f64(fade)[:, None] * want)
    z = f64(lift)[:, None] * (damp * repl - carr)
    zq = mxq(z, 0, "e4m3")
    wt = mxq(f64(w).T, 0, "e4m3")
    y = wt.T @ zq + c4.T @ zq
    return f64(back)[:, None] * y

@@ -1,0 +1,309 @@
+from contextlib import ExitStack
+
+import concourse.mybir as mybir
+from concourse.masks import make_identity
+
+K, H, T, S, M = 1024, 1024, 4096, 1024, 512
+FLOPS = 2 * K * H * S + 2 * 2 * H * K * M
+
+F32 = mybir.dt.float32
+BF16 = mybir.dt.bfloat16
+I32 = mybir.dt.int32
+U32 = mybir.dt.uint32
+U16 = mybir.dt.uint16
+U8 = mybir.dt.uint8
+FP8X4 = mybir.dt.float8_e4m3fn_x4
+FP4X4 = mybir.dt.float4_e2m1fn_x4
+ALU = mybir.AluOpType
+ACT = mybir.ActivationFunctionType
+
+P = 128
+PASS = 512
+BANK = 512
+WIDE = 384
+NARROW = M - WIDE
+
+
+def tile_list_spice_substitution_kernel(
+    tc, tab_words, tab_scales, w, c4_words, c4_scales, fade, lift, back, offs, pos1, pos2, pos3, out
+):
+    nc = tc.nc
+    with ExitStack() as ctx:
+        keep = ctx.enter_context(tc.tile_pool(name="keep", bufs=1))
+        ring = ctx.enter_context(tc.tile_pool(name="ring", bufs=2))
+        psum = ctx.enter_context(tc.psum_pool(name="psum", bufs=1))
+
+        def bank(i):
+            return psum.tile([P, BANK], F32, name="bank%d" % i, tag="bank%d" % i)
+
+        def kept(shape, dtype, name, tag=None):
+            return keep.tile(shape, dtype, name=name, tag=tag or name, align_bytes=64)
+
+        w_raw = {}
+
+        def load_w(a, b):
+            w_raw[a, b] = kept([P, 4, PASS], F32, "w_raw%d%d" % (a, b))
+            rows = w[PASS * a : PASS * (a + 1), PASS * b : PASS * (b + 1)]
+            nc.sync.dma_start(out=w_raw[a, b][:], in_=rows.rearrange("(p i) r -> p i r", i=4))
+
+        tab = {}
+
+        def load_tab(a):
+            tab[a] = kept([P, T], I32, "tab%d" % a, "w_raw%d0" % a)
+            nc.sync.dma_start(out=tab[a][:], in_=tab_words[a].rearrange("p t i -> p (t i)").bitcast(I32))
+
+        tab_sc = kept([P, T], U8, "tab_sc")
+        nc.vector.memset(tab_sc[:].bitcast(I32), 0)
+
+        def load_tab_scales(a):
+            for r in range(4):
+                (nc.sync if a == 0 else nc.gpsimd).dma_start(
+                    out=tab_sc[4 * a + r : P : 32, :].bitcast(I32), in_=tab_scales[a, r::4, :].bitcast(I32)
+                )
+
+        warm = kept([P, 1], F32, "warm")
+        warm_out = kept([P, 1], F32, "warm_out")
+        nc.vector.memset(warm[:], 0.0)
+        nc.scalar.activation(out=warm_out[:], in_=warm[:], func=ACT.Exp)
+
+        load_w(0, 0)
+        offs_sb = keep.tile([P, S // 16], U16, name="offs_sb")
+        nc.sync.dma_start(offs_sb[:], offs)
+        lists = []
+        for i, pos in enumerate((pos1, pos2, pos3)):
+            pos_sb = keep.tile([P, M // 16], U16, name="pos_sb%d" % i)
+            nc.sync.dma_start(pos_sb[:], pos)
+            lists.append(pos_sb)
+        fade_sb = kept([P, 2, 4], F32, "fade_sb")
+        nc.sync.dma_start(out=fade_sb[:], in_=fade.rearrange("(b p t) -> p b t", b=2, t=4))
+        lift_sb = kept([P, 2, 4], F32, "lift_sb")
+        nc.sync.dma_start(out=lift_sb[:], in_=lift.rearrange("(b p t) -> p b t", b=2, t=4))
+        load_w(1, 0)
+        load_w(0, 1)
+        load_w(1, 1)
+        load_tab_scales(0)
+        load_tab_scales(1)
+        ident = kept([P, P], F32, "ident")
+        make_identity(nc, ident[:])
+        neg_lift = kept([P, 8], F32, "neg_lift")
+        nc.vector.tensor_scalar(
+            out=neg_lift[:], in0=lift_sb[:].rearrange("p b t -> p (b t)"), scalar1=-1.0, scalar2=None, op0=ALU.mult
+        )
+
+        wk_codes, wk_sc, wr_codes, wr_sc, grouped, turned = {}, {}, {}, {}, {}, {}
+
+        def group_w(a, b):
+            g = kept([P, 4 * PASS], BF16, "grouped%d%d" % (a, b))
+            copy = nc.scalar.copy if (a, b) == (1, 1) else nc.vector.tensor_copy
+            copy(
+                out=g[:].rearrange("p (t m i) -> p m i t", t=4, i=4),
+                in_=w_raw[a, b][:].rearrange("p i (m t) -> p m i t", t=4),
+            )
+            grouped[a, b] = g
+
+        def quantise(src, width, name):
+            codes = kept([P, width], U32, name + "_codes")
+            scales = kept([P, width], U8, name + "_sc")
+            nc.vector.quantize_mx(out=codes[:].bitcast(FP8X4), scales=scales[:], in_=src)
+            return codes, scales
+
+        def quantise_wk(a, b):
+            wk_codes[a, b], wk_sc[a, b] = quantise(grouped[a, b][:], PASS, "wk%d%d" % (a, b))
+
+        def turn_w(a, b):
+            words = grouped[a, b][:].bitcast(F32).rearrange("p (t m u) -> p t m u", t=4, u=2)
+            g = kept([P, 4 * PASS], BF16, "turned%d%d" % (a, b))
+            for u in range(2):
+                ps = bank(4 + 2 * a + u)
+                for t in range(4):
+                    nc.tensor.transpose(ps[:, P * t : P * (t + 1)], words[:, t, :, u], ident[:])
+                nc.scalar.copy(
+                    out=g[:].rearrange("m (p u e t) -> m u p e t", u=2, e=2, t=4)[:, u],
+                    in_=ps[:].bitcast(BF16).rearrange("m (t p e) -> m p e t", t=4, e=2),
+                )
+            turned[a, b] = g
+
+        def quantise_wr(a, b):
+            wr_codes[a, b], wr_sc[a, b] = quantise(turned[a, b][:], PASS, "wr%d%d" % (a, b))
+
+        v_codes = {}
+
+        def gather_words(a, half):
+            v_codes[a, half] = kept([P, BANK], U32, "v%d%d" % (a, half))
+            cols = offs_sb[:, 32 * half : 32 * (half + 1)]
+            nc.vector.tensor_copy(out=v_codes[a, half][:], in_=tab[a][:].bitcast(U32).indirect(cols))
+
+        v_sc = kept([P, S], U8, "v_sc")
+
+        for b in range(2):
+            for a in range(2):
+                group_w(a, b)
+                quantise_wk(a, b)
+            for a in range(2):
+                turn_w(a, b)
+                quantise_wr(a, b)
+        load_tab(0)
+        load_tab(1)
+        c4_sc = kept([P, 2, K], U8, "c4_sc", "grouped10")
+        nc.vector.memset(c4_sc[:].rearrange("p b n -> p (b n)").bitcast(I32), 0)
+        c4 = kept([P, 2, 2 * K], U8, "c4", "w_raw11")
+        nc.sync.dma_start(out=c4[:].bitcast(I32), in_=c4_words.rearrange("b p c -> p b c").bitcast(I32))
+        for q in range(4):
+            nc.sync.dma_start(
+                out=c4_sc[32 * q : 32 * q + 4, :, :].bitcast(I32),
+                in_=c4_scales[:, 4 * q : 4 * q + 4, :].rearrange("b r n -> r b n").bitcast(I32),
+            )
+        back_sb = kept([P, 8], F32, "back_sb", "w_raw01")
+        with nc.allow_non_contiguous_dma(reason="one factor for each output row"):
+            nc.sync.dma_start(out=back_sb[:], in_=back.rearrange("(j p) -> p j", p=P))
+
+        nc.vector.tensor_copy(out=v_sc[:], in_=tab_sc[:].indirect(offs_sb[:]))
+        for a in range(2):
+            for half in range(2):
+                gather_words(a, half)
+
+        h = {}
+
+        def make_h(k):
+            b, t = divmod(k, 4)
+            h[k] = kept([P, S], F32, "h%d" % k)
+            for half in range(2):
+                ps = bank(2 * (k % 2) + half)
+                for a in range(2):
+                    cols = slice(P * t, P * (t + 1))
+                    nc.tensor.matmul_mx(
+                        out=ps[:],
+                        lhsT=wk_codes[a, b][:, cols].bitcast(FP8X4),
+                        lhsT_scale=wk_sc[a, b][:, cols],
+                        rhs=v_codes[a, half][:].bitcast(FP8X4),
+                        rhs_scale=v_sc[4 * a :, BANK * half : BANK * (half + 1)],
+                        start=(a == 0),
+                        stop=(a == 1),
+                    )
+                dst = h[k][:, BANK * half : BANK * (half + 1)]
+                if k == 0 and half == 1:
+                    nc.vector.tensor_copy(out=dst, in_=ps[:])
+                else:
+                    nc.scalar.copy(out=dst, in_=ps[:])
+
+        spans = ((0, WIDE), (WIDE, NARROW))
+        want, damp, prod, planes, z_codes, z_sc = {}, {}, {}, {}, {}, {}
+
+        def picked(s, k, which):
+            first, width = spans[s]
+            return h[k][:].indirect(lists[which][:, first // 16 : (first + width) // 16])
+
+        def pick_want(s, k):
+            want[s, k] = ring.tile([P, spans[s][1]], F32, name="want", tag="want")
+            nc.vector.tensor_copy(out=want[s, k][:], in_=picked(s, k, 0))
+
+        def make_damp(s, k):
+            b, t = divmod(k, 4)
+            damp[s, k] = ring.tile([P, spans[s][1]], F32, name="damp", tag="damp")
+            nc.scalar.activation(out=damp[s, k][:], in_=want[s, k][:], func=ACT.Exp, scale=fade_sb[:, b, t : t + 1])
+
+        def pick_repl(s, k):
+            prod[s, k] = ring.tile([P, spans[s][1]], F32, name="prod", tag="prod")
+            nc.vector.tensor_tensor(prod[s, k][:], picked(s, k, 1), damp[s, k][:], ALU.mult)
+
+        def pick_carr(s, k):
+            b, t = divmod(k, 4)
+            width = spans[s][1]
+            diff = ring.tile([P, width], F32, name="diff", tag="diff")
+            nc.vector.tensor_tensor(diff[:], picked(s, k, 2), prod[s, k][:], ALU.subtract)
+            if t == 0:
+                planes[s, b] = kept([P, 4, width], BF16, "planes%d%d" % (s, b))
+            nc.scalar.activation(out=planes[s, b][:, t, :], in_=diff[:], func=ACT.Copy, scale=neg_lift[:, k : k + 1])
+
+        def quantise_z(s, b, piece):
+            width = spans[s][1]
+            if piece == 0:
+                z_codes[s, b] = kept([P, width], U32, "z_codes%d%d" % (s, b))
+                z_sc[s, b] = kept([P, width], U8, "z_sc%d%d" % (s, b))
+            cols = slice(P * piece, P * (piece + 1))
+            woven = ring.tile([P, 4 * P], BF16, name="woven", tag="woven", align_bytes=64)
+            nc.scalar.copy(
+                out=woven[:].rearrange("p (c i t) -> p c t i", i=4, t=4),
+                in_=planes[s, b][:, :, cols].rearrange("p t (c i) -> p c t i", i=4),
+            )
+            nc.vector.quantize_mx(out=z_codes[s, b][:, cols].bitcast(FP8X4), scales=z_sc[s, b][:, cols], in_=woven[:])
+
+        def second_passes(s, b, j, ps, at, start, stop):
+            width = spans[s][1]
+            a, jj = divmod(j, 4)
+            n_cols = slice(P * jj, P * (jj + 1))
+            passes = []
+            for first, n in ((0, 256), (256, 128)) if width == WIDE else ((0, 128),):
+                passes.append((wr_codes[a, b][:, n_cols].bitcast(FP8X4), wr_sc[a, b][:, n_cols], first, n))
+            for first in range(0, width, P):
+                passes.append(
+                    (c4[:, b, 2 * P * j : 2 * P * (j + 1)].bitcast(FP4X4), c4_sc[:, b, P * j : P * (j + 1)], first, P)
+                )
+            for i, (codes, scales, first, n) in enumerate(passes):
+                nc.tensor.matmul_mx(
+                    out=ps[:, at + first : at + first + n],
+                    lhsT=codes,
+                    lhsT_scale=scales,
+                    rhs=z_codes[s, b][:, first : first + n].bitcast(FP8X4),
+                    rhs_scale=z_sc[s, b][:, first : first + n],
+                    start=(start and i == 0),
+                    stop=(stop and i == len(passes) - 1),
+                )
+
+        def finish_wide(j):
+            ps = bank(4 + j % 4)
+            second_passes(0, 0, j, ps, 0, True, False)
+            second_passes(0, 1, j, ps, 0, False, True)
+            res = kept([P, WIDE], F32, "res%d" % j)
+            nc.scalar.activation(out=res[:], in_=ps[:, 0:WIDE], func=ACT.Copy, scale=back_sb[:, j : j + 1])
+            nc.sync.dma_start(out=out[P * j : P * (j + 1), 0:WIDE], in_=res[:])
+
+        steps = [(s, k) for s in range(2) for k in range(8)]
+        make_h(0)
+        make_h(1)
+        pick_want(*steps[0])
+        pick_want(*steps[1])
+        make_damp(*steps[0])
+        narrow_banks = []
+        for i, (s, k) in enumerate(steps):
+            if i + 2 < 8:
+                make_h(i + 2)
+            pick_repl(s, k)
+            if i + 2 < len(steps):
+                pick_want(*steps[i + 2])
+            if i + 1 < len(steps):
+                make_damp(*steps[i + 1])
+            pick_carr(s, k)
+            if 4 <= i < 7:
+                quantise_z(0, 0, i - 4)
+            if i == 7:
+                for piece in range(3):
+                    quantise_z(0, 1, piece)
+            if i == 11:
+                quantise_z(1, 0, 0)
+            if 9 <= i:
+                finish_wide(i - 9)
+            if i == 12:
+                for pair in range(4):
+                    ps = bank(pair)
+                    narrow_banks.append(ps)
+                    second_passes(1, 0, 2 * pair, ps, 0, True, False)
+                    second_passes(1, 0, 2 * pair + 1, ps, NARROW, False, False)
+        finish_wide(7)
+        quantise_z(1, 1, 0)
+        for pair in range(4):
+            ps = narrow_banks[pair]
+            second_passes(1, 1, 2 * pair, ps, 0, False, False)
+            second_passes(1, 1, 2 * pair + 1, ps, NARROW, False, True)
+            res = kept([P, 2, NARROW], F32, "res_narrow%d" % pair)
+            for e in range(2):
+                j = 2 * pair + e
+                src = ps[:, NARROW * e : NARROW * (e + 1)]
+                if pair % 2 == 0:
+                    nc.scalar.activation(out=res[:, e, :], in_=src, func=ACT.Copy, scale=back_sb[:, j : j + 1])
+                else:
+                    nc.vector.tensor_scalar(
+                        out=res[:, e, :], in0=src, scalar1=back_sb[:, j : j + 1], scalar2=None, op0=ALU.mult
+                    )
+            rows = out[2 * P * pair : 2 * P * (pair + 1), WIDE:M]
+            nc.sync.dma_start(out=rows.rearrange("(e p) m -> p e m", p=P), in_=res[:])

@@ -22,6 +22,14 @@ PASS = 512
 BANK = 512
 WIDE = 384
 NARROW = M - WIDE
+ON_VECTOR = ()
+WEAVE_V = ((0, 1, 1), (0, 1, 2))
+DIRECT = (0, 1)
+EARLY = True
+GATE = False
+PB = 2
+GROUP_S = ((1, 1),)
+H0V = False
 
 
 def tile_list_spice_substitution_kernel(
@@ -39,34 +47,25 @@ def tile_list_spice_substitution_kernel(
         def kept(shape, dtype, name, tag=None):
             return keep.tile(shape, dtype, name=name, tag=tag or name, align_bytes=64)
 
-        w_raw = {}
-
-        def load_w(a, b):
-            w_raw[a, b] = kept([P, 4, PASS], F32, "w_raw%d%d" % (a, b))
-            rows = w[PASS * a : PASS * (a + 1), PASS * b : PASS * (b + 1)]
-            nc.sync.dma_start(out=w_raw[a, b][:], in_=rows.rearrange("(p i) r -> p i r", i=4))
-
-        tab = {}
-
-        def load_tab(a):
-            tab[a] = kept([P, T], I32, "tab%d" % a, "w_raw%d0" % a)
-            nc.sync.dma_start(out=tab[a][:], in_=tab_words[a].rearrange("p t i -> p (t i)").bitcast(I32))
-
         tab_sc = kept([P, T], U8, "tab_sc")
         nc.vector.memset(tab_sc[:].bitcast(I32), 0)
-
-        def load_tab_scales(a):
-            for r in range(4):
-                (nc.sync if a == 0 else nc.gpsimd).dma_start(
-                    out=tab_sc[4 * a + r : P : 32, :].bitcast(I32), in_=tab_scales[a, r::4, :].bitcast(I32)
-                )
-
+        for q in range(4):
+            nc.gpsimd.dma_start(
+                out=tab_sc[32 * q : 32 * q + 8, :].bitcast(I32),
+                in_=tab_scales[:, 4 * q : 4 * q + 4, :].bitcast(I32),
+            )
         warm = kept([P, 1], F32, "warm")
         warm_out = kept([P, 1], F32, "warm_out")
         nc.vector.memset(warm[:], 0.0)
         nc.scalar.activation(out=warm_out[:], in_=warm[:], func=ACT.Exp)
 
-        load_w(0, 0)
+        w_raw, tab = {}, {}
+
+        def load_w(a):
+            w_raw[a] = kept([P, 4, H], F32, "w_raw%d" % a)
+            nc.sync.dma_start(out=w_raw[a][:], in_=w[PASS * a : PASS * (a + 1), :].rearrange("(p i) r -> p i r", i=4))
+
+        load_w(0)
         offs_sb = keep.tile([P, S // 16], U16, name="offs_sb")
         nc.sync.dma_start(offs_sb[:], offs)
         lists = []
@@ -78,11 +77,8 @@ def tile_list_spice_substitution_kernel(
         nc.sync.dma_start(out=fade_sb[:], in_=fade.rearrange("(b p t) -> p b t", b=2, t=4))
         lift_sb = kept([P, 2, 4], F32, "lift_sb")
         nc.sync.dma_start(out=lift_sb[:], in_=lift.rearrange("(b p t) -> p b t", b=2, t=4))
-        load_w(1, 0)
-        load_w(0, 1)
-        load_w(1, 1)
-        load_tab_scales(0)
-        load_tab_scales(1)
+        load_w(1)
+
         ident = kept([P, P], F32, "ident")
         make_identity(nc, ident[:])
         neg_lift = kept([P, 8], F32, "neg_lift")
@@ -94,15 +90,15 @@ def tile_list_spice_substitution_kernel(
 
         def group_w(a, b):
             g = kept([P, 4 * PASS], BF16, "grouped%d%d" % (a, b))
-            copy = nc.scalar.copy if (a, b) == (1, 1) else nc.vector.tensor_copy
+            copy = nc.scalar.copy if (a, b) in GROUP_S else nc.vector.tensor_copy
             copy(
                 out=g[:].rearrange("p (t m i) -> p m i t", t=4, i=4),
-                in_=w_raw[a, b][:].rearrange("p i (m t) -> p m i t", t=4),
+                in_=w_raw[a][:, :, PASS * b : PASS * (b + 1)].rearrange("p i (m t) -> p m i t", t=4),
             )
             grouped[a, b] = g
 
-        def quantise(src, width, name):
-            codes = kept([P, width], U32, name + "_codes")
+        def quantise(src, width, name, tag=None):
+            codes = kept([P, width], U32, name + "_codes", tag)
             scales = kept([P, width], U8, name + "_sc")
             nc.vector.quantize_mx(out=codes[:].bitcast(FP8X4), scales=scales[:], in_=src)
             return codes, scales
@@ -114,7 +110,7 @@ def tile_list_spice_substitution_kernel(
             words = grouped[a, b][:].bitcast(F32).rearrange("p (t m u) -> p t m u", t=4, u=2)
             g = kept([P, 4 * PASS], BF16, "turned%d%d" % (a, b))
             for u in range(2):
-                ps = bank(4 + 2 * a + u)
+                ps = bank((4 + 2 * (2 * a + b)) % 8 + u)
                 for t in range(4):
                     nc.tensor.transpose(ps[:, P * t : P * (t + 1)], words[:, t, :, u], ident[:])
                 nc.scalar.copy(
@@ -124,7 +120,11 @@ def tile_list_spice_substitution_kernel(
             turned[a, b] = g
 
         def quantise_wr(a, b):
-            wr_codes[a, b], wr_sc[a, b] = quantise(turned[a, b][:], PASS, "wr%d%d" % (a, b))
+            if b == 0:
+                wr_codes[a] = kept([P, 2, PASS], U32, "wr%d_codes" % a, ("w_raw0", "grouped00")[a])
+            wr_codes[a, b] = wr_codes[a][:, b, :]
+            wr_sc[a, b] = kept([P, PASS], U8, "wr%d%d_sc" % (a, b))
+            nc.vector.quantize_mx(out=wr_codes[a, b].bitcast(FP8X4), scales=wr_sc[a, b][:], in_=turned[a, b][:])
 
         v_codes = {}
 
@@ -135,32 +135,35 @@ def tile_list_spice_substitution_kernel(
 
         v_sc = kept([P, S], U8, "v_sc")
 
-        for b in range(2):
-            for a in range(2):
-                group_w(a, b)
-                quantise_wk(a, b)
-            for a in range(2):
-                turn_w(a, b)
-                quantise_wr(a, b)
-        load_tab(0)
-        load_tab(1)
+        chunks = [(a, b) for a in range(2) for b in range(2)]
+        for a, b in chunks:
+            group_w(a, b)
+            quantise_wk(a, b)
+        nc.vector.tensor_copy(out=v_sc[:], in_=tab_sc[:].indirect(offs_sb[:]))
+        turn_w(0, 0)
+        for a in range(2):
+            tab[a] = kept([P, T], I32, "tab%d" % a, ("w_raw0", "grouped00")[a])
+            nc.sync.dma_start(out=tab[a][:], in_=tab_words[a].rearrange("p t i -> p (t i)").bitcast(I32))
+            for half in range(2):
+                gather_words(a, half)
+
+        for a, b in chunks[1:]:
+            turn_w(a, b)
+        for a, b in chunks:
+            quantise_wr(a, b)
         c4_sc = kept([P, 2, K], U8, "c4_sc", "grouped10")
         nc.vector.memset(c4_sc[:].rearrange("p b n -> p (b n)").bitcast(I32), 0)
-        c4 = kept([P, 2, 2 * K], U8, "c4", "w_raw11")
+        c4 = kept([P, 2, 2 * K], U8, "c4", "w_raw1")
         nc.sync.dma_start(out=c4[:].bitcast(I32), in_=c4_words.rearrange("b p c -> p b c").bitcast(I32))
+        back_sb = kept([P, 8], F32, "back_sb", "grouped11")
+        with nc.allow_non_contiguous_dma(reason="one factor for each output row"):
+            nc.sync.dma_start(out=back_sb[:], in_=back.rearrange("(j p) -> p j", p=P))
         for q in range(4):
             nc.sync.dma_start(
                 out=c4_sc[32 * q : 32 * q + 4, :, :].bitcast(I32),
                 in_=c4_scales[:, 4 * q : 4 * q + 4, :].rearrange("b r n -> r b n").bitcast(I32),
             )
-        back_sb = kept([P, 8], F32, "back_sb", "w_raw01")
-        with nc.allow_non_contiguous_dma(reason="one factor for each output row"):
-            nc.sync.dma_start(out=back_sb[:], in_=back.rearrange("(j p) -> p j", p=P))
 
-        nc.vector.tensor_copy(out=v_sc[:], in_=tab_sc[:].indirect(offs_sb[:]))
-        for a in range(2):
-            for half in range(2):
-                gather_words(a, half)
 
         h = {}
 
@@ -181,39 +184,70 @@ def tile_list_spice_substitution_kernel(
                         stop=(a == 1),
                     )
                 dst = h[k][:, BANK * half : BANK * (half + 1)]
-                if k == 0 and half == 1:
+                if k == 0 and half == 1 and H0V:
                     nc.vector.tensor_copy(out=dst, in_=ps[:])
                 else:
                     nc.scalar.copy(out=dst, in_=ps[:])
 
         spans = ((0, WIDE), (WIDE, NARROW))
-        want, damp, prod, planes, z_codes, z_sc = {}, {}, {}, {}, {}, {}
+        damp, prod, diff, planes, z_codes, z_sc = {}, {}, {}, {}, {}, {}
 
         def picked(s, k, which):
             first, width = spans[s]
             return h[k][:].indirect(lists[which][:, first // 16 : (first + width) // 16])
 
-        def pick_want(s, k):
-            want[s, k] = ring.tile([P, spans[s][1]], F32, name="want", tag="want")
-            nc.vector.tensor_copy(out=want[s, k][:], in_=picked(s, k, 0))
+        want = {}
 
-        def make_damp(s, k):
+        def pick_want(k):
+            want[k] = ring.tile([P, M], F32, name="want", tag="want")
+            nc.vector.tensor_copy(out=want[k][:], in_=h[k][:].indirect(lists[0][:]))
+
+        def make_damp(k):
             b, t = divmod(k, 4)
-            damp[s, k] = ring.tile([P, spans[s][1]], F32, name="damp", tag="damp")
-            nc.scalar.activation(out=damp[s, k][:], in_=want[s, k][:], func=ACT.Exp, scale=fade_sb[:, b, t : t + 1])
+            damp[k] = kept([P, M], F32, "damp%d" % k)
+            nc.scalar.activation(out=damp[k][:], in_=want[k][:], func=ACT.Exp, scale=fade_sb[:, b, t : t + 1])
 
         def pick_repl(s, k):
-            prod[s, k] = ring.tile([P, spans[s][1]], F32, name="prod", tag="prod")
-            nc.vector.tensor_tensor(prod[s, k][:], picked(s, k, 1), damp[s, k][:], ALU.mult)
+            first, width = spans[s]
+            prod[s, k] = ring.tile([P, width], F32, name="prod", tag="prod", bufs=PB)
+            nc.vector.tensor_tensor(prod[s, k][:], picked(s, k, 1), damp[k][:, first : first + width], ALU.mult)
 
         def pick_carr(s, k):
             b, t = divmod(k, 4)
-            width = spans[s][1]
-            diff = ring.tile([P, width], F32, name="diff", tag="diff")
-            nc.vector.tensor_tensor(diff[:], picked(s, k, 2), prod[s, k][:], ALU.subtract)
+            if s == 0:
+                diff[k] = ring.tile([P, WIDE], F32, name="diff", tag="diff", bufs=1)
+                dst = diff[k][:]
+            else:
+                if t == 0:
+                    diffs[b] = kept([P, 4, NARROW], F32, "diffs%d" % b, "planes1" if b == 0 and GATE else None)
+                dst = diffs[b][:, t, :]
+            nc.vector.tensor_tensor(dst, picked(s, k, 2), prod[s, k][:], ALU.subtract)
+            if s == 1 and b not in DIRECT:
+                if t == 0:
+                    planes[1, b] = kept([P, 4, NARROW], BF16, "planes1%d" % b)
+                nc.scalar.activation(out=planes[1, b][:, t, :], in_=dst, func=ACT.Copy, scale=neg_lift[:, k : k + 1])
+
+        def make_plane(k):
+            b, t = divmod(k, 4)
             if t == 0:
-                planes[s, b] = kept([P, 4, width], BF16, "planes%d%d" % (s, b))
-            nc.scalar.activation(out=planes[s, b][:, t, :], in_=diff[:], func=ACT.Copy, scale=neg_lift[:, k : k + 1])
+                planes[0, b] = kept([P, 4, WIDE], BF16, "planes%d" % b)
+            nc.scalar.activation(out=planes[0, b][:, t, :], in_=diff[k][:], func=ACT.Copy, scale=neg_lift[:, k : k + 1])
+
+        woven, diffs = {}, {}
+
+        def weave_z(s, b, piece):
+            woven[s, b, piece] = ring.tile([P, 4 * P], BF16, name="woven", tag="woven", align_bytes=64, bufs=3)
+            dst = woven[s, b, piece][:].rearrange("p (c i t) -> p c t i", i=4, t=4)
+            direct = s == 1 and b in DIRECT
+            src = (diffs[b] if direct else planes[s, b])[:, :, P * piece : P * (piece + 1)]
+            src = src.rearrange("p t (c i) -> p c t i", i=4)
+            if direct:
+                factor = neg_lift[:, 4 * b : 4 * b + 4].unsqueeze(1).unsqueeze(3).to_broadcast([P, P // 4, 4, 4])
+                nc.vector.tensor_tensor(dst, src, factor, ALU.mult)
+            elif (s, b, piece) in WEAVE_V:
+                nc.vector.tensor_copy(out=dst, in_=src)
+            else:
+                nc.scalar.copy(out=dst, in_=src)
 
         def quantise_z(s, b, piece):
             width = spans[s][1]
@@ -221,12 +255,9 @@ def tile_list_spice_substitution_kernel(
                 z_codes[s, b] = kept([P, width], U32, "z_codes%d%d" % (s, b))
                 z_sc[s, b] = kept([P, width], U8, "z_sc%d%d" % (s, b))
             cols = slice(P * piece, P * (piece + 1))
-            woven = ring.tile([P, 4 * P], BF16, name="woven", tag="woven", align_bytes=64)
-            nc.scalar.copy(
-                out=woven[:].rearrange("p (c i t) -> p c t i", i=4, t=4),
-                in_=planes[s, b][:, :, cols].rearrange("p t (c i) -> p c t i", i=4),
+            nc.vector.quantize_mx(
+                out=z_codes[s, b][:, cols].bitcast(FP8X4), scales=z_sc[s, b][:, cols], in_=woven[s, b, piece][:]
             )
-            nc.vector.quantize_mx(out=z_codes[s, b][:, cols].bitcast(FP8X4), scales=z_sc[s, b][:, cols], in_=woven[:])
 
         def second_passes(s, b, j, ps, at, start, stop):
             width = spans[s][1]
@@ -250,60 +281,75 @@ def tile_list_spice_substitution_kernel(
                     stop=(stop and i == len(passes) - 1),
                 )
 
+        wide_banks = {}
+
+        def open_wide(j):
+            wide_banks[j] = bank((j + 4) % 8)
+            second_passes(0, 0, j, wide_banks[j], 0, True, False)
+
         def finish_wide(j):
-            ps = bank(4 + j % 4)
-            second_passes(0, 0, j, ps, 0, True, False)
-            second_passes(0, 1, j, ps, 0, False, True)
             res = kept([P, WIDE], F32, "res%d" % j)
-            nc.scalar.activation(out=res[:], in_=ps[:, 0:WIDE], func=ACT.Copy, scale=back_sb[:, j : j + 1])
+            scaled_copy(j in ON_VECTOR, res[:], wide_banks[j][:, 0:WIDE], j)
             nc.sync.dma_start(out=out[P * j : P * (j + 1), 0:WIDE], in_=res[:])
 
-        steps = [(s, k) for s in range(2) for k in range(8)]
+        def scaled_copy(on_vector, dst, src, j):
+            if on_vector:
+                nc.vector.tensor_scalar(out=dst, in0=src, scalar1=back_sb[:, j : j + 1], scalar2=None, op0=ALU.mult)
+            else:
+                nc.scalar.activation(out=dst, in_=src, func=ACT.Copy, scale=back_sb[:, j : j + 1])
+
         make_h(0)
         make_h(1)
-        pick_want(*steps[0])
-        pick_want(*steps[1])
-        make_damp(*steps[0])
+        pick_want(0)
+        pick_want(1)
+        for k in range(8):
+            make_damp(k)
+            pick_repl(0, k)
+            if k + 2 < 8:
+                make_h(k + 2)
+                pick_want(k + 2)
+            if k > 0:
+                make_plane(k - 1)
+            pick_carr(0, k)
+            if 4 <= k < 7:
+                weave_z(0, 0, k - 4)
+                quantise_z(0, 0, k - 4)
+        for j in range(8):
+            open_wide(j)
+        make_plane(7)
+        pick_repl(1, 0)
+        for piece in range(3):
+            weave_z(0, 1, piece)
+            quantise_z(0, 1, piece)
+        for j in range(8):
+            second_passes(0, 1, j, wide_banks[j], 0, False, True)
+            if EARLY:
+                finish_wide(j)
         narrow_banks = []
-        for i, (s, k) in enumerate(steps):
-            if i + 2 < 8:
-                make_h(i + 2)
-            pick_repl(s, k)
-            if i + 2 < len(steps):
-                pick_want(*steps[i + 2])
-            if i + 1 < len(steps):
-                make_damp(*steps[i + 1])
-            pick_carr(s, k)
-            if 4 <= i < 7:
-                quantise_z(0, 0, i - 4)
-            if i == 7:
-                for piece in range(3):
-                    quantise_z(0, 1, piece)
-            if i == 11:
+        for k in range(8):
+            if not EARLY:
+                finish_wide(k)
+            if k + 1 < 8:
+                pick_repl(1, k + 1)
+            pick_carr(1, k)
+            if k == 4:
+                weave_z(1, 0, 0)
+            if k == 5:
                 quantise_z(1, 0, 0)
-            if 9 <= i:
-                finish_wide(i - 9)
-            if i == 12:
-                for pair in range(4):
-                    ps = bank(pair)
-                    narrow_banks.append(ps)
-                    second_passes(1, 0, 2 * pair, ps, 0, True, False)
-                    second_passes(1, 0, 2 * pair + 1, ps, NARROW, False, False)
-        finish_wide(7)
+        for pair in range(4):
+            ps = bank(4 + pair)
+            narrow_banks.append(ps)
+            second_passes(1, 0, 2 * pair, ps, 0, True, False)
+            second_passes(1, 0, 2 * pair + 1, ps, NARROW, False, False)
+        weave_z(1, 1, 0)
         quantise_z(1, 1, 0)
         for pair in range(4):
             ps = narrow_banks[pair]
             second_passes(1, 1, 2 * pair, ps, 0, False, False)
             second_passes(1, 1, 2 * pair + 1, ps, NARROW, False, True)
             res = kept([P, 2, NARROW], F32, "res_narrow%d" % pair)
-            for e in range(2):
-                j = 2 * pair + e
-                src = ps[:, NARROW * e : NARROW * (e + 1)]
-                if pair % 2 == 0:
-                    nc.scalar.activation(out=res[:, e, :], in_=src, func=ACT.Copy, scale=back_sb[:, j : j + 1])
-                else:
-                    nc.vector.tensor_scalar(
-                        out=res[:, e, :], in0=src, scalar1=back_sb[:, j : j + 1], scalar2=None, op0=ALU.mult
-                    )
+            factor = back_sb[:, 2 * pair : 2 * pair + 2].unsqueeze(2).to_broadcast([P, 2, NARROW])
+            sums = ps[:, 0 : 2 * NARROW].rearrange("p (e m) -> p e m", e=2)
+            nc.vector.tensor_tensor(res[:], sums, factor, ALU.mult)
             rows = out[2 * P * pair : 2 * P * (pair + 1), WIDE:M]
             nc.sync.dma_start(out=rows.rearrange("(e p) m -> p e m", p=P), in_=res[:])

@@ -20,16 +20,11 @@ ACT = mybir.ActivationFunctionType
 P = 128
 PASS = 512
 BANK = 512
-WIDE = 384
-NARROW = M - WIDE
-ON_VECTOR = ()
-WEAVE_V = ((0, 1, 1), (0, 1, 2))
-DIRECT = (0, 1)
-EARLY = True
-GATE = False
-PB = 2
+PARTS = ((0, 256, 0), (0, 256, 1), (256, 128, 0), (256, 128, 1), (384, 128, 0), (384, 128, 1))
+STORES = {3: ((0, 0), (0, 1)), 4: ((0, 2), (0, 3)), 5: ((1, 0), (1, 1))}
 GROUP_S = ((1, 1),)
-H0V = False
+SPANS = ((0, 256), (256, 128), (384, 128))
+SPAN_BANKS = ((4, 5, 6, 7), (0, 1), (2, 3, 4, 5))
 
 
 def tile_list_spice_substitution_kernel(
@@ -38,7 +33,6 @@ def tile_list_spice_substitution_kernel(
     nc = tc.nc
     with ExitStack() as ctx:
         keep = ctx.enter_context(tc.tile_pool(name="keep", bufs=1))
-        ring = ctx.enter_context(tc.tile_pool(name="ring", bufs=2))
         psum = ctx.enter_context(tc.psum_pool(name="psum", bufs=1))
 
         def bank(i):
@@ -54,18 +48,21 @@ def tile_list_spice_substitution_kernel(
                 out=tab_sc[32 * q : 32 * q + 8, :].bitcast(I32),
                 in_=tab_scales[:, 4 * q : 4 * q + 4, :].bitcast(I32),
             )
-        warm = kept([P, 1], F32, "warm")
-        warm_out = kept([P, 1], F32, "warm_out")
-        nc.vector.memset(warm[:], 0.0)
-        nc.scalar.activation(out=warm_out[:], in_=warm[:], func=ACT.Exp)
 
         w_raw, tab = {}, {}
 
-        def load_w(a):
-            w_raw[a] = kept([P, 4, H], F32, "w_raw%d" % a)
-            nc.sync.dma_start(out=w_raw[a][:], in_=w[PASS * a : PASS * (a + 1), :].rearrange("(p i) r -> p i r", i=4))
+        def load_w(a, first, count, tag):
+            tile = kept([P, 4, count * PASS], F32, "w_raw%d%d" % (a, first), tag)
+            rows = w[PASS * a : PASS * (a + 1), PASS * first : PASS * (first + count)]
+            nc.sync.dma_start(out=tile[:], in_=rows.rearrange("(p i) r -> p i r", i=4))
+            for b in range(count):
+                w_raw[a, first + b] = tile[:, :, PASS * b : PASS * (b + 1)]
 
-        load_w(0)
+        def load_tab(a, tag):
+            tab[a] = kept([P, T], I32, "tab%d" % a, tag)
+            nc.sync.dma_start(out=tab[a][:], in_=tab_words[a].rearrange("p t i -> p (t i)").bitcast(I32))
+
+        load_w(0, 0, 2, "w_raw0")
         offs_sb = keep.tile([P, S // 16], U16, name="offs_sb")
         nc.sync.dma_start(offs_sb[:], offs)
         lists = []
@@ -77,54 +74,43 @@ def tile_list_spice_substitution_kernel(
         nc.sync.dma_start(out=fade_sb[:], in_=fade.rearrange("(b p t) -> p b t", b=2, t=4))
         lift_sb = kept([P, 2, 4], F32, "lift_sb")
         nc.sync.dma_start(out=lift_sb[:], in_=lift.rearrange("(b p t) -> p b t", b=2, t=4))
-        load_w(1)
+        load_w(1, 0, 2, "w_raw1")
 
         ident = kept([P, P], F32, "ident")
         make_identity(nc, ident[:])
         neg_lift = kept([P, 8], F32, "neg_lift")
-        nc.vector.tensor_scalar(
-            out=neg_lift[:], in0=lift_sb[:].rearrange("p b t -> p (b t)"), scalar1=-1.0, scalar2=None, op0=ALU.mult
-        )
+        nc.scalar.activation(out=neg_lift[:], in_=lift_sb[:].rearrange("p b t -> p (b t)"), func=ACT.Copy, scale=-1.0)
 
-        wk_codes, wk_sc, wr_codes, wr_sc, grouped, turned = {}, {}, {}, {}, {}, {}
+        wk_codes, wk_sc, wr_codes, wr_sc, grouped, turned, turn_banks = {}, {}, {}, {}, {}, {}, {}
 
-        def group_w(a, b):
-            g = kept([P, 4 * PASS], BF16, "grouped%d%d" % (a, b))
-            copy = nc.scalar.copy if (a, b) in GROUP_S else nc.vector.tensor_copy
-            copy(
-                out=g[:].rearrange("p (t m i) -> p m i t", t=4, i=4),
-                in_=w_raw[a][:, :, PASS * b : PASS * (b + 1)].rearrange("p i (m t) -> p m i t", t=4),
-            )
-            grouped[a, b] = g
-
-        def quantise(src, width, name, tag=None):
-            codes = kept([P, width], U32, name + "_codes", tag)
-            scales = kept([P, width], U8, name + "_sc")
-            nc.vector.quantize_mx(out=codes[:].bitcast(FP8X4), scales=scales[:], in_=src)
-            return codes, scales
+        def group_w(a, b, copy, first, count):
+            if first == 0:
+                grouped[a, b] = kept([P, 4 * PASS], BF16, "grouped%d%d" % (a, b))
+            dst = grouped[a, b][:].rearrange("p (t m i) -> p m i t", t=4, i=4)
+            src = w_raw[a, b].rearrange("p i (m t) -> p m i t", t=4)
+            copy(out=dst[:, first : first + count], in_=src[:, first : first + count])
 
         def quantise_wk(a, b):
-            wk_codes[a, b], wk_sc[a, b] = quantise(grouped[a, b][:], PASS, "wk%d%d" % (a, b))
+            wk_codes[a, b] = kept([P, PASS], U32, "wk%d%d_codes" % (a, b))
+            wk_sc[a, b] = kept([P, PASS], U8, "wk%d%d_sc" % (a, b))
+            nc.vector.quantize_mx(out=wk_codes[a, b][:].bitcast(FP8X4), scales=wk_sc[a, b][:], in_=grouped[a, b][:])
 
-        def turn_w(a, b):
+        def turn_w(a, b, u):
             words = grouped[a, b][:].bitcast(F32).rearrange("p (t m u) -> p t m u", t=4, u=2)
-            g = kept([P, 4 * PASS], BF16, "turned%d%d" % (a, b))
-            for u in range(2):
-                ps = bank((4 + 2 * (2 * a + b)) % 8 + u)
-                for t in range(4):
-                    nc.tensor.transpose(ps[:, P * t : P * (t + 1)], words[:, t, :, u], ident[:])
-                nc.scalar.copy(
-                    out=g[:].rearrange("m (p u e t) -> m u p e t", u=2, e=2, t=4)[:, u],
-                    in_=ps[:].bitcast(BF16).rearrange("m (t p e) -> m p e t", t=4, e=2),
-                )
-            turned[a, b] = g
+            if u == 0:
+                turned[a, b] = kept([P, 4 * PASS], BF16, "turned%d%d" % (a, b))
+            ps = bank(4 + 2 * b + u)
+            for t in range(4):
+                nc.tensor.transpose(ps[:, P * t : P * (t + 1)], words[:, t, :, u], ident[:])
+            nc.scalar.copy(
+                out=turned[a, b][:].rearrange("m (p u e t) -> m u p e t", u=2, e=2, t=4)[:, u],
+                in_=ps[:].bitcast(BF16).rearrange("m (t p e) -> m p e t", t=4, e=2),
+            )
 
-        def quantise_wr(a, b):
-            if b == 0:
-                wr_codes[a] = kept([P, 2, PASS], U32, "wr%d_codes" % a, ("w_raw0", "grouped00")[a])
-            wr_codes[a, b] = wr_codes[a][:, b, :]
+        def quantise_wr(a, b, codes):
+            wr_codes[a, b] = codes
             wr_sc[a, b] = kept([P, PASS], U8, "wr%d%d_sc" % (a, b))
-            nc.vector.quantize_mx(out=wr_codes[a, b].bitcast(FP8X4), scales=wr_sc[a, b][:], in_=turned[a, b][:])
+            nc.vector.quantize_mx(out=codes.bitcast(FP8X4), scales=wr_sc[a, b][:], in_=turned[a, b][:])
 
         v_codes = {}
 
@@ -133,44 +119,44 @@ def tile_list_spice_substitution_kernel(
             cols = offs_sb[:, 32 * half : 32 * (half + 1)]
             nc.vector.tensor_copy(out=v_codes[a, half][:], in_=tab[a][:].bitcast(U32).indirect(cols))
 
-        v_sc = kept([P, S], U8, "v_sc")
-
         chunks = [(a, b) for a in range(2) for b in range(2)]
         for a, b in chunks:
-            group_w(a, b)
+            group_w(a, b, nc.scalar.copy if (a, b) in GROUP_S else nc.vector.tensor_copy, 0, P)
             quantise_wk(a, b)
+        v_sc = kept([P, S], U8, "v_sc")
         nc.vector.tensor_copy(out=v_sc[:], in_=tab_sc[:].indirect(offs_sb[:]))
-        turn_w(0, 0)
+        for a, b in chunks:
+            turn_w(a, b, 0)
+            turn_w(a, b, 1)
         for a in range(2):
-            tab[a] = kept([P, T], I32, "tab%d" % a, ("w_raw0", "grouped00")[a])
-            nc.sync.dma_start(out=tab[a][:], in_=tab_words[a].rearrange("p t i -> p (t i)").bitcast(I32))
+            load_tab(a, ("w_raw0", "grouped00")[a])
             for half in range(2):
                 gather_words(a, half)
+        for a in range(2):
+            wr_pair = kept([P, 2, PASS], U32, "wr%d_codes" % a, ("w_raw0", "grouped00")[a])
+            for b in range(2):
+                quantise_wr(a, b, wr_pair[:, b, :])
 
-        for a, b in chunks[1:]:
-            turn_w(a, b)
-        for a, b in chunks:
-            quantise_wr(a, b)
-        c4_sc = kept([P, 2, K], U8, "c4_sc", "grouped10")
-        nc.vector.memset(c4_sc[:].rearrange("p b n -> p (b n)").bitcast(I32), 0)
         c4 = kept([P, 2, 2 * K], U8, "c4", "w_raw1")
         nc.sync.dma_start(out=c4[:].bitcast(I32), in_=c4_words.rearrange("b p c -> p b c").bitcast(I32))
-        back_sb = kept([P, 8], F32, "back_sb", "grouped11")
-        with nc.allow_non_contiguous_dma(reason="one factor for each output row"):
-            nc.sync.dma_start(out=back_sb[:], in_=back.rearrange("(j p) -> p j", p=P))
+        c4_sc = kept([P, 2, K], U8, "c4_sc", "grouped10")
+        nc.vector.memset(c4_sc[:].rearrange("p b n -> p (b n)").bitcast(I32), 0)
         for q in range(4):
             nc.sync.dma_start(
                 out=c4_sc[32 * q : 32 * q + 4, :, :].bitcast(I32),
                 in_=c4_scales[:, 4 * q : 4 * q + 4, :].rearrange("b r n -> r b n").bitcast(I32),
             )
-
+        back_sb = kept([P, 8], F32, "back_sb", "grouped11")
+        with nc.allow_non_contiguous_dma(reason="one factor for each output row"):
+            nc.sync.dma_start(out=back_sb[:], in_=back.rearrange("(j p) -> p j", p=P))
 
         h = {}
 
-        def make_h(k):
+        def make_h(k, halves=(0, 1)):
             b, t = divmod(k, 4)
-            h[k] = kept([P, S], F32, "h%d" % k)
-            for half in range(2):
+            if 0 in halves:
+                h[k] = kept([P, S], F32, "h%d" % k)
+            for half in halves:
                 ps = bank(2 * (k % 2) + half)
                 for a in range(2):
                     cols = slice(P * t, P * (t + 1))
@@ -183,173 +169,176 @@ def tile_list_spice_substitution_kernel(
                         start=(a == 0),
                         stop=(a == 1),
                     )
-                dst = h[k][:, BANK * half : BANK * (half + 1)]
-                if k == 0 and half == 1 and H0V:
-                    nc.vector.tensor_copy(out=dst, in_=ps[:])
-                else:
-                    nc.scalar.copy(out=dst, in_=ps[:])
+                nc.scalar.copy(out=h[k][:, BANK * half : BANK * (half + 1)], in_=ps[:])
 
-        spans = ((0, WIDE), (WIDE, NARROW))
-        damp, prod, diff, planes, z_codes, z_sc = {}, {}, {}, {}, {}, {}
+        slots = [kept([P, M], F32, "slot%d" % i) for i in range(3)]
+        prods = [kept([P, M // 2], F32, "prods%d" % i) for i in range(3)]
+        damp = {}
 
-        def picked(s, k, which):
-            first, width = spans[s]
+        def picked(k, which, first, width):
             return h[k][:].indirect(lists[which][:, first // 16 : (first + width) // 16])
 
-        want = {}
-
         def pick_want(k):
-            want[k] = ring.tile([P, M], F32, name="want", tag="want")
-            nc.vector.tensor_copy(out=want[k][:], in_=h[k][:].indirect(lists[0][:]))
+            nc.vector.tensor_copy(out=slots[k % 3][:], in_=picked(k, 0, 0, M))
 
         def make_damp(k):
             b, t = divmod(k, 4)
             damp[k] = kept([P, M], F32, "damp%d" % k)
-            nc.scalar.activation(out=damp[k][:], in_=want[k][:], func=ACT.Exp, scale=fade_sb[:, b, t : t + 1])
+            nc.scalar.activation(out=damp[k][:], in_=slots[k % 3][:], func=ACT.Exp, scale=fade_sb[:, b, t : t + 1])
 
-        def pick_repl(s, k):
-            first, width = spans[s]
-            prod[s, k] = ring.tile([P, width], F32, name="prod", tag="prod", bufs=PB)
-            nc.vector.tensor_tensor(prod[s, k][:], picked(s, k, 1), damp[k][:, first : first + width], ALU.mult)
+        left0, left1, end1 = PARTS[0], PARTS[1], PARTS[-1]
+        stage = {part: kept([P, 4, 2 * P], F32, "stage%d_%d" % part[::2]) for part in PARTS[:-1]}
+        diffs = {part: kept([P, 4, part[1]], F32, "diffs%d_%d" % part[::2]) for part in PARTS[2:]}
 
-        def pick_carr(s, k):
-            b, t = divmod(k, 4)
-            if s == 0:
-                diff[k] = ring.tile([P, WIDE], F32, name="diff", tag="diff", bufs=1)
-                dst = diff[k][:]
-            else:
-                if t == 0:
-                    diffs[b] = kept([P, 4, NARROW], F32, "diffs%d" % b, "planes1" if b == 0 and GATE else None)
-                dst = diffs[b][:, t, :]
-            nc.vector.tensor_tensor(dst, picked(s, k, 2), prod[s, k][:], ALU.subtract)
-            if s == 1 and b not in DIRECT:
-                if t == 0:
-                    planes[1, b] = kept([P, 4, NARROW], BF16, "planes1%d" % b)
-                nc.scalar.activation(out=planes[1, b][:, t, :], in_=dst, func=ACT.Copy, scale=neg_lift[:, k : k + 1])
+        def planes(part):
+            halves = stage[part][:].rearrange("p t c -> p (t c)").bitcast(BF16).rearrange("p (t c) -> p t c", t=4)
+            return halves[:, :, 2 * P - part[1] // 2 : 2 * P + part[1] // 2]
 
-        def make_plane(k):
-            b, t = divmod(k, 4)
-            if t == 0:
-                planes[0, b] = kept([P, 4, WIDE], BF16, "planes%d" % b)
-            nc.scalar.activation(out=planes[0, b][:, t, :], in_=diff[k][:], func=ACT.Copy, scale=neg_lift[:, k : k + 1])
 
-        woven, diffs = {}, {}
+        def prod_of(part, t):
+            if part[0] == 0:
+                return prods[(4 * part[2] + t) % 3][:]
+            return stage[PARTS[PARTS.index(part) - 2]][:, t, P:]
 
-        def weave_z(s, b, piece):
-            woven[s, b, piece] = ring.tile([P, 4 * P], BF16, name="woven", tag="woven", align_bytes=64, bufs=3)
-            dst = woven[s, b, piece][:].rearrange("p (c i t) -> p c t i", i=4, t=4)
-            direct = s == 1 and b in DIRECT
-            src = (diffs[b] if direct else planes[s, b])[:, :, P * piece : P * (piece + 1)]
-            src = src.rearrange("p t (c i) -> p c t i", i=4)
-            if direct:
-                factor = neg_lift[:, 4 * b : 4 * b + 4].unsqueeze(1).unsqueeze(3).to_broadcast([P, P // 4, 4, 4])
-                nc.vector.tensor_tensor(dst, src, factor, ALU.mult)
-            elif (s, b, piece) in WEAVE_V:
-                nc.vector.tensor_copy(out=dst, in_=src)
-            else:
-                nc.scalar.copy(out=dst, in_=src)
+        def diff_of(part, t):
+            if part[0] == 0:
+                return slots[(4 * part[2] + t + 1) % 3][:, 0 : part[1]]
+            return diffs[part][:, t, :]
 
-        def quantise_z(s, b, piece):
-            width = spans[s][1]
-            if piece == 0:
-                z_codes[s, b] = kept([P, width], U32, "z_codes%d%d" % (s, b))
-                z_sc[s, b] = kept([P, width], U8, "z_sc%d%d" % (s, b))
-            cols = slice(P * piece, P * (piece + 1))
+        def pick_repl(part, t):
+            first, width, b = part
+            k = 4 * b + t
+            nc.vector.tensor_tensor(prod_of(part, t), picked(k, 1, first, width), damp[k][:, first : first + width], ALU.mult)
+
+        def pick_carr(part, t):
+            first, width, b = part
+            nc.vector.tensor_tensor(diff_of(part, t), picked(4 * b + t, 2, first, width), prod_of(part, t), ALU.subtract)
+
+        def make_plane(part, t):
+            k = 4 * part[2] + t
+            nc.scalar.activation(out=planes(part)[:, t, :], in_=diff_of(part, t), func=ACT.Copy, scale=neg_lift[:, k : k + 1])
+
+        woven = {part: kept([P, 4 * part[1]], BF16, "woven%d_%d" % part[::2])[:] for part in PARTS[:-1]}
+        woven[end1] = stage[PARTS[-2]][:, 0, :].bitcast(BF16)
+        z_codes = {part: kept([P, part[1]], U32, "z_codes%d_%d" % part[::2]) for part in PARTS}
+        z_sc = {part: kept([P, part[1]], U8, "z_sc%d_%d" % part[::2]) for part in PARTS}
+
+        def woven_view(part, at, count):
+            return woven[part][:, 4 * at : 4 * (at + count)].rearrange("p (c i t) -> p c t i", i=4, t=4)
+
+        def weave(part, at, count, copy=nc.scalar.copy):
+            src = planes(part)[:, :, at : at + count].rearrange("p t (c i) -> p c t i", i=4)
+            copy(out=woven_view(part, at, count), in_=src)
+
+        def weave_last():
+            src = diffs[end1][:].rearrange("p t (c i) -> p c t i", i=4)
+            factor = neg_lift[:, 4:8].unsqueeze(1).unsqueeze(3).to_broadcast([P, P // 4, 4, 4])
+            nc.vector.tensor_tensor(woven_view(end1, 0, P), src, factor, ALU.mult)
+
+        def quantise_z(part, at, count):
+            cols = slice(at, at + count)
             nc.vector.quantize_mx(
-                out=z_codes[s, b][:, cols].bitcast(FP8X4), scales=z_sc[s, b][:, cols], in_=woven[s, b, piece][:]
+                out=z_codes[part][:, cols].bitcast(FP8X4), scales=z_sc[part][:, cols], in_=woven[part][:, 4 * at : 4 * (at + count)]
             )
 
-        def second_passes(s, b, j, ps, at, start, stop):
-            width = spans[s][1]
-            a, jj = divmod(j, 4)
-            n_cols = slice(P * jj, P * (jj + 1))
+        sums = {}
+
+        def second_passes(s, i, b):
+            first, width = SPANS[s]
+            per_bank = 8 // len(SPAN_BANKS[s])
+            if b == 0:
+                sums[s, i] = bank(SPAN_BANKS[s][i])
+            part = PARTS[2 * s + b]
+            at = first - part[0]
             passes = []
-            for first, n in ((0, 256), (256, 128)) if width == WIDE else ((0, 128),):
-                passes.append((wr_codes[a, b][:, n_cols].bitcast(FP8X4), wr_sc[a, b][:, n_cols], first, n))
-            for first in range(0, width, P):
-                passes.append(
-                    (c4[:, b, 2 * P * j : 2 * P * (j + 1)].bitcast(FP4X4), c4_sc[:, b, P * j : P * (j + 1)], first, P)
-                )
-            for i, (codes, scales, first, n) in enumerate(passes):
+            for e in range(per_bank):
+                j = per_bank * i + e
+                a, jj = divmod(j, 4)
+                n_cols = slice(P * jj, P * (jj + 1))
+                passes.append((wr_codes[a, b][:, n_cols].bitcast(FP8X4), wr_sc[a, b][:, n_cols], e, 0, width))
+                for c in range(0, width, P):
+                    passes.append(
+                        (c4[:, b, 2 * P * j : 2 * P * (j + 1)].bitcast(FP4X4), c4_sc[:, b, P * j : P * (j + 1)], e, c, P)
+                    )
+            for n, (codes, scales, e, c, count) in enumerate(passes):
                 nc.tensor.matmul_mx(
-                    out=ps[:, at + first : at + first + n],
+                    out=sums[s, i][:, width * e + c : width * e + c + count],
                     lhsT=codes,
                     lhsT_scale=scales,
-                    rhs=z_codes[s, b][:, first : first + n].bitcast(FP8X4),
-                    rhs_scale=z_sc[s, b][:, first : first + n],
-                    start=(start and i == 0),
-                    stop=(stop and i == len(passes) - 1),
+                    rhs=z_codes[part][:, at + c : at + c + count].bitcast(FP8X4),
+                    rhs_scale=z_sc[part][:, at + c : at + c + count],
+                    start=(b == 0 and n == 0),
+                    stop=(b == 1 and n == len(passes) - 1),
                 )
 
-        wide_banks = {}
-
-        def open_wide(j):
-            wide_banks[j] = bank((j + 4) % 8)
-            second_passes(0, 0, j, wide_banks[j], 0, True, False)
-
-        def finish_wide(j):
-            res = kept([P, WIDE], F32, "res%d" % j)
-            scaled_copy(j in ON_VECTOR, res[:], wide_banks[j][:, 0:WIDE], j)
-            nc.sync.dma_start(out=out[P * j : P * (j + 1), 0:WIDE], in_=res[:])
-
-        def scaled_copy(on_vector, dst, src, j):
-            if on_vector:
-                nc.vector.tensor_scalar(out=dst, in0=src, scalar1=back_sb[:, j : j + 1], scalar2=None, op0=ALU.mult)
+        def finish(s, i):
+            first, width = SPANS[s]
+            per_bank = 8 // len(SPAN_BANKS[s])
+            res = kept([P, per_bank, width], F32, "res%d_%d" % (s, i))
+            j0 = per_bank * i
+            if s == 2:
+                factor = back_sb[:, j0 : j0 + per_bank].unsqueeze(2).to_broadcast([P, per_bank, width])
+                src = sums[s, i][:, 0 : per_bank * width].rearrange("p (e m) -> p e m", e=per_bank)
+                nc.vector.tensor_tensor(res[:], src, factor, ALU.mult)
             else:
-                nc.scalar.activation(out=dst, in_=src, func=ACT.Copy, scale=back_sb[:, j : j + 1])
+                for e in range(per_bank):
+                    nc.scalar.activation(
+                        out=res[:, e, :],
+                        in_=sums[s, i][:, width * e : width * (e + 1)],
+                        func=ACT.Copy,
+                        scale=back_sb[:, j0 + e : j0 + e + 1],
+                    )
+            rows = out[P * j0 : P * (j0 + per_bank), first : first + width]
+            nc.sync.dma_start(out=rows.rearrange("(e p) m -> p e m", p=P), in_=res[:])
+
+        def all_banks(s, b):
+            for i in range(len(SPAN_BANKS[s])):
+                second_passes(s, i, b)
+
+
+        def left(k):
+            return PARTS[k // 4], k % 4
 
         make_h(0)
         make_h(1)
         pick_want(0)
         pick_want(1)
-        for k in range(8):
-            make_damp(k)
-            pick_repl(0, k)
-            if k + 2 < 8:
-                make_h(k + 2)
-                pick_want(k + 2)
-            if k > 0:
-                make_plane(k - 1)
-            pick_carr(0, k)
-            if 4 <= k < 7:
-                weave_z(0, 0, k - 4)
-                quantise_z(0, 0, k - 4)
-        for j in range(8):
-            open_wide(j)
-        make_plane(7)
-        pick_repl(1, 0)
-        for piece in range(3):
-            weave_z(0, 1, piece)
-            quantise_z(0, 1, piece)
-        for j in range(8):
-            second_passes(0, 1, j, wide_banks[j], 0, False, True)
-            if EARLY:
-                finish_wide(j)
-        narrow_banks = []
-        for k in range(8):
-            if not EARLY:
-                finish_wide(k)
+        make_h(2, (0,))
+        make_damp(0)
+        pick_repl(*left(0))
+        for k in range(1, 8):
             if k + 1 < 8:
-                pick_repl(1, k + 1)
-            pick_carr(1, k)
-            if k == 4:
-                weave_z(1, 0, 0)
-            if k == 5:
-                quantise_z(1, 0, 0)
-        for pair in range(4):
-            ps = bank(4 + pair)
-            narrow_banks.append(ps)
-            second_passes(1, 0, 2 * pair, ps, 0, True, False)
-            second_passes(1, 0, 2 * pair + 1, ps, NARROW, False, False)
-        weave_z(1, 1, 0)
-        quantise_z(1, 1, 0)
-        for pair in range(4):
-            ps = narrow_banks[pair]
-            second_passes(1, 1, 2 * pair, ps, 0, False, False)
-            second_passes(1, 1, 2 * pair + 1, ps, NARROW, False, True)
-            res = kept([P, 2, NARROW], F32, "res_narrow%d" % pair)
-            factor = back_sb[:, 2 * pair : 2 * pair + 2].unsqueeze(2).to_broadcast([P, 2, NARROW])
-            sums = ps[:, 0 : 2 * NARROW].rearrange("p (e m) -> p e m", e=2)
-            nc.vector.tensor_tensor(res[:], sums, factor, ALU.mult)
-            rows = out[2 * P * pair : 2 * P * (pair + 1), WIDE:M]
-            nc.sync.dma_start(out=rows.rearrange("(e p) m -> p e m", p=P), in_=res[:])
+                make_h(k + 1, (1,) if k == 1 else (0, 1))
+                pick_want(k + 1)
+            make_damp(k)
+            pick_repl(*left(k))
+            pick_carr(*left(k - 1))
+            if k >= 2:
+                make_plane(*left(k - 2))
+            if k >= 6:
+                weave(left0, (k - 6) * P, P)
+        quantise_z(left0, 0, 2 * P)
+        all_banks(0, 0)
+        pick_carr(left1, 3)
+        make_plane(left1, 2)
+        make_plane(left1, 3)
+        for n in range(2, len(PARTS)):
+            part, before = PARTS[n], PARTS[n - 1]
+            pick_repl(part, 0)
+            for t in range(1, 4):
+                pick_repl(part, t)
+                pick_carr(part, t - 1)
+            pick_carr(part, 3)
+            weave(before, 0, before[1])
+            quantise_z(before, 0, before[1])
+            all_banks((n - 1) // 2, (n - 1) % 2)
+            for s, i in STORES.get(n, ()):
+                finish(s, i)
+            if part != end1:
+                for t in range(4):
+                    make_plane(part, t)
+        weave_last()
+        quantise_z(end1, 0, P)
+        for i in range(4):
+            second_passes(2, i, 1)
+            finish(2, i)

@@ -1,7 +1,6 @@
 from contextlib import ExitStack
 
 import concourse.mybir as mybir
-from concourse.masks import make_identity
 
 K, H, T, S, M = 1024, 1024, 4096, 1024, 512
 FLOPS = 2 * K * H * S + 2 * 2 * H * K * M
@@ -43,11 +42,7 @@ def tile_list_spice_substitution_kernel(
 
         tab_sc = kept([P, T], U8, "tab_sc")
         nc.vector.memset(tab_sc[:].bitcast(I32), 0)
-        for q in range(4):
-            nc.gpsimd.dma_start(
-                out=tab_sc[32 * q : 32 * q + 8, :].bitcast(I32),
-                in_=tab_scales[:, 4 * q : 4 * q + 4, :].bitcast(I32),
-            )
+        nc.sync.dma_start(out=tab_sc[0:P:4, :].bitcast(I32), in_=tab_scales.rearrange("a q t -> (a q) t").bitcast(I32))
 
         w_raw, tab = {}, {}
 
@@ -70,14 +65,16 @@ def tile_list_spice_substitution_kernel(
             pos_sb = keep.tile([P, M // 16], U16, name="pos_sb%d" % i)
             nc.sync.dma_start(pos_sb[:], pos)
             lists.append(pos_sb)
-        fade_sb = kept([P, 2, 4], F32, "fade_sb")
-        nc.sync.dma_start(out=fade_sb[:], in_=fade.rearrange("(b p t) -> p b t", b=2, t=4))
         lift_sb = kept([P, 2, 4], F32, "lift_sb")
         nc.sync.dma_start(out=lift_sb[:], in_=lift.rearrange("(b p t) -> p b t", b=2, t=4))
+        zeros = kept([P, P], F32, "zeros", "w_raw1")
+        nc.gpsimd.memset(zeros[:], 0.0)
+        ident = kept([P, P], F32, "ident")
+        nc.gpsimd.affine_select(
+            out=ident[:], in_=zeros[:], compare_op=ALU.not_equal, fill=1.0, base=0, pattern=[[-1, P]], channel_multiplier=1
+        )
         load_w(1, 0, 2, "w_raw1")
 
-        ident = kept([P, P], F32, "ident")
-        make_identity(nc, ident[:])
         neg_lift = kept([P, 8], F32, "neg_lift")
         nc.scalar.activation(out=neg_lift[:], in_=lift_sb[:].rearrange("p b t -> p (b t)"), func=ACT.Copy, scale=-1.0)
 
@@ -119,27 +116,44 @@ def tile_list_spice_substitution_kernel(
             cols = offs_sb[:, 32 * half : 32 * (half + 1)]
             nc.vector.tensor_copy(out=v_codes[a, half][:], in_=tab[a][:].bitcast(U32).indirect(cols))
 
+        v_sc = kept([P, S], U8, "v_sc")
+        picked_sc = kept([P, S], U8, "picked_sc")
+
+        def place_scales(a):
+            for q in range(4):
+                first = 4 * (16 * a + 4 * q)
+                nc.sync.dma_start(
+                    out=v_sc[32 * q + 4 * a : 32 * q + 4 * a + 4, :].bitcast(I32),
+                    in_=picked_sc[first : first + 16 : 4, :].bitcast(I32),
+                )
+
         chunks = [(a, b) for a in range(2) for b in range(2)]
         for a, b in chunks:
             group_w(a, b, nc.scalar.copy if (a, b) in GROUP_S else nc.vector.tensor_copy, 0, P)
+            if (a, b) == (0, 1):
+                nc.vector.tensor_copy(out=picked_sc[:], in_=tab_sc[:].indirect(offs_sb[:]))
+        for a, b in chunks:
             quantise_wk(a, b)
-        v_sc = kept([P, S], U8, "v_sc")
-        nc.vector.tensor_copy(out=v_sc[:], in_=tab_sc[:].indirect(offs_sb[:]))
         for a, b in chunks:
             turn_w(a, b, 0)
             turn_w(a, b, 1)
+        load_tab(0, "w_raw0")
+        place_scales(0)
+        load_tab(1, "tab_sc")
+        place_scales(1)
         for a in range(2):
-            load_tab(a, ("w_raw0", "grouped00")[a])
             for half in range(2):
                 gather_words(a, half)
         for a in range(2):
-            wr_pair = kept([P, 2, PASS], U32, "wr%d_codes" % a, ("w_raw0", "grouped00")[a])
+            wr_pair = kept([P, 2, PASS], U32, "wr%d_codes" % a, ("w_raw0", "tab_sc")[a])
             for b in range(2):
                 quantise_wr(a, b, wr_pair[:, b, :])
 
+        fade_sb = kept([P, 2, 4], F32, "fade_sb", "grouped01")
+        nc.sync.dma_start(out=fade_sb[:], in_=fade.rearrange("(b p t) -> p b t", b=2, t=4))
         c4 = kept([P, 2, 2 * K], U8, "c4", "w_raw1")
         nc.sync.dma_start(out=c4[:].bitcast(I32), in_=c4_words.rearrange("b p c -> p b c").bitcast(I32))
-        c4_sc = kept([P, 2, K], U8, "c4_sc", "grouped10")
+        c4_sc = kept([P, 2, K], U8, "c4_sc", "grouped00")
         nc.vector.memset(c4_sc[:].rearrange("p b n -> p (b n)").bitcast(I32), 0)
         for q in range(4):
             nc.sync.dma_start(

@@ -20,8 +20,8 @@ P = 128
 PASS = 512
 BANK = 512
 PARTS = ((0, 256, 0), (0, 256, 1), (256, 128, 0), (256, 128, 1), (384, 128, 0), (384, 128, 1))
-STORES = {3: ((0, 0), (0, 1)), 4: ((0, 2), (0, 3)), 5: ((1, 0), (1, 1))}
-GROUP_S = ((1, 1),)
+STORES = {3: ((0, 0), (0, 1)), 4: ((0, 2),), 5: ((0, 3), (1, 0), (1, 1))}
+GROUP_S = ((0, 1), (1, 1))
 SPANS = ((0, 256), (256, 128), (384, 128))
 SPAN_BANKS = ((4, 5, 6, 7), (0, 1), (2, 3, 4, 5))
 
@@ -32,6 +32,7 @@ def tile_list_spice_substitution_kernel(
     nc = tc.nc
     with ExitStack() as ctx:
         keep = ctx.enter_context(tc.tile_pool(name="keep", bufs=1))
+        shared = ctx.enter_context(tc.tile_pool(name="shared", bufs=1))
         psum = ctx.enter_context(tc.psum_pool(name="psum", bufs=1))
 
         def bank(i):
@@ -40,24 +41,26 @@ def tile_list_spice_substitution_kernel(
         def kept(shape, dtype, name, tag=None):
             return keep.tile(shape, dtype, name=name, tag=tag or name, align_bytes=64)
 
+        def placed(shape, dtype, name, offset):
+            return shared.tile(shape, dtype, name=name, align_bytes=64, offset=offset)
+
         tab_sc = kept([P, T], U8, "tab_sc")
         nc.vector.memset(tab_sc[:].bitcast(I32), 0)
         nc.sync.dma_start(out=tab_sc[0:P:4, :].bitcast(I32), in_=tab_scales.rearrange("a q t -> (a q) t").bitcast(I32))
 
         w_raw, tab = {}, {}
 
-        def load_w(a, first, count, tag):
-            tile = kept([P, 4, count * PASS], F32, "w_raw%d%d" % (a, first), tag)
+        def load_w(a, first, count, tile):
             rows = w[PASS * a : PASS * (a + 1), PASS * first : PASS * (first + count)]
             nc.sync.dma_start(out=tile[:], in_=rows.rearrange("(p i) r -> p i r", i=4))
             for b in range(count):
                 w_raw[a, first + b] = tile[:, :, PASS * b : PASS * (b + 1)]
 
-        def load_tab(a, tag):
-            tab[a] = kept([P, T], I32, "tab%d" % a, tag)
+        def load_tab(a, tile):
+            tab[a] = tile
             nc.sync.dma_start(out=tab[a][:], in_=tab_words[a].rearrange("p t i -> p (t i)").bitcast(I32))
 
-        load_w(0, 0, 2, "w_raw0")
+        load_w(0, 0, 2, kept([P, 4, H], F32, "w_raw0"))
         offs_sb = keep.tile([P, S // 16], U16, name="offs_sb")
         nc.sync.dma_start(offs_sb[:], offs)
         lists = []
@@ -65,18 +68,15 @@ def tile_list_spice_substitution_kernel(
             pos_sb = keep.tile([P, M // 16], U16, name="pos_sb%d" % i)
             nc.sync.dma_start(pos_sb[:], pos)
             lists.append(pos_sb)
-        lift_sb = kept([P, 2, 4], F32, "lift_sb")
-        nc.sync.dma_start(out=lift_sb[:], in_=lift.rearrange("(b p t) -> p b t", b=2, t=4))
-        zeros = kept([P, P], F32, "zeros", "w_raw1")
+        zeros = placed([P, P], F32, "zeros", 4 * T - 2 * P)
         nc.gpsimd.memset(zeros[:], 0.0)
         ident = kept([P, P], F32, "ident")
         nc.gpsimd.affine_select(
             out=ident[:], in_=zeros[:], compare_op=ALU.not_equal, fill=1.0, base=0, pattern=[[-1, P]], channel_multiplier=1
         )
-        load_w(1, 0, 2, "w_raw1")
+        load_w(1, 0, 2, placed([P, 4, H], F32, "w_raw1", 0))
+        load_tab(0, placed([P, T], I32, "tab0", 4 * T))
 
-        neg_lift = kept([P, 8], F32, "neg_lift")
-        nc.scalar.activation(out=neg_lift[:], in_=lift_sb[:].rearrange("p b t -> p (b t)"), func=ACT.Copy, scale=-1.0)
 
         wk_codes, wk_sc, wr_codes, wr_sc, grouped, turned, turn_banks = {}, {}, {}, {}, {}, {}, {}
 
@@ -86,6 +86,9 @@ def tile_list_spice_substitution_kernel(
             dst = grouped[a, b][:].rearrange("p (t m i) -> p m i t", t=4, i=4)
             src = w_raw[a, b].rearrange("p i (m t) -> p m i t", t=4)
             copy(out=dst[:, first : first + count], in_=src[:, first : first + count])
+
+        def cast_on_scalar(out, in_):
+            nc.scalar.activation(out=out, in_=in_, func=ACT.Copy)
 
         def quantise_wk(a, b):
             wk_codes[a, b] = kept([P, PASS], U32, "wk%d%d_codes" % (a, b))
@@ -116,20 +119,20 @@ def tile_list_spice_substitution_kernel(
             cols = offs_sb[:, 32 * half : 32 * (half + 1)]
             nc.vector.tensor_copy(out=v_codes[a, half][:], in_=tab[a][:].bitcast(U32).indirect(cols))
 
-        v_sc = kept([P, S], U8, "v_sc")
+        v_sc = [kept([P, S], U8, "v_sc%d" % a) for a in range(2)]
         picked_sc = kept([P, S], U8, "picked_sc")
 
         def place_scales(a):
             for q in range(4):
                 first = 4 * (16 * a + 4 * q)
                 nc.sync.dma_start(
-                    out=v_sc[32 * q + 4 * a : 32 * q + 4 * a + 4, :].bitcast(I32),
+                    out=v_sc[a][32 * q : 32 * q + 4, :].bitcast(I32),
                     in_=picked_sc[first : first + 16 : 4, :].bitcast(I32),
                 )
 
         chunks = [(a, b) for a in range(2) for b in range(2)]
         for a, b in chunks:
-            group_w(a, b, nc.scalar.copy if (a, b) in GROUP_S else nc.vector.tensor_copy, 0, P)
+            group_w(a, b, cast_on_scalar if (a, b) in GROUP_S else nc.vector.tensor_copy, 0, P)
             if (a, b) == (0, 1):
                 nc.vector.tensor_copy(out=picked_sc[:], in_=tab_sc[:].indirect(offs_sb[:]))
         for a, b in chunks:
@@ -137,21 +140,24 @@ def tile_list_spice_substitution_kernel(
         for a, b in chunks:
             turn_w(a, b, 0)
             turn_w(a, b, 1)
-        load_tab(0, "w_raw0")
         place_scales(0)
-        load_tab(1, "tab_sc")
+        load_tab(1, kept([P, T], I32, "tab1", "tab_sc"))
         place_scales(1)
         for a in range(2):
             for half in range(2):
                 gather_words(a, half)
         for a in range(2):
-            wr_pair = kept([P, 2, PASS], U32, "wr%d_codes" % a, ("w_raw0", "tab_sc")[a])
+            wr_pair = placed([P, 2, PASS], U32, "wr0_codes", 4 * T) if a == 0 else kept([P, 2, PASS], U32, "wr1_codes", "tab_sc")
             for b in range(2):
                 quantise_wr(a, b, wr_pair[:, b, :])
 
         fade_sb = kept([P, 2, 4], F32, "fade_sb", "grouped01")
         nc.sync.dma_start(out=fade_sb[:], in_=fade.rearrange("(b p t) -> p b t", b=2, t=4))
-        c4 = kept([P, 2, 2 * K], U8, "c4", "w_raw1")
+        lift_sb = kept([P, 2, 4], F32, "lift_sb", "w_raw0")
+        nc.sync.dma_start(out=lift_sb[:], in_=lift.rearrange("(b p t) -> p b t", b=2, t=4))
+        neg_lift = kept([P, 8], F32, "neg_lift")
+        nc.scalar.activation(out=neg_lift[:], in_=lift_sb[:].rearrange("p b t -> p (b t)"), func=ACT.Copy, scale=-1.0)
+        c4 = placed([P, 2, 2 * K], U8, "c4", 0)
         nc.sync.dma_start(out=c4[:].bitcast(I32), in_=c4_words.rearrange("b p c -> p b c").bitcast(I32))
         c4_sc = kept([P, 2, K], U8, "c4_sc", "grouped00")
         nc.vector.memset(c4_sc[:].rearrange("p b n -> p (b n)").bitcast(I32), 0)
@@ -166,24 +172,34 @@ def tile_list_spice_substitution_kernel(
 
         h = {}
 
-        def make_h(k, halves=(0, 1)):
+        h_banks = {}
+
+        def first_pass(k, half, a):
             b, t = divmod(k, 4)
-            if 0 in halves:
+            if a == 0:
+                h_banks[k, half] = bank(2 * (k if k < 4 else k % 2) + half)
+            cols = slice(P * t, P * (t + 1))
+            nc.tensor.matmul_mx(
+                out=h_banks[k, half][:],
+                lhsT=wk_codes[a, b][:, cols].bitcast(FP8X4),
+                lhsT_scale=wk_sc[a, b][:, cols],
+                rhs=v_codes[a, half][:].bitcast(FP8X4),
+                rhs_scale=v_sc[a][:, BANK * half : BANK * (half + 1)],
+                start=(a == 0),
+                stop=(a == 1),
+            )
+
+        def finish_h(k, half):
+            first_pass(k, half, 1)
+            if half == 0:
                 h[k] = kept([P, S], F32, "h%d" % k)
-            for half in halves:
-                ps = bank(2 * (k % 2) + half)
-                for a in range(2):
-                    cols = slice(P * t, P * (t + 1))
-                    nc.tensor.matmul_mx(
-                        out=ps[:],
-                        lhsT=wk_codes[a, b][:, cols].bitcast(FP8X4),
-                        lhsT_scale=wk_sc[a, b][:, cols],
-                        rhs=v_codes[a, half][:].bitcast(FP8X4),
-                        rhs_scale=v_sc[4 * a :, BANK * half : BANK * (half + 1)],
-                        start=(a == 0),
-                        stop=(a == 1),
-                    )
-                nc.scalar.copy(out=h[k][:, BANK * half : BANK * (half + 1)], in_=ps[:])
+            nc.scalar.copy(out=h[k][:, BANK * half : BANK * (half + 1)], in_=h_banks[k, half][:])
+
+        def make_h(k):
+            for half in range(2):
+                if k >= 4:
+                    first_pass(k, half, 0)
+                finish_h(k, half)
 
         slots = [kept([P, M], F32, "slot%d" % i) for i in range(3)]
         prods = [kept([P, M // 2], F32, "prods%d" % i) for i in range(3)]
@@ -212,7 +228,8 @@ def tile_list_spice_substitution_kernel(
         def prod_of(part, t):
             if part[0] == 0:
                 return prods[(4 * part[2] + t) % 3][:]
-            return stage[PARTS[PARTS.index(part) - 2]][:, t, P:]
+            back_by = 1 if (part, t) == (end1, 3) else 2
+            return stage[PARTS[PARTS.index(part) - back_by]][:, t, P:]
 
         def diff_of(part, t):
             if part[0] == 0:
@@ -313,16 +330,19 @@ def tile_list_spice_substitution_kernel(
         def left(k):
             return PARTS[k // 4], k % 4
 
-        make_h(0)
-        make_h(1)
+        for k in range(4):
+            for half in range(2):
+                first_pass(k, half, 0)
+        for half in range(2):
+            for k in range(2):
+                finish_h(k, half)
         pick_want(0)
         pick_want(1)
-        make_h(2, (0,))
         make_damp(0)
         pick_repl(*left(0))
         for k in range(1, 8):
             if k + 1 < 8:
-                make_h(k + 1, (1,) if k == 1 else (0, 1))
+                make_h(k + 1)
                 pick_want(k + 1)
             make_damp(k)
             pick_repl(*left(k))
@@ -338,14 +358,21 @@ def tile_list_spice_substitution_kernel(
         make_plane(left1, 3)
         for n in range(2, len(PARTS)):
             part, before = PARTS[n], PARTS[n - 1]
+            held = 1 if part == end1 else 0
             pick_repl(part, 0)
             for t in range(1, 4):
-                pick_repl(part, t)
+                if t < 4 - held:
+                    pick_repl(part, t)
                 pick_carr(part, t - 1)
-            pick_carr(part, 3)
+            if not held:
+                pick_carr(part, 3)
             weave(before, 0, before[1])
+            if held:
+                pick_repl(part, 3)
             quantise_z(before, 0, before[1])
             all_banks((n - 1) // 2, (n - 1) % 2)
+            if held:
+                pick_carr(part, 3)
             for s, i in STORES.get(n, ()):
                 finish(s, i)
             if part != end1:

@@ -19,9 +19,11 @@ ACT = mybir.ActivationFunctionType
 P = 128
 PASS = 512
 BANK = 512
-PARTS = ((0, 256, 0), (0, 256, 1), (256, 128, 0), (256, 128, 1), (384, 128, 0), (384, 128, 1))
-STORES = {3: ((0, 0), (0, 1)), 4: ((0, 2),), 5: ((0, 3), (1, 0), (1, 1))}
-GROUP_S = ((0, 1), (1, 1))
+PARTS = ((0, 384, 0), (0, 256, 1), (256, 128, 1), (384, 128, 0), (384, 128, 1))
+STORES = {3: ((0, 0), (0, 1)), 4: ((0, 2), (0, 3), (1, 0), (1, 1))}
+GROUP_S = ((0, 1),)
+LATE = 6 * T
+TURN = (1, 2)
 SPANS = ((0, 256), (256, 128), (384, 128))
 SPAN_BANKS = ((4, 5, 6, 7), (0, 1), (2, 3, 4, 5))
 
@@ -44,7 +46,7 @@ def tile_list_spice_substitution_kernel(
         def placed(shape, dtype, name, offset):
             return shared.tile(shape, dtype, name=name, align_bytes=64, offset=offset)
 
-        tab_sc = kept([P, T], U8, "tab_sc")
+        tab_sc = placed([P, T], U8, "tab_sc", LATE + 4 * T - T // 2)
         nc.vector.memset(tab_sc[:].bitcast(I32), 0)
         nc.sync.dma_start(out=tab_sc[0:P:4, :].bitcast(I32), in_=tab_scales.rearrange("a q t -> (a q) t").bitcast(I32))
 
@@ -68,14 +70,14 @@ def tile_list_spice_substitution_kernel(
             pos_sb = keep.tile([P, M // 16], U16, name="pos_sb%d" % i)
             nc.sync.dma_start(pos_sb[:], pos)
             lists.append(pos_sb)
-        zeros = placed([P, P], F32, "zeros", 4 * T - 2 * P)
+        zeros = placed([P, P], F32, "zeros", 2 * T - 2 * P)
         nc.gpsimd.memset(zeros[:], 0.0)
         ident = kept([P, P], F32, "ident")
         nc.gpsimd.affine_select(
             out=ident[:], in_=zeros[:], compare_op=ALU.not_equal, fill=1.0, base=0, pattern=[[-1, P]], channel_multiplier=1
         )
-        load_w(1, 0, 2, placed([P, 4, H], F32, "w_raw1", 0))
-        load_tab(0, placed([P, T], I32, "tab0", 4 * T))
+        load_w(1, 0, 1, placed([P, 4, PASS], F32, "w_raw10", 0))
+        load_tab(0, placed([P, T], I32, "tab0", 2 * T))
 
 
         wk_codes, wk_sc, wr_codes, wr_sc, grouped, turned, turn_banks = {}, {}, {}, {}, {}, {}, {}
@@ -91,7 +93,8 @@ def tile_list_spice_substitution_kernel(
             nc.scalar.activation(out=out, in_=in_, func=ACT.Copy)
 
         def quantise_wk(a, b):
-            wk_codes[a, b] = kept([P, PASS], U32, "wk%d%d_codes" % (a, b))
+            name = "wk%d%d_codes" % (a, b)
+            wk_codes[a, b] = placed([P, PASS], U32, name, LATE + 4 * T + 64) if (a, b) == (1, 1) else kept([P, PASS], U32, name)
             wk_sc[a, b] = kept([P, PASS], U8, "wk%d%d_sc" % (a, b))
             nc.vector.quantize_mx(out=wk_codes[a, b][:].bitcast(FP8X4), scales=wk_sc[a, b][:], in_=grouped[a, b][:])
 
@@ -99,7 +102,7 @@ def tile_list_spice_substitution_kernel(
             words = grouped[a, b][:].bitcast(F32).rearrange("p (t m u) -> p t m u", t=4, u=2)
             if u == 0:
                 turned[a, b] = kept([P, 4 * PASS], BF16, "turned%d%d" % (a, b))
-            ps = bank(4 + 2 * b + u)
+            ps = bank(min(2 * (2 * a + b), 4) + u)
             for t in range(4):
                 nc.tensor.transpose(ps[:, P * t : P * (t + 1)], words[:, t, :, u], ident[:])
             nc.scalar.copy(
@@ -107,7 +110,8 @@ def tile_list_spice_substitution_kernel(
                 in_=ps[:].bitcast(BF16).rearrange("m (t p e) -> m p e t", t=4, e=2),
             )
 
-        def quantise_wr(a, b, codes):
+        def quantise_wr(a, b):
+            codes = wr_all[:, b, :] if a == 0 else placed([P, PASS], U32, "wr1%d_codes" % b, (4 * T, LATE)[b])[:]
             wr_codes[a, b] = codes
             wr_sc[a, b] = kept([P, PASS], U8, "wr%d%d_sc" % (a, b))
             nc.vector.quantize_mx(out=codes.bitcast(FP8X4), scales=wr_sc[a, b][:], in_=turned[a, b][:])
@@ -130,7 +134,7 @@ def tile_list_spice_substitution_kernel(
                     in_=picked_sc[first : first + 16 : 4, :].bitcast(I32),
                 )
 
-        chunks = [(a, b) for a in range(2) for b in range(2)]
+        chunks = [(0, 0), (0, 1), (1, 0)]
         for a, b in chunks:
             group_w(a, b, cast_on_scalar if (a, b) in GROUP_S else nc.vector.tensor_copy, 0, P)
             if (a, b) == (0, 1):
@@ -141,34 +145,33 @@ def tile_list_spice_substitution_kernel(
             turn_w(a, b, 0)
             turn_w(a, b, 1)
         place_scales(0)
-        load_tab(1, kept([P, T], I32, "tab1", "tab_sc"))
+        load_tab(1, placed([P, T], I32, "tab1", LATE))
         place_scales(1)
+        fade_sb = placed([P, 2, 4], F32, "fade_sb", LATE + 4 * T)
+        nc.sync.dma_start(out=fade_sb[:], in_=fade.rearrange("(b p t) -> p b t", b=2, t=4))
+        load_w(1, 1, 1, placed([P, 4, PASS], F32, "w_raw11", LATE + 4 * T + 64))
+        lift_sb = kept([P, 2, 4], F32, "lift_sb", "grouped01")
+        nc.sync.dma_start(out=lift_sb[:], in_=lift.rearrange("(b p t) -> p b t", b=2, t=4))
         for a in range(2):
             for half in range(2):
                 gather_words(a, half)
-        for a in range(2):
-            wr_pair = placed([P, 2, PASS], U32, "wr0_codes", 4 * T) if a == 0 else kept([P, 2, PASS], U32, "wr1_codes", "tab_sc")
-            for b in range(2):
-                quantise_wr(a, b, wr_pair[:, b, :])
+        wr_all = kept([P, 2, PASS], U32, "wr_codes", "w_raw0")
+        for a, b in chunks[:2]:
+            quantise_wr(a, b)
 
-        fade_sb = kept([P, 2, 4], F32, "fade_sb", "grouped01")
-        nc.sync.dma_start(out=fade_sb[:], in_=fade.rearrange("(b p t) -> p b t", b=2, t=4))
-        lift_sb = kept([P, 2, 4], F32, "lift_sb", "w_raw0")
-        nc.sync.dma_start(out=lift_sb[:], in_=lift.rearrange("(b p t) -> p b t", b=2, t=4))
         neg_lift = kept([P, 8], F32, "neg_lift")
-        nc.scalar.activation(out=neg_lift[:], in_=lift_sb[:].rearrange("p b t -> p (b t)"), func=ACT.Copy, scale=-1.0)
-        c4 = placed([P, 2, 2 * K], U8, "c4", 0)
+        nc.gpsimd.tensor_scalar(
+            out=neg_lift[:], in0=lift_sb[:].rearrange("p b t -> p (b t)"), scalar1=-1.0, scalar2=0.0, op0=ALU.mult, op1=ALU.add
+        )
+        c4 = placed([P, 2, 2 * K], U8, "c4", 2 * T)
         nc.sync.dma_start(out=c4[:].bitcast(I32), in_=c4_words.rearrange("b p c -> p b c").bitcast(I32))
-        c4_sc = kept([P, 2, K], U8, "c4_sc", "grouped00")
-        nc.vector.memset(c4_sc[:].rearrange("p b n -> p (b n)").bitcast(I32), 0)
+        c4_sc = kept([P, 2, K], U8, "c4_sc", "turned01")
+        nc.gpsimd.memset(c4_sc[:].rearrange("p b n -> p (b n)").bitcast(I32), 0)
         for q in range(4):
             nc.sync.dma_start(
                 out=c4_sc[32 * q : 32 * q + 4, :, :].bitcast(I32),
                 in_=c4_scales[:, 4 * q : 4 * q + 4, :].rearrange("b r n -> r b n").bitcast(I32),
             )
-        back_sb = kept([P, 8], F32, "back_sb", "grouped11")
-        with nc.allow_non_contiguous_dma(reason="one factor for each output row"):
-            nc.sync.dma_start(out=back_sb[:], in_=back.rearrange("(j p) -> p j", p=P))
 
         h = {}
 
@@ -201,20 +204,26 @@ def tile_list_spice_substitution_kernel(
                     first_pass(k, half, 0)
                 finish_h(k, half)
 
-        slots = [kept([P, M], F32, "slot%d" % i) for i in range(3)]
-        prods = [kept([P, M // 2], F32, "prods%d" % i) for i in range(3)]
+        after_late = LATE + 4 * T + 64
+        first_want = placed([P, M], F32, "first_want", after_late)
+        slots = [placed([P, M], F32, "slot%d" % i, after_late + 4 * M * (i + 1)) for i in range(3)]
+
+        def want_of(k):
+            return first_want if k == 0 else slots[k % 3]
+
+        prods = [kept([P, 3 * P], F32, "prods%d" % i) for i in range(3)]
         damp = {}
 
         def picked(k, which, first, width):
             return h[k][:].indirect(lists[which][:, first // 16 : (first + width) // 16])
 
         def pick_want(k):
-            nc.vector.tensor_copy(out=slots[k % 3][:], in_=picked(k, 0, 0, M))
+            nc.vector.tensor_copy(out=want_of(k)[:], in_=picked(k, 0, 0, M))
 
         def make_damp(k):
             b, t = divmod(k, 4)
             damp[k] = kept([P, M], F32, "damp%d" % k)
-            nc.scalar.activation(out=damp[k][:], in_=slots[k % 3][:], func=ACT.Exp, scale=fade_sb[:, b, t : t + 1])
+            nc.scalar.activation(out=damp[k][:], in_=want_of(k)[:], func=ACT.Exp, scale=fade_sb[:, b, t : t + 1])
 
         left0, left1, end1 = PARTS[0], PARTS[1], PARTS[-1]
         stage = {part: kept([P, 4, 2 * P], F32, "stage%d_%d" % part[::2]) for part in PARTS[:-1]}
@@ -227,7 +236,7 @@ def tile_list_spice_substitution_kernel(
 
         def prod_of(part, t):
             if part[0] == 0:
-                return prods[(4 * part[2] + t) % 3][:]
+                return prods[(4 * part[2] + t) % 3][:, 0 : part[1]]
             back_by = 1 if (part, t) == (end1, 3) else 2
             return stage[PARTS[PARTS.index(part) - back_by]][:, t, P:]
 
@@ -279,7 +288,7 @@ def tile_list_spice_substitution_kernel(
             per_bank = 8 // len(SPAN_BANKS[s])
             if b == 0:
                 sums[s, i] = bank(SPAN_BANKS[s][i])
-            part = PARTS[2 * s + b]
+            part = PARTS[((0, 0, 3), (1, 2, 4))[b][s]]
             at = first - part[0]
             passes = []
             for e in range(per_bank):
@@ -336,23 +345,39 @@ def tile_list_spice_substitution_kernel(
         for half in range(2):
             for k in range(2):
                 finish_h(k, half)
+        make_h(2)
+        make_h(3)
+        group_w(1, 1, nc.vector.tensor_copy, 0, P)
         pick_want(0)
+        quantise_wr(1, 0)
         pick_want(1)
+        back_sb = kept([P, 8], F32, "back_sb", "turned10")
+        with nc.allow_non_contiguous_dma(reason="one factor for each output row"):
+            nc.sync.dma_start(out=back_sb[:], in_=back.rearrange("(j p) -> p j", p=P))
         make_damp(0)
+        quantise_wk(1, 1)
         pick_repl(*left(0))
         for k in range(1, 8):
             if k + 1 < 8:
-                make_h(k + 1)
                 pick_want(k + 1)
             make_damp(k)
             pick_repl(*left(k))
             pick_carr(*left(k - 1))
+            if k in TURN:
+                turn_w(1, 1, TURN.index(k))
+            if k == TURN[1]:
+                quantise_wr(1, 1)
+            if 4 <= k + 2 < 8:
+                make_h(k + 2)
             if k >= 2:
                 make_plane(*left(k - 2))
-            if k >= 6:
-                weave(left0, (k - 6) * P, P)
-        quantise_z(left0, 0, 2 * P)
-        all_banks(0, 0)
+            if k >= 5:
+                weave(left0, (k - 5) * P, P)
+            if k == 6:
+                quantise_z(left0, 0, 2 * P)
+                all_banks(0, 0)
+        quantise_z(left0, 2 * P, P)
+        all_banks(1, 0)
         pick_carr(left1, 3)
         make_plane(left1, 2)
         make_plane(left1, 3)
@@ -370,7 +395,7 @@ def tile_list_spice_substitution_kernel(
             if held:
                 pick_repl(part, 3)
             quantise_z(before, 0, before[1])
-            all_banks((n - 1) // 2, (n - 1) % 2)
+            all_banks(n - 2, before[2])
             if held:
                 pick_carr(part, 3)
             for s, i in STORES.get(n, ()):

@@ -165,13 +165,6 @@ def tile_list_spice_substitution_kernel(
         )
         c4 = placed([P, 2, 2 * K], U8, "c4", 2 * T)
         nc.sync.dma_start(out=c4[:].bitcast(I32), in_=c4_words.rearrange("b p c -> p b c").bitcast(I32))
-        c4_sc = kept([P, 2, K], U8, "c4_sc", "turned01")
-        nc.gpsimd.memset(c4_sc[:].rearrange("p b n -> p (b n)").bitcast(I32), 0)
-        for q in range(4):
-            nc.sync.dma_start(
-                out=c4_sc[32 * q : 32 * q + 4, :, :].bitcast(I32),
-                in_=c4_scales[:, 4 * q : 4 * q + 4, :].rearrange("b r n -> r b n").bitcast(I32),
-            )
 
         h = {}
 
@@ -250,9 +243,11 @@ def tile_list_spice_substitution_kernel(
             k = 4 * b + t
             nc.vector.tensor_tensor(prod_of(part, t), picked(k, 1, first, width), damp[k][:, first : first + width], ALU.mult)
 
-        def pick_carr(part, t):
+        def pick_carr(part, t, at=0, count=None):
             first, width, b = part
-            nc.vector.tensor_tensor(diff_of(part, t), picked(4 * b + t, 2, first, width), prod_of(part, t), ALU.subtract)
+            cols = slice(at, at + (count or width))
+            carr = picked(4 * b + t, 2, first + at, count or width)
+            nc.vector.tensor_tensor(diff_of(part, t)[:, cols], carr, prod_of(part, t)[:, cols], ALU.subtract)
 
         def make_plane(part, t):
             k = 4 * part[2] + t
@@ -270,10 +265,10 @@ def tile_list_spice_substitution_kernel(
             src = planes(part)[:, :, at : at + count].rearrange("p t (c i) -> p c t i", i=4)
             copy(out=woven_view(part, at, count), in_=src)
 
-        def weave_last():
-            src = diffs[end1][:].rearrange("p t (c i) -> p c t i", i=4)
-            factor = neg_lift[:, 4:8].unsqueeze(1).unsqueeze(3).to_broadcast([P, P // 4, 4, 4])
-            nc.vector.tensor_tensor(woven_view(end1, 0, P), src, factor, ALU.mult)
+        def weave_last(at, count):
+            src = diffs[end1][:, :, at : at + count].rearrange("p t (c i) -> p c t i", i=4)
+            factor = neg_lift[:, 4:8].unsqueeze(1).unsqueeze(3).to_broadcast([P, count // 4, 4, 4])
+            nc.vector.tensor_tensor(woven_view(end1, at, count), src, factor, ALU.mult)
 
         def quantise_z(part, at, count):
             cols = slice(at, at + count)
@@ -349,6 +344,13 @@ def tile_list_spice_substitution_kernel(
         make_h(3)
         group_w(1, 1, nc.vector.tensor_copy, 0, P)
         pick_want(0)
+        c4_sc = placed([P, 2, K], U8, "c4_sc", 5 * T)
+        nc.vector.memset(c4_sc[:].rearrange("p b n -> p (b n)").bitcast(I32), 0)
+        for q in range(4):
+            nc.sync.dma_start(
+                out=c4_sc[32 * q : 32 * q + 4, :, :].bitcast(I32),
+                in_=c4_scales[:, 4 * q : 4 * q + 4, :].rearrange("b r n -> r b n").bitcast(I32),
+            )
         quantise_wr(1, 0)
         pick_want(1)
         back_sb = kept([P, 8], F32, "back_sb", "turned10")
@@ -397,14 +399,17 @@ def tile_list_spice_substitution_kernel(
             quantise_z(before, 0, before[1])
             all_banks(n - 2, before[2])
             if held:
-                pick_carr(part, 3)
+                for at in (0, P // 2):
+                    pick_carr(part, 3, at, P // 2)
             for s, i in STORES.get(n, ()):
                 finish(s, i)
             if part != end1:
                 for t in range(4):
                     make_plane(part, t)
-        weave_last()
-        quantise_z(end1, 0, P)
+        for at in (0, P // 2):
+            weave_last(at, P // 2)
+        for at in (0, P // 2):
+            quantise_z(end1, at, P // 2)
         for i in range(4):
             second_passes(2, i, 1)
             finish(2, i)

@@ -21,9 +21,8 @@ PASS = 512
 BANK = 512
 PARTS = ((0, 384, 0), (0, 256, 1), (256, 128, 1), (384, 128, 0), (384, 128, 1))
 STORES = {3: ((0, 0), (0, 1)), 4: ((0, 2), (0, 3), (1, 0), (1, 1))}
-GROUP_S = ((0, 1),)
+GROUP_S = ((0, 0),)
 LATE = 6 * T
-TURN = (1, 2)
 SPANS = ((0, 256), (256, 128), (384, 128))
 SPAN_BANKS = ((4, 5, 6, 7), (0, 1), (2, 3, 4, 5))
 
@@ -62,7 +61,7 @@ def tile_list_spice_substitution_kernel(
             tab[a] = tile
             nc.sync.dma_start(out=tab[a][:], in_=tab_words[a].rearrange("p t i -> p (t i)").bitcast(I32))
 
-        load_w(0, 0, 2, kept([P, 4, H], F32, "w_raw0"))
+        load_w(0, 0, 1, kept([P, 4, PASS], F32, "w_raw00"))
         offs_sb = keep.tile([P, S // 16], U16, name="offs_sb")
         nc.sync.dma_start(offs_sb[:], offs)
         lists = []
@@ -94,7 +93,7 @@ def tile_list_spice_substitution_kernel(
 
         def quantise_wk(a, b):
             name = "wk%d%d_codes" % (a, b)
-            wk_codes[a, b] = placed([P, PASS], U32, name, LATE + 4 * T + 64) if (a, b) == (1, 1) else kept([P, PASS], U32, name)
+            wk_codes[a, b] = placed([P, PASS], U32, name, LATE + 4 * T + 64) if (a, b) == (0, 1) else kept([P, PASS], U32, name)
             wk_sc[a, b] = kept([P, PASS], U8, "wk%d%d_sc" % (a, b))
             nc.vector.quantize_mx(out=wk_codes[a, b][:].bitcast(FP8X4), scales=wk_sc[a, b][:], in_=grouped[a, b][:])
 
@@ -102,7 +101,7 @@ def tile_list_spice_substitution_kernel(
             words = grouped[a, b][:].bitcast(F32).rearrange("p (t m u) -> p t m u", t=4, u=2)
             if u == 0:
                 turned[a, b] = kept([P, 4 * PASS], BF16, "turned%d%d" % (a, b))
-            ps = bank(min(2 * (2 * a + b), 4) + u)
+            ps = bank(4 * b + 2 * a + u)
             for t in range(4):
                 nc.tensor.transpose(ps[:, P * t : P * (t + 1)], words[:, t, :, u], ident[:])
             nc.scalar.copy(
@@ -111,7 +110,7 @@ def tile_list_spice_substitution_kernel(
             )
 
         def quantise_wr(a, b):
-            codes = wr_all[:, b, :] if a == 0 else placed([P, PASS], U32, "wr1%d_codes" % b, (4 * T, LATE)[b])[:]
+            codes = placed([P, PASS], U32, "wr%d%d_codes" % (a, b), (4 * T, LATE)[b] + 4 * PASS * a)[:]
             wr_codes[a, b] = codes
             wr_sc[a, b] = kept([P, PASS], U8, "wr%d%d_sc" % (a, b))
             nc.vector.quantize_mx(out=codes.bitcast(FP8X4), scales=wr_sc[a, b][:], in_=turned[a, b][:])
@@ -124,7 +123,6 @@ def tile_list_spice_substitution_kernel(
             nc.vector.tensor_copy(out=v_codes[a, half][:], in_=tab[a][:].bitcast(U32).indirect(cols))
 
         v_sc = [kept([P, S], U8, "v_sc%d" % a) for a in range(2)]
-        picked_sc = kept([P, S], U8, "picked_sc")
 
         def place_scales(a):
             for q in range(4):
@@ -134,10 +132,11 @@ def tile_list_spice_substitution_kernel(
                     in_=picked_sc[first : first + 16 : 4, :].bitcast(I32),
                 )
 
-        chunks = [(0, 0), (0, 1), (1, 0)]
+        chunks = [(0, 0), (1, 0)]
         for a, b in chunks:
             group_w(a, b, cast_on_scalar if (a, b) in GROUP_S else nc.vector.tensor_copy, 0, P)
-            if (a, b) == (0, 1):
+            if (a, b) == (0, 0):
+                picked_sc = kept([P, S], U8, "picked_sc", "w_raw00")
                 nc.vector.tensor_copy(out=picked_sc[:], in_=tab_sc[:].indirect(offs_sb[:]))
         for a, b in chunks:
             quantise_wk(a, b)
@@ -149,21 +148,17 @@ def tile_list_spice_substitution_kernel(
         place_scales(1)
         fade_sb = placed([P, 2, 4], F32, "fade_sb", LATE + 4 * T)
         nc.sync.dma_start(out=fade_sb[:], in_=fade.rearrange("(b p t) -> p b t", b=2, t=4))
-        load_w(1, 1, 1, placed([P, 4, PASS], F32, "w_raw11", LATE + 4 * T + 64))
-        lift_sb = kept([P, 2, 4], F32, "lift_sb", "grouped01")
-        nc.sync.dma_start(out=lift_sb[:], in_=lift.rearrange("(b p t) -> p b t", b=2, t=4))
+        load_w(0, 1, 1, placed([P, 4, PASS], F32, "w_raw01", LATE + 4 * T + 64))
+        load_w(1, 1, 1, kept([P, 4, PASS], F32, "w_raw11", "w_raw00"))
         for a in range(2):
             for half in range(2):
                 gather_words(a, half)
-        wr_all = kept([P, 2, PASS], U32, "wr_codes", "w_raw0")
-        for a, b in chunks[:2]:
+        for a, b in chunks:
             quantise_wr(a, b)
 
-        neg_lift = kept([P, 8], F32, "neg_lift")
-        nc.gpsimd.tensor_scalar(
-            out=neg_lift[:], in0=lift_sb[:].rearrange("p b t -> p (b t)"), scalar1=-1.0, scalar2=0.0, op0=ALU.mult, op1=ALU.add
-        )
-        c4 = placed([P, 2, 2 * K], U8, "c4", 2 * T)
+        lift_sb = placed([P, 2, 4], F32, "lift_sb", 5 * T + 2 * K)
+        nc.sync.dma_start(out=lift_sb[:], in_=lift.rearrange("(b p t) -> p b t", b=2, t=4))
+        c4 = placed([P, 2, 2 * K], U8, "c4", LATE + T)
         nc.sync.dma_start(out=c4[:].bitcast(I32), in_=c4_words.rearrange("b p c -> p b c").bitcast(I32))
 
         h = {}
@@ -342,7 +337,7 @@ def tile_list_spice_substitution_kernel(
                 finish_h(k, half)
         make_h(2)
         make_h(3)
-        group_w(1, 1, nc.vector.tensor_copy, 0, P)
+        group_w(0, 1, nc.vector.tensor_copy, 0, P)
         pick_want(0)
         c4_sc = placed([P, 2, K], U8, "c4_sc", 5 * T)
         nc.vector.memset(c4_sc[:].rearrange("p b n -> p (b n)").bitcast(I32), 0)
@@ -351,33 +346,61 @@ def tile_list_spice_substitution_kernel(
                 out=c4_sc[32 * q : 32 * q + 4, :, :].bitcast(I32),
                 in_=c4_scales[:, 4 * q : 4 * q + 4, :].rearrange("b r n -> r b n").bitcast(I32),
             )
-        quantise_wr(1, 0)
         pick_want(1)
-        back_sb = kept([P, 8], F32, "back_sb", "turned10")
-        with nc.allow_non_contiguous_dma(reason="one factor for each output row"):
-            nc.sync.dma_start(out=back_sb[:], in_=back.rearrange("(j p) -> p j", p=P))
-        make_damp(0)
-        quantise_wk(1, 1)
-        pick_repl(*left(0))
-        for k in range(1, 8):
-            if k + 1 < 8:
-                pick_want(k + 1)
+
+        def turn_late(n):
+            a, u = divmod(n, 2)
+            turn_w(a, 1, u)
+            if u == 1:
+                quantise_wr(a, 1)
+
+        def step(k):
             make_damp(k)
             pick_repl(*left(k))
             pick_carr(*left(k - 1))
-            if k in TURN:
-                turn_w(1, 1, TURN.index(k))
-            if k == TURN[1]:
-                quantise_wr(1, 1)
-            if 4 <= k + 2 < 8:
-                make_h(k + 2)
-            if k >= 2:
-                make_plane(*left(k - 2))
-            if k >= 5:
-                weave(left0, (k - 5) * P, P)
-            if k == 6:
-                quantise_z(left0, 0, 2 * P)
-                all_banks(0, 0)
+
+        def ahead(k):
+            make_plane(*left(k - 4))
+            pick_want(k)
+
+        make_damp(0)
+        neg_lift = kept([P, 8], F32, "neg_lift")
+        nc.scalar.activation(out=neg_lift[:], in_=lift_sb[:].rearrange("p b t -> p (b t)"), func=ACT.Copy, scale=-1.0)
+        quantise_wk(0, 1)
+        pick_repl(*left(0))
+        pick_want(2)
+        step(1)
+        group_w(1, 1, cast_on_scalar, 0, P)
+        quantise_wk(1, 1)
+        pick_want(3)
+        step(2)
+        turn_late(0)
+        step(3)
+        turn_late(1)
+        back_sb = kept([P, 8], F32, "back_sb", "grouped01")
+        with nc.allow_non_contiguous_dma(reason="one factor for each output row"):
+            nc.sync.dma_start(out=back_sb[:], in_=back.rearrange("(j p) -> p j", p=P))
+        make_h(4)
+        ahead(4)
+        make_h(5)
+        ahead(5)
+        turn_late(2)
+        step(4)
+        make_h(6)
+        ahead(6)
+        step(5)
+        turn_late(3)
+        make_h(7)
+        ahead(7)
+        weave(left0, 0, P)
+        step(6)
+        make_plane(left1, 0)
+        weave(left0, P, P)
+        quantise_z(left0, 0, 2 * P)
+        all_banks(0, 0)
+        step(7)
+        make_plane(left1, 1)
+        weave(left0, 2 * P, P)
         quantise_z(left0, 2 * P, P)
         all_banks(1, 0)
         pick_carr(left1, 3)

@@ -19,12 +19,10 @@ ACT = mybir.ActivationFunctionType
 P = 128
 PASS = 512
 BANK = 512
-PARTS = ((0, 384, 0), (0, 256, 1), (256, 128, 1), (384, 128, 0), (384, 128, 1))
-STORES = {3: ((0, 0), (0, 1)), 4: ((0, 2), (0, 3), (1, 0), (1, 1))}
 GROUP_S = ((0, 0),)
 LATE = 6 * T
 SPANS = ((0, 256), (256, 128), (384, 128))
-SPAN_BANKS = ((4, 5, 6, 7), (0, 1), (2, 3, 4, 5))
+SPAN_BANKS = (((4, 0, 2), (5, 2, 2), (6, 4, 2), (7, 6, 2)), ((0, 0, 4), (1, 4, 4)), ((2, 0, 3), (3, 3, 3), (4, 6, 2)))
 
 
 def tile_list_spice_substitution_kernel(
@@ -93,7 +91,7 @@ def tile_list_spice_substitution_kernel(
 
         def quantise_wk(a, b):
             name = "wk%d%d_codes" % (a, b)
-            wk_codes[a, b] = placed([P, PASS], U32, name, LATE + 4 * T + 64) if (a, b) == (0, 1) else kept([P, PASS], U32, name)
+            wk_codes[a, b] = kept([P, PASS], U32, name)
             wk_sc[a, b] = kept([P, PASS], U8, "wk%d%d_sc" % (a, b))
             nc.vector.quantize_mx(out=wk_codes[a, b][:].bitcast(FP8X4), scales=wk_sc[a, b][:], in_=grouped[a, b][:])
 
@@ -101,7 +99,7 @@ def tile_list_spice_substitution_kernel(
             words = grouped[a, b][:].bitcast(F32).rearrange("p (t m u) -> p t m u", t=4, u=2)
             if u == 0:
                 turned[a, b] = kept([P, 4 * PASS], BF16, "turned%d%d" % (a, b))
-            ps = bank(4 * b + 2 * a + u)
+            ps = bank(2 * a + u)
             for t in range(4):
                 nc.tensor.transpose(ps[:, P * t : P * (t + 1)], words[:, t, :, u], ident[:])
             nc.scalar.copy(
@@ -168,7 +166,7 @@ def tile_list_spice_substitution_kernel(
         def first_pass(k, half, a):
             b, t = divmod(k, 4)
             if a == 0:
-                h_banks[k, half] = bank(2 * (k if k < 4 else k % 2) + half)
+                h_banks[k, half] = bank(2 * (k % 4) + half)
             cols = slice(P * t, P * (t + 1))
             nc.tensor.matmul_mx(
                 out=h_banks[k, half][:],
@@ -180,11 +178,15 @@ def tile_list_spice_substitution_kernel(
                 stop=(a == 1),
             )
 
-        def finish_h(k, half):
+        def copy_h(k, half, first, count):
+            at = BANK * half + first
+            nc.scalar.copy(out=h[k][:, at : at + count], in_=h_banks[k, half][:, first : first + count])
+
+        def finish_h(k, half, count=BANK):
             first_pass(k, half, 1)
             if half == 0:
                 h[k] = kept([P, S], F32, "h%d" % k)
-            nc.scalar.copy(out=h[k][:, BANK * half : BANK * (half + 1)], in_=h_banks[k, half][:])
+            copy_h(k, half, 0, count)
 
         def make_h(k):
             for half in range(2):
@@ -192,121 +194,102 @@ def tile_list_spice_substitution_kernel(
                     first_pass(k, half, 0)
                 finish_h(k, half)
 
-        after_late = LATE + 4 * T + 64
-        first_want = placed([P, M], F32, "first_want", after_late)
-        slots = [placed([P, M], F32, "slot%d" % i, after_late + 4 * M * (i + 1)) for i in range(3)]
+        WIDE = 3 * P
+        diffs0 = kept([P, 4, M], F32, "diffs0")
+        diffs1 = kept([P, 4, WIDE], F32, "diffs1")
+        diffs_last = kept([P, 4, P], F32, "diffs_last")
+        fade_flat = fade_sb[:].rearrange("p b t -> p (b t)")
+        nc.scalar.copy(out=diffs0[:, :, 0:1], in_=fade_flat[:, 1:5].unsqueeze(2))
+        fade5 = kept([P, 1], F32, "fade5", "woven0")
+        nc.scalar.copy(out=fade5[:], in_=fade_flat[:, 5:6])
 
-        def want_of(k):
-            return first_want if k == 0 else slots[k % 3]
+        def fade_of(k):
+            if 1 <= k <= 4:
+                return diffs0[:, k - 1, 0:1]
+            if k == 5:
+                return fade5[:]
+            return fade_flat[:, k : k + 1]
 
-        prods = [kept([P, 3 * P], F32, "prods%d" % i) for i in range(3)]
-        damp = {}
+        prods = [placed([P, M], F32, "prods%d" % i, LATE + 4 * T + 64 + 4 * M * i) for i in range(3)]
+        damp, prod = {}, {}
 
         def picked(k, which, first, width):
             return h[k][:].indirect(lists[which][:, first // 16 : (first + width) // 16])
 
-        def pick_want(k):
-            nc.vector.tensor_copy(out=want_of(k)[:], in_=picked(k, 0, 0, M))
+        def make_damp(k, first=0, width=M):
+            if first == 0:
+                damp[k] = kept([P, M], F32, "damp%d" % k)
+            nc.scalar.activation(
+                out=damp[k][:, first : first + width], in_=picked(k, 0, first, width), func=ACT.Exp, scale=fade_of(k)
+            )
 
-        def make_damp(k):
-            b, t = divmod(k, 4)
-            damp[k] = kept([P, M], F32, "damp%d" % k)
-            nc.scalar.activation(out=damp[k][:], in_=want_of(k)[:], func=ACT.Exp, scale=fade_sb[:, b, t : t + 1])
+        def pick_repl(k, first, width, into):
+            prod[k, first] = into
+            nc.vector.tensor_tensor(into, picked(k, 1, first, width), damp[k][:, first : first + width], ALU.mult)
 
-        left0, left1, end1 = PARTS[0], PARTS[1], PARTS[-1]
-        stage = {part: kept([P, 4, 2 * P], F32, "stage%d_%d" % part[::2]) for part in PARTS[:-1]}
-        diffs = {part: kept([P, 4, part[1]], F32, "diffs%d_%d" % part[::2]) for part in PARTS[2:]}
+        def diff_of(k, first, width):
+            if k < 4:
+                return diffs0[:, k, first : first + width]
+            if first < WIDE:
+                return diffs1[:, k - 4, first : first + width]
+            return diffs_last[:, k - 4, first - WIDE : first - WIDE + width]
 
-        def planes(part):
-            halves = stage[part][:].rearrange("p t c -> p (t c)").bitcast(BF16).rearrange("p (t c) -> p t c", t=4)
-            return halves[:, :, 2 * P - part[1] // 2 : 2 * P + part[1] // 2]
+        def pick_carr(k, first, width, src=None):
+            src = prod[k, first] if src is None else src
+            nc.vector.tensor_tensor(diff_of(k, first, width), picked(k, 2, first, width), src, ALU.subtract)
 
+        woven = [kept([P, 4 * M], BF16, "woven%d" % b) for b in range(2)]
+        z_codes = [kept([P, M], U32, "z_codes%d" % b) for b in range(2)]
+        z_sc = [kept([P, M], U8, "z_sc%d" % b) for b in range(2)]
 
-        def prod_of(part, t):
-            if part[0] == 0:
-                return prods[(4 * part[2] + t) % 3][:, 0 : part[1]]
-            back_by = 1 if (part, t) == (end1, 3) else 2
-            return stage[PARTS[PARTS.index(part) - back_by]][:, t, P:]
+        def woven_view(b, first, count):
+            return woven[b][:, 4 * first : 4 * (first + count)].rearrange("p (c i t) -> p c t i", i=4, t=4)
 
-        def diff_of(part, t):
-            if part[0] == 0:
-                return slots[(4 * part[2] + t + 1) % 3][:, 0 : part[1]]
-            return diffs[part][:, t, :]
+        def weave(b, first, count):
+            tile, at = (diffs0, first) if b == 0 else (diffs1, first) if first < WIDE else (diffs_last, first - WIDE)
+            src = tile[:, :, at : at + count].rearrange("p t (c i) -> p c t i", i=4)
+            factor = neg_lift[:, 4 * b : 4 * b + 4].unsqueeze(1).unsqueeze(3).to_broadcast([P, count // 4, 4, 4])
+            nc.vector.tensor_tensor(woven_view(b, first, count), src, factor, ALU.mult)
 
-        def pick_repl(part, t):
-            first, width, b = part
-            k = 4 * b + t
-            nc.vector.tensor_tensor(prod_of(part, t), picked(k, 1, first, width), damp[k][:, first : first + width], ALU.mult)
+        def fetch_carr(k, first, width, into):
+            nc.scalar.activation(out=into, in_=picked(k, 2, first, width), func=ACT.Copy)
 
-        def pick_carr(part, t, at=0, count=None):
-            first, width, b = part
-            cols = slice(at, at + (count or width))
-            carr = picked(4 * b + t, 2, first + at, count or width)
-            nc.vector.tensor_tensor(diff_of(part, t)[:, cols], carr, prod_of(part, t)[:, cols], ALU.subtract)
-
-        def make_plane(part, t):
-            k = 4 * part[2] + t
-            nc.scalar.activation(out=planes(part)[:, t, :], in_=diff_of(part, t), func=ACT.Copy, scale=neg_lift[:, k : k + 1])
-
-        woven = {part: kept([P, 4 * part[1]], BF16, "woven%d_%d" % part[::2])[:] for part in PARTS[:-1]}
-        woven[end1] = stage[PARTS[-2]][:, 0, :].bitcast(BF16)
-        z_codes = {part: kept([P, part[1]], U32, "z_codes%d_%d" % part[::2]) for part in PARTS}
-        z_sc = {part: kept([P, part[1]], U8, "z_sc%d_%d" % part[::2]) for part in PARTS}
-
-        def woven_view(part, at, count):
-            return woven[part][:, 4 * at : 4 * (at + count)].rearrange("p (c i t) -> p c t i", i=4, t=4)
-
-        def weave(part, at, count, copy=nc.scalar.copy):
-            src = planes(part)[:, :, at : at + count].rearrange("p t (c i) -> p c t i", i=4)
-            copy(out=woven_view(part, at, count), in_=src)
-
-        def weave_last(at, count):
-            src = diffs[end1][:, :, at : at + count].rearrange("p t (c i) -> p c t i", i=4)
-            factor = neg_lift[:, 4:8].unsqueeze(1).unsqueeze(3).to_broadcast([P, count // 4, 4, 4])
-            nc.vector.tensor_tensor(woven_view(end1, at, count), src, factor, ALU.mult)
-
-        def quantise_z(part, at, count):
-            cols = slice(at, at + count)
+        def quantise_z(b, first, count):
+            cols = slice(first, first + count)
             nc.vector.quantize_mx(
-                out=z_codes[part][:, cols].bitcast(FP8X4), scales=z_sc[part][:, cols], in_=woven[part][:, 4 * at : 4 * (at + count)]
+                out=z_codes[b][:, cols].bitcast(FP8X4), scales=z_sc[b][:, cols], in_=woven[b][:, 4 * first : 4 * (first + count)]
             )
 
         sums = {}
 
         def second_passes(s, i, b):
             first, width = SPANS[s]
-            per_bank = 8 // len(SPAN_BANKS[s])
+            which, j0, per_bank = SPAN_BANKS[s][i]
             if b == 0:
-                sums[s, i] = bank(SPAN_BANKS[s][i])
-            part = PARTS[((0, 0, 3), (1, 2, 4))[b][s]]
-            at = first - part[0]
+                sums[s, i] = bank(which)
             passes = []
             for e in range(per_bank):
-                j = per_bank * i + e
+                j = j0 + e
                 a, jj = divmod(j, 4)
                 n_cols = slice(P * jj, P * (jj + 1))
-                passes.append((wr_codes[a, b][:, n_cols].bitcast(FP8X4), wr_sc[a, b][:, n_cols], e, 0, width))
-                for c in range(0, width, P):
-                    passes.append(
-                        (c4[:, b, 2 * P * j : 2 * P * (j + 1)].bitcast(FP4X4), c4_sc[:, b, P * j : P * (j + 1)], e, c, P)
-                    )
-            for n, (codes, scales, e, c, count) in enumerate(passes):
+                passes.append((c4[:, b, 2 * P * j : 2 * P * (j + 1)].bitcast(FP4X4), c4_sc[:, b, P * j : P * (j + 1)], e))
+                passes.append((wr_codes[a, b][:, n_cols].bitcast(FP8X4), wr_sc[a, b][:, n_cols], e))
+            for n, (codes, scales, e) in enumerate(passes):
                 nc.tensor.matmul_mx(
-                    out=sums[s, i][:, width * e + c : width * e + c + count],
+                    out=sums[s, i][:, width * e : width * (e + 1)],
                     lhsT=codes,
                     lhsT_scale=scales,
-                    rhs=z_codes[part][:, at + c : at + c + count].bitcast(FP8X4),
-                    rhs_scale=z_sc[part][:, at + c : at + c + count],
+                    rhs=z_codes[b][:, first : first + width].bitcast(FP8X4),
+                    rhs_scale=z_sc[b][:, first : first + width],
                     start=(b == 0 and n == 0),
                     stop=(b == 1 and n == len(passes) - 1),
                 )
 
         def finish(s, i):
             first, width = SPANS[s]
-            per_bank = 8 // len(SPAN_BANKS[s])
+            j0, per_bank = SPAN_BANKS[s][i][1:]
             res = kept([P, per_bank, width], F32, "res%d_%d" % (s, i))
-            j0 = per_bank * i
-            if s == 2:
+            if s == 2 and i % 2 == 0:
                 factor = back_sb[:, j0 : j0 + per_bank].unsqueeze(2).to_broadcast([P, per_bank, width])
                 src = sums[s, i][:, 0 : per_bank * width].rearrange("p (e m) -> p e m", e=per_bank)
                 nc.vector.tensor_tensor(res[:], src, factor, ALU.mult)
@@ -325,20 +308,25 @@ def tile_list_spice_substitution_kernel(
             for i in range(len(SPAN_BANKS[s])):
                 second_passes(s, i, b)
 
+        def turn_late(n):
+            a, u = divmod(n, 2)
+            turn_w(a, 1, u)
 
-        def left(k):
-            return PARTS[k // 4], k % 4
+        def width_of(k):
+            return M if k < 4 else WIDE
+
+        def step(k):
+            make_damp(k)
+            pick_repl(k, 0, width_of(k), prods[k % 3][:, 0 : width_of(k)])
+            pick_carr(k - 1, 0, width_of(k - 1))
 
         for k in range(4):
             for half in range(2):
                 first_pass(k, half, 0)
-        for half in range(2):
-            for k in range(2):
-                finish_h(k, half)
-        make_h(2)
-        make_h(3)
+        finish_h(0, 0)
+        finish_h(1, 0)
+        finish_h(0, 1)
         group_w(0, 1, nc.vector.tensor_copy, 0, P)
-        pick_want(0)
         c4_sc = placed([P, 2, K], U8, "c4_sc", 5 * T)
         nc.vector.memset(c4_sc[:].rearrange("p b n -> p (b n)").bitcast(I32), 0)
         for q in range(4):
@@ -346,93 +334,86 @@ def tile_list_spice_substitution_kernel(
                 out=c4_sc[32 * q : 32 * q + 4, :, :].bitcast(I32),
                 in_=c4_scales[:, 4 * q : 4 * q + 4, :].rearrange("b r n -> r b n").bitcast(I32),
             )
-        pick_want(1)
-
-        def turn_late(n):
-            a, u = divmod(n, 2)
-            turn_w(a, 1, u)
-            if u == 1:
-                quantise_wr(a, 1)
-
-        def step(k):
-            make_damp(k)
-            pick_repl(*left(k))
-            pick_carr(*left(k - 1))
-
-        def ahead(k):
-            make_plane(*left(k - 4))
-            pick_want(k)
-
-        make_damp(0)
+        finish_h(1, 1, 2 * P)
+        quantise_wk(0, 1)
+        for first in (0, 2 * P):
+            make_damp(0, first, 2 * P)
+            pick_repl(0, first, 2 * P, prods[0][:, first : first + 2 * P])
+        group_w(1, 1, nc.vector.tensor_copy, 0, P)
+        copy_h(1, 1, 2 * P, 2 * P)
+        make_damp(1)
+        pick_repl(1, 0, M, prods[1][:])
+        quantise_wk(1, 1)
+        pick_carr(0, 0, M, prods[0][:])
         neg_lift = kept([P, 8], F32, "neg_lift")
         nc.scalar.activation(out=neg_lift[:], in_=lift_sb[:].rearrange("p b t -> p (b t)"), func=ACT.Copy, scale=-1.0)
-        quantise_wk(0, 1)
-        pick_repl(*left(0))
-        pick_want(2)
-        step(1)
-        group_w(1, 1, cast_on_scalar, 0, P)
-        quantise_wk(1, 1)
-        pick_want(3)
-        step(2)
+        for k in range(2, 5):
+            make_h(k)
+            step(k)
+        pick_carr(4, 0, WIDE)
+        make_h(5)
+        make_damp(5)
+        pick_repl(5, 0, WIDE, prods[2][:, 0:WIDE])
+        weave(0, 0, 2 * P)
+        pick_carr(5, 0, WIDE)
+        weave(0, 2 * P, 2 * P)
+        for first in (0, 2 * P):
+            quantise_z(0, first, 2 * P)
+        prod67 = kept([P, 2, WIDE], F32, "prod67")
+        carr67 = kept([P, 2, WIDE], F32, "carr67")
+        make_h(6)
+        make_damp(6)
+        pick_repl(6, 0, WIDE, prod67[:, 0, :])
+        make_h(7)
         turn_late(0)
-        step(3)
+        make_damp(7)
         turn_late(1)
+        for k in (6, 7):
+            fetch_carr(k, 0, WIDE, carr67[:, k - 6, :])
         back_sb = kept([P, 8], F32, "back_sb", "grouped01")
         with nc.allow_non_contiguous_dma(reason="one factor for each output row"):
             nc.sync.dma_start(out=back_sb[:], in_=back.rearrange("(j p) -> p j", p=P))
-        make_h(4)
-        ahead(4)
-        make_h(5)
-        ahead(5)
         turn_late(2)
-        step(4)
-        make_h(6)
-        ahead(6)
-        step(5)
         turn_late(3)
-        make_h(7)
-        ahead(7)
-        weave(left0, 0, P)
-        step(6)
-        make_plane(left1, 0)
-        weave(left0, P, P)
-        quantise_z(left0, 0, 2 * P)
+        carr_last = kept([P, 4, P], F32, "carr_last")
+        for k in range(4, 8):
+            fetch_carr(k, WIDE, P, carr_last[:, k - 4, :])
         all_banks(0, 0)
-        step(7)
-        make_plane(left1, 1)
-        weave(left0, 2 * P, P)
-        quantise_z(left0, 2 * P, P)
-        all_banks(1, 0)
-        pick_carr(left1, 3)
-        make_plane(left1, 2)
-        make_plane(left1, 3)
-        for n in range(2, len(PARTS)):
-            part, before = PARTS[n], PARTS[n - 1]
-            held = 1 if part == end1 else 0
-            pick_repl(part, 0)
-            for t in range(1, 4):
-                if t < 4 - held:
-                    pick_repl(part, t)
-                pick_carr(part, t - 1)
-            if not held:
-                pick_carr(part, 3)
-            weave(before, 0, before[1])
-            if held:
-                pick_repl(part, 3)
-            quantise_z(before, 0, before[1])
-            all_banks(n - 2, before[2])
-            if held:
-                for at in (0, P // 2):
-                    pick_carr(part, 3, at, P // 2)
-            for s, i in STORES.get(n, ()):
-                finish(s, i)
-            if part != end1:
-                for t in range(4):
-                    make_plane(part, t)
-        for at in (0, P // 2):
-            weave_last(at, P // 2)
-        for at in (0, P // 2):
-            quantise_z(end1, at, P // 2)
+        def subtract67(first, width):
+            cols = slice(first, first + width)
+            nc.vector.tensor_tensor(diffs1[:, 2:4, cols], carr67[:, :, cols], prod67[:, :, cols], ALU.subtract)
+
+        pick_repl(7, 0, 2 * P, prod67[:, 1, 0 : 2 * P])
+        quantise_wr(0, 1)
+        subtract67(0, 2 * P)
+        pick_repl(7, 2 * P, P, prod67[:, 1, 2 * P : WIDE])
+        weave(1, 0, 2 * P)
+        subtract67(2 * P, P)
+        quantise_z(1, 0, 2 * P)
+        prod_last = kept([P, 4, P], F32, "prod_last", "prod67")
+        pick_repl(4, WIDE, P, prod_last[:, 0, :])
+        quantise_wr(1, 1)
         for i in range(4):
+            second_passes(0, i, 1)
+            finish(0, i)
+        all_banks(1, 0)
+        weave(1, 2 * P, P)
+        pick_repl(5, WIDE, P, prod_last[:, 1, :])
+        quantise_z(1, 2 * P, P)
+        for i in range(2):
+            second_passes(1, i, 1)
+            finish(1, i)
+        all_banks(2, 0)
+        for k in (6, 7):
+            pick_repl(k, WIDE, P, prod_last[:, k - 4, :])
+        nc.vector.tensor_tensor(diffs_last[:, 0:3, :], carr_last[:, 0:3, :], prod_last[:, 0:3, :], ALU.subtract)
+        for at in (0, P // 2):
+            cols = slice(at, at + P // 2)
+            nc.vector.tensor_tensor(diffs_last[:, 3, cols], carr_last[:, 3, cols], prod_last[:, 3, cols], ALU.subtract)
+        for at in (0, P // 2):
+            weave(1, WIDE + at, P // 2)
+        for at in (0, P // 2):
+            quantise_z(1, WIDE + at, P // 2)
+        for i in range(3):
             second_passes(2, i, 1)
             finish(2, i)

@@ -59,6 +59,10 @@ def tile_list_spice_substitution_kernel(
             tab[a] = tile
             nc.sync.dma_start(out=tab[a][:], in_=tab_words[a].rearrange("p t i -> p (t i)").bitcast(I32))
 
+        fade_sb = shared.tile([P, 2, 8], F32, name="fade_sb", offset=2 * T - 32)
+        nc.sync.dma_start(out=fade_sb[:, :, 0:4], in_=fade.rearrange("(b p t) -> p b t", b=2, t=4))
+        fade_kept = kept([P, 2, 4], F32, "fade_kept")
+        nc.scalar.copy(out=fade_kept[:], in_=fade_sb[:, :, 0:4])
         load_w(0, 0, 1, kept([P, 4, PASS], F32, "w_raw00"))
         offs_sb = keep.tile([P, S // 16], U16, name="offs_sb")
         nc.sync.dma_start(offs_sb[:], offs)
@@ -67,7 +71,7 @@ def tile_list_spice_substitution_kernel(
             pos_sb = keep.tile([P, M // 16], U16, name="pos_sb%d" % i)
             nc.sync.dma_start(pos_sb[:], pos)
             lists.append(pos_sb)
-        zeros = placed([P, P], F32, "zeros", 2 * T - 2 * P)
+        zeros = kept([P, P], F32, "zeros")
         nc.gpsimd.memset(zeros[:], 0.0)
         ident = kept([P, P], F32, "ident")
         nc.gpsimd.affine_select(
@@ -134,7 +138,7 @@ def tile_list_spice_substitution_kernel(
         for a, b in chunks:
             group_w(a, b, cast_on_scalar if (a, b) in GROUP_S else nc.vector.tensor_copy, 0, P)
             if (a, b) == (0, 0):
-                picked_sc = kept([P, S], U8, "picked_sc", "w_raw00")
+                picked_sc = kept([P, S], U8, "picked_sc", "w_raw11")
                 nc.vector.tensor_copy(out=picked_sc[:], in_=tab_sc[:].indirect(offs_sb[:]))
         for a, b in chunks:
             quantise_wk(a, b)
@@ -144,17 +148,15 @@ def tile_list_spice_substitution_kernel(
         place_scales(0)
         load_tab(1, placed([P, T], I32, "tab1", LATE))
         place_scales(1)
-        fade_sb = placed([P, 2, 4], F32, "fade_sb", LATE + 4 * T)
-        nc.sync.dma_start(out=fade_sb[:], in_=fade.rearrange("(b p t) -> p b t", b=2, t=4))
         load_w(0, 1, 1, placed([P, 4, PASS], F32, "w_raw01", LATE + 4 * T + 64))
-        load_w(1, 1, 1, kept([P, 4, PASS], F32, "w_raw11", "w_raw00"))
+        load_w(1, 1, 1, kept([P, 4, PASS], F32, "w_raw11"))
         for a in range(2):
             for half in range(2):
                 gather_words(a, half)
         for a, b in chunks:
             quantise_wr(a, b)
 
-        lift_sb = placed([P, 2, 4], F32, "lift_sb", 5 * T + 2 * K)
+        lift_sb = placed([P, 2, 4], F32, "lift_sb", LATE + 2 * T + 2 * K)
         nc.sync.dma_start(out=lift_sb[:], in_=lift.rearrange("(b p t) -> p b t", b=2, t=4))
         c4 = placed([P, 2, 2 * K], U8, "c4", LATE + T)
         nc.sync.dma_start(out=c4[:].bitcast(I32), in_=c4_words.rearrange("b p c -> p b c").bitcast(I32))
@@ -198,7 +200,7 @@ def tile_list_spice_substitution_kernel(
         diffs0 = kept([P, 4, M], F32, "diffs0")
         diffs1 = kept([P, 4, WIDE], F32, "diffs1")
         diffs_last = kept([P, 4, P], F32, "diffs_last")
-        fade_flat = fade_sb[:].rearrange("p b t -> p (b t)")
+        fade_flat = fade_kept[:].rearrange("p b t -> p (b t)")
         nc.scalar.copy(out=diffs0[:, :, 0:1], in_=fade_flat[:, 1:5].unsqueeze(2))
         fade5 = kept([P, 1], F32, "fade5", "woven0")
         nc.scalar.copy(out=fade5[:], in_=fade_flat[:, 5:6])
@@ -242,13 +244,16 @@ def tile_list_spice_substitution_kernel(
         z_codes = [kept([P, M], U32, "z_codes%d" % b) for b in range(2)]
         z_sc = [kept([P, M], U8, "z_sc%d" % b) for b in range(2)]
 
+        def woven_of(b, first, count):
+            return woven[b][:, 4 * first : 4 * (first + count)]
+
         def woven_view(b, first, count):
-            return woven[b][:, 4 * first : 4 * (first + count)].rearrange("p (c i t) -> p c t i", i=4, t=4)
+            return woven_of(b, first, count).rearrange("p (c i t) -> p c t i", i=2, t=4)
 
         def weave(b, first, count):
             tile, at = (diffs0, first) if b == 0 else (diffs1, first) if first < WIDE else (diffs_last, first - WIDE)
-            src = tile[:, :, at : at + count].rearrange("p t (c i) -> p c t i", i=4)
-            factor = neg_lift[:, 4 * b : 4 * b + 4].unsqueeze(1).unsqueeze(3).to_broadcast([P, count // 4, 4, 4])
+            src = tile[:, :, at : at + count].rearrange("p t (c i) -> p c t i", i=2)
+            factor = neg_lift[:, 4 * b : 4 * b + 4].unsqueeze(1).unsqueeze(3).to_broadcast([P, count // 2, 4, 2])
             nc.vector.tensor_tensor(woven_view(b, first, count), src, factor, ALU.mult)
 
         def fetch_carr(k, first, width, into):
@@ -257,7 +262,7 @@ def tile_list_spice_substitution_kernel(
         def quantise_z(b, first, count):
             cols = slice(first, first + count)
             nc.vector.quantize_mx(
-                out=z_codes[b][:, cols].bitcast(FP8X4), scales=z_sc[b][:, cols], in_=woven[b][:, 4 * first : 4 * (first + count)]
+                out=z_codes[b][:, cols].bitcast(FP8X4), scales=z_sc[b][:, cols], in_=woven_of(b, first, count)
             )
 
         sums = {}
@@ -327,8 +332,7 @@ def tile_list_spice_substitution_kernel(
         finish_h(1, 0)
         finish_h(0, 1)
         group_w(0, 1, nc.vector.tensor_copy, 0, P)
-        c4_sc = placed([P, 2, K], U8, "c4_sc", 5 * T)
-        nc.vector.memset(c4_sc[:].rearrange("p b n -> p (b n)").bitcast(I32), 0)
+        c4_sc = placed([P, 2, K], U8, "c4_sc", LATE + 2 * T)
         for q in range(4):
             nc.sync.dma_start(
                 out=c4_sc[32 * q : 32 * q + 4, :, :].bitcast(I32),
@@ -354,16 +358,15 @@ def tile_list_spice_substitution_kernel(
         make_h(5)
         make_damp(5)
         pick_repl(5, 0, WIDE, prods[2][:, 0:WIDE])
-        weave(0, 0, 2 * P)
+        weave(0, 0, M)
         pick_carr(5, 0, WIDE)
-        weave(0, 2 * P, 2 * P)
-        for first in (0, 2 * P):
-            quantise_z(0, first, 2 * P)
-        prod67 = kept([P, 2, WIDE], F32, "prod67")
+        quantise_z(0, 0, M)
+        prod6 = kept([P, WIDE], F32, "prod6")
+        prod7 = kept([P, 2 * P], F32, "prod7")
         carr67 = kept([P, 2, WIDE], F32, "carr67")
         make_h(6)
         make_damp(6)
-        pick_repl(6, 0, WIDE, prod67[:, 0, :])
+        pick_repl(6, 0, WIDE, prod6[:])
         make_h(7)
         turn_late(0)
         make_damp(7)
@@ -379,19 +382,20 @@ def tile_list_spice_substitution_kernel(
         for k in range(4, 8):
             fetch_carr(k, WIDE, P, carr_last[:, k - 4, :])
         all_banks(0, 0)
-        def subtract67(first, width):
+        def subtract(k, first, width, src):
             cols = slice(first, first + width)
-            nc.vector.tensor_tensor(diffs1[:, 2:4, cols], carr67[:, :, cols], prod67[:, :, cols], ALU.subtract)
+            nc.vector.tensor_tensor(diffs1[:, k - 4, cols], carr67[:, k - 6, cols], src, ALU.subtract)
 
-        pick_repl(7, 0, 2 * P, prod67[:, 1, 0 : 2 * P])
+        pick_repl(7, 0, 2 * P, prod7[:])
         quantise_wr(0, 1)
-        subtract67(0, 2 * P)
-        pick_repl(7, 2 * P, P, prod67[:, 1, 2 * P : WIDE])
+        subtract(6, 0, WIDE, prod6[:])
+        subtract(7, 0, 2 * P, prod7[:])
+        pick_repl(7, 2 * P, P, prod6[:, 0:P])
         weave(1, 0, 2 * P)
-        subtract67(2 * P, P)
-        quantise_z(1, 0, 2 * P)
-        prod_last = kept([P, 4, P], F32, "prod_last", "prod67")
+        subtract(7, 2 * P, P, prod6[:, 0:P])
+        prod_last = kept([P, 4, P], F32, "prod_last", "prod7")
         pick_repl(4, WIDE, P, prod_last[:, 0, :])
+        quantise_z(1, 0, 2 * P)
         quantise_wr(1, 1)
         for i in range(4):
             second_passes(0, i, 1)
@@ -404,8 +408,8 @@ def tile_list_spice_substitution_kernel(
             second_passes(1, i, 1)
             finish(1, i)
         all_banks(2, 0)
-        for k in (6, 7):
-            pick_repl(k, WIDE, P, prod_last[:, k - 4, :])
+        pick_repl(6, WIDE, P, prod_last[:, 2, :])
+        pick_repl(7, WIDE, P, prod_last[:, 3, :])
         nc.vector.tensor_tensor(diffs_last[:, 0:3, :], carr_last[:, 0:3, :], prod_last[:, 0:3, :], ALU.subtract)
         for at in (0, P // 2):
             cols = slice(at, at + P // 2)

@@ -244,7 +244,11 @@ def tile_list_spice_substitution_kernel(
         z_codes = [kept([P, M], U32, "z_codes%d" % b) for b in range(2)]
         z_sc = [kept([P, M], U8, "z_sc%d" % b) for b in range(2)]
 
+        late_woven = {}
+
         def woven_of(b, first, count):
+            if b == 0 and first >= WIDE:
+                return late_woven[0][:]
             return woven[b][:, 4 * first : 4 * (first + count)]
 
         def woven_view(b, first, count):
@@ -358,9 +362,9 @@ def tile_list_spice_substitution_kernel(
         make_h(5)
         make_damp(5)
         pick_repl(5, 0, WIDE, prods[2][:, 0:WIDE])
-        weave(0, 0, M)
+        weave(0, 0, WIDE)
         pick_carr(5, 0, WIDE)
-        quantise_z(0, 0, M)
+        quantise_z(0, 0, WIDE)
         prod6 = kept([P, WIDE], F32, "prod6")
         prod7 = kept([P, 2 * P], F32, "prod7")
         carr67 = kept([P, 2, WIDE], F32, "carr67")
@@ -370,40 +374,44 @@ def tile_list_spice_substitution_kernel(
         make_h(7)
         turn_late(0)
         make_damp(7)
-        turn_late(1)
         for k in (6, 7):
             fetch_carr(k, 0, WIDE, carr67[:, k - 6, :])
+        turn_late(1)
         back_sb = kept([P, 8], F32, "back_sb", "grouped01")
         with nc.allow_non_contiguous_dma(reason="one factor for each output row"):
             nc.sync.dma_start(out=back_sb[:], in_=back.rearrange("(j p) -> p j", p=P))
         turn_late(2)
         turn_late(3)
-        carr_last = kept([P, 4, P], F32, "carr_last")
-        for k in range(4, 8):
-            fetch_carr(k, WIDE, P, carr_last[:, k - 4, :])
         all_banks(0, 0)
         def subtract(k, first, width, src):
             cols = slice(first, first + width)
             nc.vector.tensor_tensor(diffs1[:, k - 4, cols], carr67[:, k - 6, cols], src, ALU.subtract)
 
         pick_repl(7, 0, 2 * P, prod7[:])
-        quantise_wr(0, 1)
         subtract(6, 0, WIDE, prod6[:])
         subtract(7, 0, 2 * P, prod7[:])
         pick_repl(7, 2 * P, P, prod6[:, 0:P])
         weave(1, 0, 2 * P)
+        quantise_wr(0, 1)
+        quantise_z(1, 0, 2 * P)
         subtract(7, 2 * P, P, prod6[:, 0:P])
         prod_last = kept([P, 4, P], F32, "prod_last", "prod7")
         pick_repl(4, WIDE, P, prod_last[:, 0, :])
-        quantise_z(1, 0, 2 * P)
+        weave(1, 2 * P, P)
         quantise_wr(1, 1)
+        quantise_z(1, 2 * P, P)
+        carr_last = kept([P, 4, P], F32, "carr_last")
         for i in range(4):
             second_passes(0, i, 1)
             finish(0, i)
+            if i == 1:
+                for k in range(4, 8):
+                    fetch_carr(k, WIDE, P, carr_last[:, k - 4, :])
         all_banks(1, 0)
-        weave(1, 2 * P, P)
+        late_woven[0] = kept([P, 4 * P], BF16, "late_woven", "prod6")
+        weave(0, WIDE, P)
         pick_repl(5, WIDE, P, prod_last[:, 1, :])
-        quantise_z(1, 2 * P, P)
+        quantise_z(0, WIDE, P)
         for i in range(2):
             second_passes(1, i, 1)
             finish(1, i)

@@ -19,10 +19,13 @@ ACT = mybir.ActivationFunctionType
 P = 128
 PASS = 512
 BANK = 512
-GROUP_S = ((0, 0),)
-LATE = 6 * T
 SPANS = ((0, 256), (256, 128), (384, 128))
-SPAN_BANKS = (((4, 0, 2), (5, 2, 2), (6, 4, 2), (7, 6, 2)), ((0, 0, 4), (1, 4, 4)), ((2, 0, 3), (3, 3, 3), (4, 6, 2)))
+SPAN_BANKS = (
+    ((4, 0, 2), (5, 2, 2), (6, 4, 2), (7, 6, 2)),
+    ((2, 0, 4), (3, 4, 4)),
+    ((0, 0, 2), (1, 2, 2), (4, 4, 2), (5, 6, 2)),
+)
+TAB0, TAB1, AFTER = 2 * T, 6 * T, 10 * T + 64
 
 
 def tile_list_spice_substitution_kernel(
@@ -43,9 +46,13 @@ def tile_list_spice_substitution_kernel(
         def placed(shape, dtype, name, offset):
             return shared.tile(shape, dtype, name=name, align_bytes=64, offset=offset)
 
-        tab_sc = placed([P, T], U8, "tab_sc", LATE + 4 * T - T // 2)
+        tab_sc = placed([P, T], U8, "tab_sc", TAB1 + 4 * T - T // 2)
         nc.vector.memset(tab_sc[:].bitcast(I32), 0)
         nc.sync.dma_start(out=tab_sc[0:P:4, :].bitcast(I32), in_=tab_scales.rearrange("a q t -> (a q) t").bitcast(I32))
+        fade_in = shared.tile([P, 2, 8], F32, name="fade_in", offset=TAB0 - 32)
+        nc.sync.dma_start(out=fade_in[:, :, 0:4], in_=fade.rearrange("(b p t) -> p b t", b=2, t=4))
+        fade_sb = kept([P, 8], F32, "fade_sb")
+        nc.scalar.copy(out=fade_sb[:].rearrange("p (b t) -> p b t", b=2), in_=fade_in[:, :, 0:4])
 
         w_raw, tab = {}, {}
 
@@ -55,15 +62,11 @@ def tile_list_spice_substitution_kernel(
             for b in range(count):
                 w_raw[a, first + b] = tile[:, :, PASS * b : PASS * (b + 1)]
 
-        def load_tab(a, tile):
-            tab[a] = tile
+        def load_tab(a, offset):
+            tab[a] = placed([P, T], I32, "tab%d" % a, offset)
             nc.sync.dma_start(out=tab[a][:], in_=tab_words[a].rearrange("p t i -> p (t i)").bitcast(I32))
 
-        fade_sb = shared.tile([P, 2, 8], F32, name="fade_sb", offset=2 * T - 32)
-        nc.sync.dma_start(out=fade_sb[:, :, 0:4], in_=fade.rearrange("(b p t) -> p b t", b=2, t=4))
-        fade_kept = kept([P, 2, 4], F32, "fade_kept")
-        nc.scalar.copy(out=fade_kept[:], in_=fade_sb[:, :, 0:4])
-        load_w(0, 0, 1, kept([P, 4, PASS], F32, "w_raw00"))
+        load_w(0, 0, 2, kept([P, 4, 2 * PASS], F32, "w_upper"))
         offs_sb = keep.tile([P, S // 16], U16, name="offs_sb")
         nc.sync.dma_start(offs_sb[:], offs)
         lists = []
@@ -78,53 +81,50 @@ def tile_list_spice_substitution_kernel(
             out=ident[:], in_=zeros[:], compare_op=ALU.not_equal, fill=1.0, base=0, pattern=[[-1, P]], channel_multiplier=1
         )
         load_w(1, 0, 1, placed([P, 4, PASS], F32, "w_raw10", 0))
-        load_tab(0, placed([P, T], I32, "tab0", 2 * T))
+        load_tab(0, TAB0)
 
+        wk_codes, wk_sc, wr_codes, wr_sc, grouped, turned = {}, {}, {}, {}, {}, {}
 
-        wk_codes, wk_sc, wr_codes, wr_sc, grouped, turned, turn_banks = {}, {}, {}, {}, {}, {}, {}
-
-        def group_w(a, b, copy, first, count):
-            if first == 0:
-                grouped[a, b] = kept([P, 4 * PASS], BF16, "grouped%d%d" % (a, b))
+        def group_w(a, b, copy):
+            grouped[a, b] = kept([P, 4 * PASS], BF16, "grouped%d%d" % (a, b))
             dst = grouped[a, b][:].rearrange("p (t m i) -> p m i t", t=4, i=4)
-            src = w_raw[a, b].rearrange("p i (m t) -> p m i t", t=4)
-            copy(out=dst[:, first : first + count], in_=src[:, first : first + count])
+            copy(out=dst, in_=w_raw[a, b].rearrange("p i (m t) -> p m i t", t=4))
 
         def cast_on_scalar(out, in_):
             nc.scalar.activation(out=out, in_=in_, func=ACT.Copy)
 
         def quantise_wk(a, b):
-            name = "wk%d%d_codes" % (a, b)
-            wk_codes[a, b] = kept([P, PASS], U32, name)
+            wk_codes[a, b] = kept([P, PASS], U32, "wk%d%d_codes" % (a, b))
             wk_sc[a, b] = kept([P, PASS], U8, "wk%d%d_sc" % (a, b))
             nc.vector.quantize_mx(out=wk_codes[a, b][:].bitcast(FP8X4), scales=wk_sc[a, b][:], in_=grouped[a, b][:])
 
-        def turn_w(a, b, u):
+        def turn_w(a, b, first_bank):
             words = grouped[a, b][:].bitcast(F32).rearrange("p (t m u) -> p t m u", t=4, u=2)
-            if u == 0:
-                turned[a, b] = kept([P, 4 * PASS], BF16, "turned%d%d" % (a, b))
-            ps = bank(2 * a + u)
-            for t in range(4):
-                nc.tensor.transpose(ps[:, P * t : P * (t + 1)], words[:, t, :, u], ident[:])
-            nc.scalar.copy(
-                out=turned[a, b][:].rearrange("m (p u e t) -> m u p e t", u=2, e=2, t=4)[:, u],
-                in_=ps[:].bitcast(BF16).rearrange("m (t p e) -> m p e t", t=4, e=2),
-            )
+            turned[a, b] = kept([P, 4 * PASS], BF16, "turned%d%d" % (a, b))
+            for u in range(2):
+                ps = bank(first_bank + u)
+                for t in range(4):
+                    nc.tensor.transpose(ps[:, P * t : P * (t + 1)], words[:, t, :, u], ident[:])
+                nc.scalar.copy(
+                    out=turned[a, b][:].rearrange("m (p u e t) -> m u p e t", u=2, e=2, t=4)[:, u],
+                    in_=ps[:].bitcast(BF16).rearrange("m (t p e) -> m p e t", t=4, e=2),
+                )
 
-        def quantise_wr(a, b):
-            codes = placed([P, PASS], U32, "wr%d%d_codes" % (a, b), (4 * T, LATE)[b] + 4 * PASS * a)[:]
+        def quantise_wr(a, b, codes):
             wr_codes[a, b] = codes
             wr_sc[a, b] = kept([P, PASS], U8, "wr%d%d_sc" % (a, b))
-            nc.vector.quantize_mx(out=codes.bitcast(FP8X4), scales=wr_sc[a, b][:], in_=turned[a, b][:])
+            nc.vector.quantize_mx(out=codes[:].bitcast(FP8X4), scales=wr_sc[a, b][:], in_=turned[a, b][:])
 
         v_codes = {}
+        v_sc = [kept([P, S], U8, "v_sc%d" % a) for a in range(2)]
 
         def gather_words(a, half):
             v_codes[a, half] = kept([P, BANK], U32, "v%d%d" % (a, half))
-            cols = offs_sb[:, 32 * half : 32 * (half + 1)]
-            nc.vector.tensor_copy(out=v_codes[a, half][:], in_=tab[a][:].bitcast(U32).indirect(cols))
-
-        v_sc = [kept([P, S], U8, "v_sc%d" % a) for a in range(2)]
+            count = BANK // 2 if (a, half) == (1, 0) else BANK
+            for first in range(0, BANK, count):
+                at = (BANK * half + first) // 16
+                cols = offs_sb[:, at : at + count // 16]
+                nc.vector.tensor_copy(out=v_codes[a, half][:, first : first + count], in_=tab[a][:].bitcast(U32).indirect(cols))
 
         def place_scales(a):
             for q in range(4):
@@ -134,36 +134,43 @@ def tile_list_spice_substitution_kernel(
                     in_=picked_sc[first : first + 16 : 4, :].bitcast(I32),
                 )
 
-        chunks = [(0, 0), (1, 0)]
-        for a, b in chunks:
-            group_w(a, b, cast_on_scalar if (a, b) in GROUP_S else nc.vector.tensor_copy, 0, P)
-            if (a, b) == (0, 0):
-                picked_sc = kept([P, S], U8, "picked_sc", "w_raw11")
-                nc.vector.tensor_copy(out=picked_sc[:], in_=tab_sc[:].indirect(offs_sb[:]))
-        for a, b in chunks:
+        early = ((0, 0), (0, 1), (1, 0))
+        picked_sc = kept([P, S], U8, "picked_sc")
+        nc.vector.tensor_copy(out=picked_sc[:], in_=tab_sc[:].indirect(offs_sb[:]))
+        for n, (a, b) in enumerate(early):
+            group_w(a, b, cast_on_scalar if n == 0 else nc.vector.tensor_copy)
+        for a, b in early:
             quantise_wk(a, b)
-        for a, b in chunks:
-            turn_w(a, b, 0)
-            turn_w(a, b, 1)
+        for n, (a, b) in enumerate(early):
+            turn_w(a, b, 2 * n)
         place_scales(0)
-        load_tab(1, placed([P, T], I32, "tab1", LATE))
+        load_tab(1, TAB1)
         place_scales(1)
-        load_w(0, 1, 1, placed([P, 4, PASS], F32, "w_raw01", LATE + 4 * T + 64))
-        load_w(1, 1, 1, kept([P, 4, PASS], F32, "w_raw11"))
+        late_halves = [placed([P, 4, PASS // 2], F32, "w_late%d" % half, (AFTER, 0)[half]) for half in range(2)]
+        for half in range(2):
+            rows = w[PASS:, PASS + PASS // 2 * half : PASS + PASS // 2 * (half + 1)]
+            nc.sync.dma_start(out=late_halves[half][:], in_=rows.rearrange("(p i) r -> p i r", i=4))
         for a in range(2):
             for half in range(2):
                 gather_words(a, half)
-        for a, b in chunks:
-            quantise_wr(a, b)
+        for n, (a, b) in enumerate(early):
+            quantise_wr(a, b, placed([P, PASS], U32, "wr%d%d_codes" % (a, b), TAB0 + T + 4 * PASS * n))
 
-        lift_sb = placed([P, 2, 4], F32, "lift_sb", LATE + 2 * T + 2 * K)
+        lift_sb = placed([P, 2, 4], F32, "lift_sb", TAB1)
         nc.sync.dma_start(out=lift_sb[:], in_=lift.rearrange("(b p t) -> p b t", b=2, t=4))
-        c4 = placed([P, 2, 2 * K], U8, "c4", LATE + T)
+        c4 = placed([P, 2, 2 * K], U8, "c4", TAB1 + T)
         nc.sync.dma_start(out=c4[:].bitcast(I32), in_=c4_words.rearrange("b p c -> p b c").bitcast(I32))
+        c4_sc = placed([P, 2, K], U8, "c4_sc", TAB1 + 2 * T)
+        for q in range(4):
+            nc.sync.dma_start(
+                out=c4_sc[32 * q : 32 * q + 4, :, :].bitcast(I32),
+                in_=c4_scales[:, 4 * q : 4 * q + 4, :].rearrange("b r n -> r b n").bitcast(I32),
+            )
+        back_sb = placed([P, 8], F32, "back_sb", TAB1 + 3 * T)
+        with nc.allow_non_contiguous_dma(reason="one factor for each output row"):
+            nc.sync.dma_start(out=back_sb[:], in_=back.rearrange("(j p) -> p j", p=P))
 
-        h = {}
-
-        h_banks = {}
+        h, h_banks = {}, {}
 
         def first_pass(k, half, a):
             b, t = divmod(k, 4)
@@ -179,6 +186,28 @@ def tile_list_spice_substitution_kernel(
                 start=(a == 0),
                 stop=(a == 1),
             )
+
+        def quarter_passes(q, a):
+            if a == 0:
+                h_banks["quarter", q] = bank(2 * q)
+            cols = slice(2 * P * q, 2 * P * (q + 1))
+            for k in range(2):
+                nc.tensor.matmul_mx(
+                    out=h_banks["quarter", q][:, 2 * P * k : 2 * P * (k + 1)],
+                    lhsT=wk_codes[a, 0][:, P * k : P * (k + 1)].bitcast(FP8X4),
+                    lhsT_scale=wk_sc[a, 0][:, P * k : P * (k + 1)],
+                    rhs=v_codes[a, 0][:, cols].bitcast(FP8X4),
+                    rhs_scale=v_sc[a][:, cols],
+                    start=(a == 0 and k == 0),
+                    stop=(a == 1 and k == 1),
+                )
+
+        def finish_quarter(q):
+            quarter_passes(q, 1)
+            for k in range(2):
+                if q == 0:
+                    h[k] = kept([P, S], F32, "h%d" % k)
+                nc.scalar.copy(out=h[k][:, 2 * P * q : 2 * P * (q + 1)], in_=h_banks["quarter", q][:, 2 * P * k : 2 * P * (k + 1)])
 
         def copy_h(k, half, first, count):
             at = BANK * half + first
@@ -196,24 +225,24 @@ def tile_list_spice_substitution_kernel(
                     first_pass(k, half, 0)
                 finish_h(k, half)
 
-        WIDE = 3 * P
+        WIDE = SPANS[2][0]
         diffs0 = kept([P, 4, M], F32, "diffs0")
         diffs1 = kept([P, 4, WIDE], F32, "diffs1")
         diffs_last = kept([P, 4, P], F32, "diffs_last")
-        fade_flat = fade_kept[:].rearrange("p b t -> p (b t)")
-        nc.scalar.copy(out=diffs0[:, :, 0:1], in_=fade_flat[:, 1:5].unsqueeze(2))
-        fade5 = kept([P, 1], F32, "fade5", "woven0")
-        nc.scalar.copy(out=fade5[:], in_=fade_flat[:, 5:6])
+        nc.scalar.copy(out=diffs0[:, 1, 0:1], in_=fade_sb[:, 2:3])
+        fade4 = kept([P, 1], F32, "fade4", "woven0")
+        nc.scalar.copy(out=fade4[:], in_=fade_sb[:, 4:5])
+        nc.scalar.copy(out=diffs1[:, 1:3, 0:1], in_=fade_sb[:, 6:8].unsqueeze(2))
 
         def fade_of(k):
-            if 1 <= k <= 4:
-                return diffs0[:, k - 1, 0:1]
-            if k == 5:
-                return fade5[:]
-            return fade_flat[:, k : k + 1]
+            if k == 2:
+                return diffs0[:, 1, 0:1]
+            if k >= 6:
+                return diffs1[:, k - 5, 0:1]
+            return fade4[:] if k == 4 else fade_sb[:, k : k + 1]
 
-        prods = [placed([P, M], F32, "prods%d" % i, LATE + 4 * T + 64 + 4 * M * i) for i in range(3)]
-        damp, prod = {}, {}
+        prods = [placed([P, M], F32, "prods%d" % i, 4 * M * i) for i in range(3)]
+        damp = {}
 
         def picked(k, which, first, width):
             return h[k][:].indirect(lists[which][:, first // 16 : (first + width) // 16])
@@ -226,48 +255,34 @@ def tile_list_spice_substitution_kernel(
             )
 
         def pick_repl(k, first, width, into):
-            prod[k, first] = into
             nc.vector.tensor_tensor(into, picked(k, 1, first, width), damp[k][:, first : first + width], ALU.mult)
 
-        def diff_of(k, first, width):
-            if k < 4:
-                return diffs0[:, k, first : first + width]
-            if first < WIDE:
-                return diffs1[:, k - 4, first : first + width]
-            return diffs_last[:, k - 4, first - WIDE : first - WIDE + width]
-
-        def pick_carr(k, first, width, src=None):
-            src = prod[k, first] if src is None else src
-            nc.vector.tensor_tensor(diff_of(k, first, width), picked(k, 2, first, width), src, ALU.subtract)
-
-        woven = [kept([P, 4 * M], BF16, "woven%d" % b) for b in range(2)]
-        z_codes = [kept([P, M], U32, "z_codes%d" % b) for b in range(2)]
-        z_sc = [kept([P, M], U8, "z_sc%d" % b) for b in range(2)]
-
-        late_woven = {}
-
-        def woven_of(b, first, count):
-            if b == 0 and first >= WIDE:
-                return late_woven[0][:]
-            return woven[b][:, 4 * first : 4 * (first + count)]
-
-        def woven_view(b, first, count):
-            return woven_of(b, first, count).rearrange("p (c i t) -> p c t i", i=2, t=4)
-
-        def weave(b, first, count):
-            tile, at = (diffs0, first) if b == 0 else (diffs1, first) if first < WIDE else (diffs_last, first - WIDE)
-            src = tile[:, :, at : at + count].rearrange("p t (c i) -> p c t i", i=2)
-            factor = neg_lift[:, 4 * b : 4 * b + 4].unsqueeze(1).unsqueeze(3).to_broadcast([P, count // 2, 4, 2])
-            nc.vector.tensor_tensor(woven_view(b, first, count), src, factor, ALU.mult)
+        def pick_carr(k, first, width, prod, into):
+            nc.vector.tensor_tensor(into, picked(k, 2, first, width), prod, ALU.subtract)
 
         def fetch_carr(k, first, width, into):
             nc.scalar.activation(out=into, in_=picked(k, 2, first, width), func=ACT.Copy)
 
-        def quantise_z(b, first, count):
+        def repl(k, first=0, width=None):
+            width = width or (M if k < 4 else WIDE)
+            pick_repl(k, first, width, prods[k % 3][:, first : first + width])
+
+        def carr(k, first=0, width=None):
+            width = width or (M if k < 4 else WIDE)
+            into = diffs0[:, k, first : first + width] if k < 4 else diffs1[:, k - 4, :]
+            pick_carr(k, first, width, prods[k % 3][:, first : first + width], into)
+
+        z_codes = [kept([P, M], U32, "z_codes%d" % b) for b in range(2)]
+        z_sc = [kept([P, M], U8, "z_sc%d" % b) for b in range(2)]
+
+        def weave(b, diffs, into):
+            src = diffs.rearrange("p t (c i) -> p c t i", i=2)
+            factor = neg_lift[:, 4 * b : 4 * b + 4].unsqueeze(1).unsqueeze(3).to_broadcast([P, diffs.shape[2] // 2, 4, 2])
+            nc.vector.tensor_tensor(into.rearrange("p (c i t) -> p c t i", i=2, t=4), src, factor, ALU.mult)
+
+        def quantise_z(b, first, count, woven):
             cols = slice(first, first + count)
-            nc.vector.quantize_mx(
-                out=z_codes[b][:, cols].bitcast(FP8X4), scales=z_sc[b][:, cols], in_=woven_of(b, first, count)
-            )
+            nc.vector.quantize_mx(out=z_codes[b][:, cols].bitcast(FP8X4), scales=z_sc[b][:, cols], in_=woven)
 
         sums = {}
 
@@ -317,115 +332,108 @@ def tile_list_spice_substitution_kernel(
             for i in range(len(SPAN_BANKS[s])):
                 second_passes(s, i, b)
 
-        def turn_late(n):
-            a, u = divmod(n, 2)
-            turn_w(a, 1, u)
+        def close(s, i):
+            second_passes(s, i, 1)
+            finish(s, i)
 
-        def width_of(k):
-            return M if k < 4 else WIDE
-
-        def step(k):
-            make_damp(k)
-            pick_repl(k, 0, width_of(k), prods[k % 3][:, 0 : width_of(k)])
-            pick_carr(k - 1, 0, width_of(k - 1))
-
+        for q in range(2):
+            quarter_passes(q, 0)
         for k in range(4):
             for half in range(2):
-                first_pass(k, half, 0)
-        finish_h(0, 0)
-        finish_h(1, 0)
+                if k >= 2 or half == 1:
+                    first_pass(k, half, 0)
+        for q in range(2):
+            finish_quarter(q)
+        finish_h(2, 0)
         finish_h(0, 1)
-        group_w(0, 1, nc.vector.tensor_copy, 0, P)
-        c4_sc = placed([P, 2, K], U8, "c4_sc", LATE + 2 * T)
-        for q in range(4):
-            nc.sync.dma_start(
-                out=c4_sc[32 * q : 32 * q + 4, :, :].bitcast(I32),
-                in_=c4_scales[:, 4 * q : 4 * q + 4, :].rearrange("b r n -> r b n").bitcast(I32),
-            )
+        grouped[1, 1] = kept([P, 4 * PASS], BF16, "grouped11")
+        for half in range(2):
+            dst = grouped[1, 1][:].rearrange("p (t m i) -> p m i t", t=4, i=4)[:, P // 2 * half : P // 2 * (half + 1)]
+            nc.vector.tensor_copy(out=dst, in_=late_halves[half][:].rearrange("p i (m t) -> p m i t", t=4))
         finish_h(1, 1, 2 * P)
-        quantise_wk(0, 1)
+        quantise_wk(1, 1)
         for first in (0, 2 * P):
             make_damp(0, first, 2 * P)
-            pick_repl(0, first, 2 * P, prods[0][:, first : first + 2 * P])
-        group_w(1, 1, nc.vector.tensor_copy, 0, P)
+            repl(0, first, 2 * P)
         copy_h(1, 1, 2 * P, 2 * P)
+        for first in (0, 2 * P):
+            carr(0, first, 2 * P)
         make_damp(1)
-        pick_repl(1, 0, M, prods[1][:])
-        quantise_wk(1, 1)
-        pick_carr(0, 0, M, prods[0][:])
+        repl(1)
         neg_lift = kept([P, 8], F32, "neg_lift")
         nc.scalar.activation(out=neg_lift[:], in_=lift_sb[:].rearrange("p b t -> p (b t)"), func=ACT.Copy, scale=-1.0)
-        for k in range(2, 5):
-            make_h(k)
-            step(k)
-        pick_carr(4, 0, WIDE)
+        finish_h(2, 1)
+        make_damp(2)
+        repl(2)
+        carr(1)
+        carr(2)
+        make_h(3)
+        make_damp(3)
+        for first in (0, 2 * P):
+            repl(3, first, 2 * P)
+        for first in (0, 2 * P):
+            carr(3, first, 2 * P)
+        make_h(4)
+        make_damp(4)
+        repl(4)
+        woven0 = kept([P, 4 * WIDE], BF16, "woven0")
+        weave(0, diffs0[:, :, 0:WIDE], woven0[:])
+        carr(4)
+        quantise_z(0, 0, WIDE, woven0[:])
+
+        first1, first2 = SPANS[1][0], SPANS[2][0]
+        prod6 = kept([P, WIDE], F32, "prod6")
+        prod7 = kept([P, first1], F32, "prod7")
+        carr67 = kept([P, 2, WIDE], F32, "carr67")
         make_h(5)
         make_damp(5)
-        pick_repl(5, 0, WIDE, prods[2][:, 0:WIDE])
-        weave(0, 0, WIDE)
-        pick_carr(5, 0, WIDE)
-        quantise_z(0, 0, WIDE)
-        prod6 = kept([P, WIDE], F32, "prod6")
-        prod7 = kept([P, 2 * P], F32, "prod7")
-        carr67 = kept([P, 2, WIDE], F32, "carr67")
+        repl(5)
         make_h(6)
         make_damp(6)
         pick_repl(6, 0, WIDE, prod6[:])
+        carr(5)
         make_h(7)
-        turn_late(0)
+        fetch_carr(6, 0, WIDE, carr67[:, 0, :])
         make_damp(7)
-        for k in (6, 7):
-            fetch_carr(k, 0, WIDE, carr67[:, k - 6, :])
-        turn_late(1)
-        back_sb = kept([P, 8], F32, "back_sb", "grouped01")
-        with nc.allow_non_contiguous_dma(reason="one factor for each output row"):
-            nc.sync.dma_start(out=back_sb[:], in_=back.rearrange("(j p) -> p j", p=P))
-        turn_late(2)
-        turn_late(3)
+        fetch_carr(7, 0, WIDE, carr67[:, 1, :])
+        turn_w(1, 1, 0)
         all_banks(0, 0)
-        def subtract(k, first, width, src):
-            cols = slice(first, first + width)
-            nc.vector.tensor_tensor(diffs1[:, k - 4, cols], carr67[:, k - 6, cols], src, ALU.subtract)
-
-        pick_repl(7, 0, 2 * P, prod7[:])
-        subtract(6, 0, WIDE, prod6[:])
-        subtract(7, 0, 2 * P, prod7[:])
-        pick_repl(7, 2 * P, P, prod6[:, 0:P])
-        weave(1, 0, 2 * P)
-        quantise_wr(0, 1)
-        quantise_z(1, 0, 2 * P)
-        subtract(7, 2 * P, P, prod6[:, 0:P])
-        prod_last = kept([P, 4, P], F32, "prod_last", "prod7")
-        pick_repl(4, WIDE, P, prod_last[:, 0, :])
-        weave(1, 2 * P, P)
-        quantise_wr(1, 1)
-        quantise_z(1, 2 * P, P)
-        carr_last = kept([P, 4, P], F32, "carr_last")
-        for i in range(4):
-            second_passes(0, i, 1)
-            finish(0, i)
-            if i == 1:
-                for k in range(4, 8):
-                    fetch_carr(k, WIDE, P, carr_last[:, k - 4, :])
         all_banks(1, 0)
-        late_woven[0] = kept([P, 4 * P], BF16, "late_woven", "prod6")
-        weave(0, WIDE, P)
-        pick_repl(5, WIDE, P, prod_last[:, 1, :])
-        quantise_z(0, WIDE, P)
+        pick_repl(7, 0, first1, prod7[:])
+        nc.vector.tensor_tensor(diffs1[:, 2, :], carr67[:, 0, :], prod6[:], ALU.subtract)
+        nc.vector.tensor_tensor(diffs1[:, 3, 0:first1], carr67[:, 1, 0:first1], prod7[:], ALU.subtract)
+        pick_repl(7, first1, P, prod6[:, 0:P])
+        woven1 = kept([P, 4 * M], BF16, "woven1")
+        weave(1, diffs1[:, :, 0:first1], woven1[:, 0 : 4 * first1])
+        quantise_z(1, 0, first1, woven1[:, 0 : 4 * first1])
+        quantise_wr(1, 1, kept([P, PASS], U32, "wr11_codes"))
+
+        nc.vector.tensor_tensor(diffs1[:, 3, first1:], carr67[:, 1, first1:], prod6[:, 0:P], ALU.subtract)
+        prod_c = kept([P, 4, P], F32, "prod_c", "prod7")
+        pick_repl(4, first2, P, prod_c[:, 0, :])
+        late_woven = kept([P, 4 * P], BF16, "late_woven", "prod6")
+        weave(0, diffs0[:, :, first2:], late_woven[:])
+        weave(1, diffs1[:, :, first1:], woven1[:, 4 * first1 : 4 * first2])
+        quantise_z(0, first2, P, late_woven[:])
+        quantise_z(1, first1, P, woven1[:, 4 * first1 : 4 * first2])
+        carr_c = kept([P, 4, P], F32, "carr_c")
+        for t in range(4):
+            fetch_carr(4 + t, first2, P, carr_c[:, t, :])
+        for i in range(4):
+            close(0, i)
         for i in range(2):
-            second_passes(1, i, 1)
-            finish(1, i)
+            close(1, i)
         all_banks(2, 0)
-        pick_repl(6, WIDE, P, prod_last[:, 2, :])
-        pick_repl(7, WIDE, P, prod_last[:, 3, :])
-        nc.vector.tensor_tensor(diffs_last[:, 0:3, :], carr_last[:, 0:3, :], prod_last[:, 0:3, :], ALU.subtract)
-        for at in (0, P // 2):
-            cols = slice(at, at + P // 2)
-            nc.vector.tensor_tensor(diffs_last[:, 3, cols], carr_last[:, 3, cols], prod_last[:, 3, cols], ALU.subtract)
-        for at in (0, P // 2):
-            weave(1, WIDE + at, P // 2)
-        for at in (0, P // 2):
-            quantise_z(1, WIDE + at, P // 2)
-        for i in range(3):
-            second_passes(2, i, 1)
-            finish(2, i)
+        for t in range(1, 4):
+            pick_repl(4 + t, first2, P, prod_c[:, t, :])
+        nc.vector.tensor_tensor(diffs_last[:, 0:3, :], carr_c[:, 0:3, :], prod_c[:, 0:3, :], ALU.subtract)
+        halves = [slice(at, at + P // 2) for at in (0, P // 2)]
+        for cols in halves:
+            nc.vector.tensor_tensor(diffs_last[:, 3, cols], carr_c[:, 3, cols], prod_c[:, 3, cols], ALU.subtract)
+        last = [woven1[:, 4 * (first2 + cols.start) : 4 * (first2 + cols.stop)] for cols in halves]
+        for n, cols in enumerate(halves):
+            weave(1, diffs_last[:, :, cols], last[n])
+        for n, cols in enumerate(halves):
+            quantise_z(1, first2 + cols.start, P // 2, last[n])
+        for i in range(4):
+            close(2, i)

@@ -325,8 +325,11 @@ def tile_list_spice_substitution_kernel(
                         func=ACT.Copy,
                         scale=back_sb[:, j0 + e : j0 + e + 1],
                     )
-            rows = out[P * j0 : P * (j0 + per_bank), first : first + width]
-            nc.sync.dma_start(out=rows.rearrange("(e p) m -> p e m", p=P), in_=res[:])
+                    if (s, i) == (0, 0):
+                        nc.sync.dma_start(out=out[P * e : P * (e + 1), first : first + width], in_=res[:, e, :])
+            if (s, i) != (0, 0):
+                rows = out[P * j0 : P * (j0 + per_bank), first : first + width]
+                nc.sync.dma_start(out=rows.rearrange("(e p) m -> p e m", p=P), in_=res[:])
 
         def all_banks(s, b):
             for i in range(len(SPAN_BANKS[s])):
@@ -402,19 +405,22 @@ def tile_list_spice_substitution_kernel(
         pick_repl(7, 0, first1, prod7[:])
         nc.vector.tensor_tensor(diffs1[:, 2, :], carr67[:, 0, :], prod6[:], ALU.subtract)
         nc.vector.tensor_tensor(diffs1[:, 3, 0:first1], carr67[:, 1, 0:first1], prod7[:], ALU.subtract)
-        pick_repl(7, first1, P, prod6[:, 0:P])
-        woven1 = kept([P, 4 * M], BF16, "woven1")
-        weave(1, diffs1[:, :, 0:first1], woven1[:, 0 : 4 * first1])
-        quantise_z(1, 0, first1, woven1[:, 0 : 4 * first1])
-        quantise_wr(1, 1, kept([P, PASS], U32, "wr11_codes"))
-
-        nc.vector.tensor_tensor(diffs1[:, 3, first1:], carr67[:, 1, first1:], prod6[:, 0:P], ALU.subtract)
-        prod_c = kept([P, 4, P], F32, "prod_c", "prod7")
-        pick_repl(4, first2, P, prod_c[:, 0, :])
         late_woven = kept([P, 4 * P], BF16, "late_woven", "prod6")
         weave(0, diffs0[:, :, first2:], late_woven[:])
-        weave(1, diffs1[:, :, first1:], woven1[:, 4 * first1 : 4 * first2])
+        woven1 = kept([P, 4 * M], BF16, "woven1")
+        weave(1, diffs1[:, :, 0:first1], woven1[:, 0 : 4 * first1])
         quantise_z(0, first2, P, late_woven[:])
+        prod7b = kept([P, P], F32, "prod7b", "prod7")
+        pick_repl(7, first1, P, prod7b[:])
+        quantise_z(1, 0, first1, woven1[:, 0 : 4 * first1])
+        for i in range(2):
+            second_passes(2, i, 0)
+
+        nc.vector.tensor_tensor(diffs1[:, 3, first1:], carr67[:, 1, first1:], prod7b[:], ALU.subtract)
+        quantise_wr(1, 1, kept([P, PASS], U32, "wr11_codes"))
+        weave(1, diffs1[:, :, first1:], woven1[:, 4 * first1 : 4 * first2])
+        prod_c = kept([P, 4, P], F32, "prod_c", "prod7")
+        pick_repl(4, first2, P, prod_c[:, 0, :])
         quantise_z(1, first1, P, woven1[:, 4 * first1 : 4 * first2])
         carr_c = kept([P, 4, P], F32, "carr_c")
         for t in range(4):
@@ -423,13 +429,14 @@ def tile_list_spice_substitution_kernel(
             close(0, i)
         for i in range(2):
             close(1, i)
-        all_banks(2, 0)
+        for i in range(2, 4):
+            second_passes(2, i, 0)
         for t in range(1, 4):
             pick_repl(4 + t, first2, P, prod_c[:, t, :])
-        nc.vector.tensor_tensor(diffs_last[:, 0:3, :], carr_c[:, 0:3, :], prod_c[:, 0:3, :], ALU.subtract)
+        nc.vector.tensor_tensor(diffs_last[:, 0:2, :], carr_c[:, 0:2, :], prod_c[:, 0:2, :], ALU.subtract)
         halves = [slice(at, at + P // 2) for at in (0, P // 2)]
         for cols in halves:
-            nc.vector.tensor_tensor(diffs_last[:, 3, cols], carr_c[:, 3, cols], prod_c[:, 3, cols], ALU.subtract)
+            nc.vector.tensor_tensor(diffs_last[:, 2:4, cols], carr_c[:, 2:4, cols], prod_c[:, 2:4, cols], ALU.subtract)
         last = [woven1[:, 4 * (first2 + cols.start) : 4 * (first2 + cols.stop)] for cols in halves]
         for n, cols in enumerate(halves):
             weave(1, diffs_last[:, :, cols], last[n])

@@ -21,10 +21,11 @@ PASS = 512
 BANK = 512
 SPANS = ((0, 256), (256, 128), (384, 128))
 SPAN_BANKS = (
-    ((4, 0, 2), (5, 2, 2), (6, 4, 2), (7, 6, 2)),
-    ((2, 0, 4), (3, 4, 4)),
-    ((0, 0, 2), (1, 2, 2), (4, 4, 2), (5, 6, 2)),
+    ((0, 0, 2), (1, 2, 2), (2, 4, 2), (3, 6, 2)),
+    ((6, 0, 4), (7, 4, 4)),
+    ((4, 0, 2), (5, 2, 2), (0, 4, 2), (1, 6, 2)),
 )
+HALF = M // 2
 TAB0, TAB1, AFTER = 2 * T, 6 * T, 10 * T + 64
 
 
@@ -120,7 +121,7 @@ def tile_list_spice_substitution_kernel(
 
         def gather_words(a, half):
             v_codes[a, half] = kept([P, BANK], U32, "v%d%d" % (a, half))
-            count = BANK // 2 if (a, half) == (1, 0) else BANK
+            count = BANK // 2 if a == 1 else BANK
             for first in range(0, BANK, count):
                 at = (BANK * half + first) // 16
                 cols = offs_sb[:, at : at + count // 16]
@@ -189,14 +190,15 @@ def tile_list_spice_substitution_kernel(
 
         def quarter_passes(q, a):
             if a == 0:
-                h_banks["quarter", q] = bank(2 * q)
+                h_banks["quarter", q] = bank(q)
             cols = slice(2 * P * q, 2 * P * (q + 1))
+            within = slice(2 * P * (q % 2), 2 * P * (q % 2 + 1))
             for k in range(2):
                 nc.tensor.matmul_mx(
                     out=h_banks["quarter", q][:, 2 * P * k : 2 * P * (k + 1)],
                     lhsT=wk_codes[a, 0][:, P * k : P * (k + 1)].bitcast(FP8X4),
                     lhsT_scale=wk_sc[a, 0][:, P * k : P * (k + 1)],
-                    rhs=v_codes[a, 0][:, cols].bitcast(FP8X4),
+                    rhs=v_codes[a, q // 2][:, within].bitcast(FP8X4),
                     rhs_scale=v_sc[a][:, cols],
                     start=(a == 0 and k == 0),
                     stop=(a == 1 and k == 1),
@@ -209,15 +211,11 @@ def tile_list_spice_substitution_kernel(
                     h[k] = kept([P, S], F32, "h%d" % k)
                 nc.scalar.copy(out=h[k][:, 2 * P * q : 2 * P * (q + 1)], in_=h_banks["quarter", q][:, 2 * P * k : 2 * P * (k + 1)])
 
-        def copy_h(k, half, first, count):
-            at = BANK * half + first
-            nc.scalar.copy(out=h[k][:, at : at + count], in_=h_banks[k, half][:, first : first + count])
-
-        def finish_h(k, half, count=BANK):
+        def finish_h(k, half, copy=nc.scalar.copy):
             first_pass(k, half, 1)
             if half == 0:
                 h[k] = kept([P, S], F32, "h%d" % k)
-            copy_h(k, half, 0, count)
+            copy(out=h[k][:, BANK * half : BANK * (half + 1)], in_=h_banks[k, half][:])
 
         def make_h(k):
             for half in range(2):
@@ -225,52 +223,20 @@ def tile_list_spice_substitution_kernel(
                     first_pass(k, half, 0)
                 finish_h(k, half)
 
-        WIDE = SPANS[2][0]
-        diffs0 = kept([P, 4, M], F32, "diffs0")
-        diffs1 = kept([P, 4, WIDE], F32, "diffs1")
-        diffs_last = kept([P, 4, P], F32, "diffs_last")
-        nc.scalar.copy(out=diffs0[:, 1, 0:1], in_=fade_sb[:, 2:3])
-        fade4 = kept([P, 1], F32, "fade4", "woven0")
-        nc.scalar.copy(out=fade4[:], in_=fade_sb[:, 4:5])
-        nc.scalar.copy(out=diffs1[:, 1:3, 0:1], in_=fade_sb[:, 6:8].unsqueeze(2))
-
-        def fade_of(k):
-            if k == 2:
-                return diffs0[:, 1, 0:1]
-            if k >= 6:
-                return diffs1[:, k - 5, 0:1]
-            return fade4[:] if k == 4 else fade_sb[:, k : k + 1]
-
-        prods = [placed([P, M], F32, "prods%d" % i, 4 * M * i) for i in range(3)]
-        damp = {}
-
         def picked(k, which, first, width):
             return h[k][:].indirect(lists[which][:, first // 16 : (first + width) // 16])
 
-        def make_damp(k, first=0, width=M):
-            if first == 0:
-                damp[k] = kept([P, M], F32, "damp%d" % k)
-            nc.scalar.activation(
-                out=damp[k][:, first : first + width], in_=picked(k, 0, first, width), func=ACT.Exp, scale=fade_of(k)
-            )
+        def make_damp(k, first, into, factor):
+            nc.scalar.activation(out=into, in_=picked(k, 0, first, HALF), func=ACT.Exp, scale=factor)
 
-        def pick_repl(k, first, width, into):
-            nc.vector.tensor_tensor(into, picked(k, 1, first, width), damp[k][:, first : first + width], ALU.mult)
+        def pick_repl(k, first, width, damp, into):
+            nc.vector.tensor_tensor(into, picked(k, 1, first, width), damp, ALU.mult)
 
         def pick_carr(k, first, width, prod, into):
             nc.vector.tensor_tensor(into, picked(k, 2, first, width), prod, ALU.subtract)
 
         def fetch_carr(k, first, width, into):
             nc.scalar.activation(out=into, in_=picked(k, 2, first, width), func=ACT.Copy)
-
-        def repl(k, first=0, width=None):
-            width = width or (M if k < 4 else WIDE)
-            pick_repl(k, first, width, prods[k % 3][:, first : first + width])
-
-        def carr(k, first=0, width=None):
-            width = width or (M if k < 4 else WIDE)
-            into = diffs0[:, k, first : first + width] if k < 4 else diffs1[:, k - 4, :]
-            pick_carr(k, first, width, prods[k % 3][:, first : first + width], into)
 
         z_codes = [kept([P, M], U32, "z_codes%d" % b) for b in range(2)]
         z_sc = [kept([P, M], U8, "z_sc%d" % b) for b in range(2)]
@@ -325,11 +291,8 @@ def tile_list_spice_substitution_kernel(
                         func=ACT.Copy,
                         scale=back_sb[:, j0 + e : j0 + e + 1],
                     )
-                    if (s, i) == (0, 0):
-                        nc.sync.dma_start(out=out[P * e : P * (e + 1), first : first + width], in_=res[:, e, :])
-            if (s, i) != (0, 0):
-                rows = out[P * j0 : P * (j0 + per_bank), first : first + width]
-                nc.sync.dma_start(out=rows.rearrange("(e p) m -> p e m", p=P), in_=res[:])
+            rows = out[P * j0 : P * (j0 + per_bank), first : first + width]
+            nc.sync.dma_start(out=rows.rearrange("(e p) m -> p e m", p=P), in_=res[:])
 
         def all_banks(s, b):
             for i in range(len(SPAN_BANKS[s])):
@@ -339,108 +302,150 @@ def tile_list_spice_substitution_kernel(
             second_passes(s, i, 1)
             finish(s, i)
 
-        for q in range(2):
+        diffs = [kept([P, 4, M], F32, "diffs%d" % b) for b in range(2)]
+        nc.scalar.copy(out=diffs[0][:, 1, 0:1], in_=fade_sb[:, 2:3])
+        fade_at = {k: fade_sb[:, k : k + 1] for k in range(8)}
+        fade_at[2] = diffs[0][:, 1, 0:1]
+        for half in range(2):
+            held = kept([P, 1], F32, "fade%d" % (4 + half), "woven0%d" % half)
+            nc.scalar.copy(out=held[:], in_=fade_sb[:, 4 + half : 5 + half])
+            fade_at[4 + half] = held[:]
+        damps = kept([P, 4, M], F32, "damps")
+        prods = [placed([P, M], F32, "prods%d" % i, 4 * M * i) for i in range(3)]
+
+        def tile_damp(k, first, width):
+            into = damps[:, k % 4, first : first + width]
+            nc.scalar.activation(out=into, in_=picked(k, 0, first, width), func=ACT.Exp, scale=fade_at[k])
+
+        def tile_repl(k, first, width):
+            cols = slice(first, first + width)
+            pick_repl(k, first, width, damps[:, k % 4, cols], prods[k % 3][:, cols])
+
+        def tile_carr(k, first, width):
+            cols = slice(first, first + width)
+            pick_carr(k, first, width, prods[k % 3][:, cols], diffs[k // 4][:, k % 4, cols])
+
+        def upper_weave(s):
+            first, width = SPANS[s]
+            woven = kept([P, 4 * width], BF16, "woven0%d" % s)
+            weave(0, diffs[0][:, :, first : first + width], woven[:])
+            return woven
+
+        for q in range(4):
             quarter_passes(q, 0)
-        for k in range(4):
+        for k in range(2, 4):
             for half in range(2):
-                if k >= 2 or half == 1:
-                    first_pass(k, half, 0)
+                first_pass(k, half, 0)
         for q in range(2):
             finish_quarter(q)
-        finish_h(2, 0)
-        finish_h(0, 1)
+        finish_h(2, 0, nc.vector.tensor_copy)
+        for q in range(2, 4):
+            finish_quarter(q)
         grouped[1, 1] = kept([P, 4 * PASS], BF16, "grouped11")
         for half in range(2):
             dst = grouped[1, 1][:].rearrange("p (t m i) -> p m i t", t=4, i=4)[:, P // 2 * half : P // 2 * (half + 1)]
             nc.vector.tensor_copy(out=dst, in_=late_halves[half][:].rearrange("p i (m t) -> p m i t", t=4))
-        finish_h(1, 1, 2 * P)
         quantise_wk(1, 1)
-        for first in (0, 2 * P):
-            make_damp(0, first, 2 * P)
-            repl(0, first, 2 * P)
-        copy_h(1, 1, 2 * P, 2 * P)
-        for first in (0, 2 * P):
-            carr(0, first, 2 * P)
-        make_damp(1)
-        repl(1)
+        for first in (0, HALF):
+            tile_damp(0, first, HALF)
+            tile_repl(0, first, HALF)
+        for first in (0, HALF):
+            tile_carr(0, first, HALF)
+        tile_damp(1, 0, M)
+        tile_repl(1, 0, M)
         neg_lift = kept([P, 8], F32, "neg_lift")
         nc.scalar.activation(out=neg_lift[:], in_=lift_sb[:].rearrange("p b t -> p (b t)"), func=ACT.Copy, scale=-1.0)
         finish_h(2, 1)
-        make_damp(2)
-        repl(2)
-        carr(1)
-        carr(2)
+        tile_damp(2, 0, M)
+        WIDE = SPANS[2][0]
+        tile_repl(2, 0, WIDE)
+        tile_carr(1, 0, M)
+        tile_carr(2, 0, WIDE)
         make_h(3)
-        make_damp(3)
-        for first in (0, 2 * P):
-            repl(3, first, 2 * P)
-        for first in (0, 2 * P):
-            carr(3, first, 2 * P)
-        make_h(4)
-        make_damp(4)
-        repl(4)
-        woven0 = kept([P, 4 * WIDE], BF16, "woven0")
-        weave(0, diffs0[:, :, 0:WIDE], woven0[:])
-        carr(4)
-        quantise_z(0, 0, WIDE, woven0[:])
+        tile_damp(3, 0, M)
+        for step in (tile_repl, tile_carr):
+            for first in (0, WIDE // 2):
+                step(3, first, WIDE // 2)
+        for half in range(2):
+            k = 4 + half
+            make_h(k)
+            tile_damp(k, 0, HALF)
+            tile_repl(k, 0, HALF)
+            woven = upper_weave(half)
+            tile_carr(k, 0, HALF)
+            quantise_z(0, *SPANS[half], woven[:])
+        last_prod = kept([P, 2, HALF], F32, "last_prod")
+        last_carr = kept([P, 2, HALF], F32, "last_carr")
+        for k in range(6, 8):
+            make_h(k)
+            tile_damp(k, 0, HALF)
+            pick_repl(k, 0, HALF, damps[:, k % 4, 0:HALF], last_prod[:, k - 6, :])
 
-        first1, first2 = SPANS[1][0], SPANS[2][0]
-        prod6 = kept([P, WIDE], F32, "prod6")
-        prod7 = kept([P, first1], F32, "prod7")
-        carr67 = kept([P, 2, WIDE], F32, "carr67")
-        make_h(5)
-        make_damp(5)
-        repl(5)
-        make_h(6)
-        make_damp(6)
-        pick_repl(6, 0, WIDE, prod6[:])
-        carr(5)
-        make_h(7)
-        fetch_carr(6, 0, WIDE, carr67[:, 0, :])
-        make_damp(7)
-        fetch_carr(7, 0, WIDE, carr67[:, 1, :])
-        turn_w(1, 1, 0)
+        right_damp = kept([P, 4, HALF], F32, "right_damp")
+        part_prod = kept([P, 4, P], F32, "part_prod")
+        part_carr = {s: kept([P, 4, P], F32, "part_carr%d" % s) for s in (1, 2)}
+        woven1 = kept([P, 4 * M], BF16, "woven1")
+
+        def part_repl(s, t):
+            first = SPANS[s][0]
+            pick_repl(4 + t, first, P, right_damp[:, t, first - HALF : first - HALF + P], part_prod[:, t, :])
+
+        def part_fetch(s):
+            for t in range(4):
+                fetch_carr(4 + t, SPANS[s][0], P, part_carr[s][:, t, :])
+
+        def part_subtract(s, first, count):
+            at = first - SPANS[s][0]
+            cols = slice(at, at + count)
+            nc.vector.tensor_tensor(diffs[1][:, :, first : first + count], part_carr[s][:, :, cols], part_prod[:, :, cols], ALU.subtract)
+
+        def lower_weave(s, first, count):
+            weave(1, diffs[1][:, :, first : first + count], woven1[:, 4 * first : 4 * (first + count)])
+
+        def lower_quantise(s, first, count):
+            quantise_z(1, first, count, woven1[:, 4 * first : 4 * (first + count)])
+
+        for t in range(4):
+            make_damp(4 + t, HALF, right_damp[:, t, :], fade_sb[:, 4 + t : 5 + t])
+            if t == 1:
+                for k in range(6, 8):
+                    fetch_carr(k, 0, HALF, last_carr[:, k - 6, :])
+        part_fetch(1)
+        turn_w(1, 1, 4)
         all_banks(0, 0)
         all_banks(1, 0)
-        pick_repl(7, 0, first1, prod7[:])
-        nc.vector.tensor_tensor(diffs1[:, 2, :], carr67[:, 0, :], prod6[:], ALU.subtract)
-        nc.vector.tensor_tensor(diffs1[:, 3, 0:first1], carr67[:, 1, 0:first1], prod7[:], ALU.subtract)
-        late_woven = kept([P, 4 * P], BF16, "late_woven", "prod6")
-        weave(0, diffs0[:, :, first2:], late_woven[:])
-        woven1 = kept([P, 4 * M], BF16, "woven1")
-        weave(1, diffs1[:, :, 0:first1], woven1[:, 0 : 4 * first1])
-        quantise_z(0, first2, P, late_woven[:])
-        prod7b = kept([P, P], F32, "prod7b", "prod7")
-        pick_repl(7, first1, P, prod7b[:])
-        quantise_z(1, 0, first1, woven1[:, 0 : 4 * first1])
+        part_repl(1, 0)
+        part_repl(1, 1)
+        nc.vector.tensor_tensor(diffs[1][:, 2:4, 0:HALF], last_carr[:], last_prod[:], ALU.subtract)
+        lower_weave(0, *SPANS[0])
+        part_repl(1, 2)
+        lower_quantise(0, *SPANS[0])
+        part_repl(1, 3)
         for i in range(2):
-            second_passes(2, i, 0)
-
-        nc.vector.tensor_tensor(diffs1[:, 3, first1:], carr67[:, 1, first1:], prod7b[:], ALU.subtract)
+            close(0, i)
+        upper_prod = kept([P, 2, P], F32, "upper_prod", "last_prod")
+        for k in range(2, 4):
+            pick_repl(k, WIDE, P, damps[:, k, WIDE:], upper_prod[:, k - 2, :])
+        part_subtract(1, *SPANS[1])
+        for k in range(2, 4):
+            pick_carr(k, WIDE, P, upper_prod[:, k - 2, :], diffs[0][:, k, WIDE:])
+        lower_weave(1, *SPANS[1])
         quantise_wr(1, 1, kept([P, PASS], U32, "wr11_codes"))
-        weave(1, diffs1[:, :, first1:], woven1[:, 4 * first1 : 4 * first2])
-        prod_c = kept([P, 4, P], F32, "prod_c", "prod7")
-        pick_repl(4, first2, P, prod_c[:, 0, :])
-        quantise_z(1, first1, P, woven1[:, 4 * first1 : 4 * first2])
-        carr_c = kept([P, 4, P], F32, "carr_c")
-        for t in range(4):
-            fetch_carr(4 + t, first2, P, carr_c[:, t, :])
-        for i in range(4):
+        lower_quantise(1, *SPANS[1])
+        part_fetch(2)
+        for i in range(2, 4):
             close(0, i)
         for i in range(2):
             close(1, i)
-        for i in range(2, 4):
-            second_passes(2, i, 0)
-        for t in range(1, 4):
-            pick_repl(4 + t, first2, P, prod_c[:, t, :])
-        nc.vector.tensor_tensor(diffs_last[:, 0:2, :], carr_c[:, 0:2, :], prod_c[:, 0:2, :], ALU.subtract)
-        halves = [slice(at, at + P // 2) for at in (0, P // 2)]
-        for cols in halves:
-            nc.vector.tensor_tensor(diffs_last[:, 2:4, cols], carr_c[:, 2:4, cols], prod_c[:, 2:4, cols], ALU.subtract)
-        last = [woven1[:, 4 * (first2 + cols.start) : 4 * (first2 + cols.stop)] for cols in halves]
-        for n, cols in enumerate(halves):
-            weave(1, diffs_last[:, :, cols], last[n])
-        for n, cols in enumerate(halves):
-            quantise_z(1, first2 + cols.start, P // 2, last[n])
+        for t in range(2):
+            part_repl(2, t)
+        woven = upper_weave(2)
+        quantise_z(0, *SPANS[2], woven[:])
+        all_banks(2, 0)
+        for t in range(2, 4):
+            part_repl(2, t)
+        for step in (part_subtract, lower_weave, lower_quantise):
+            for first in (SPANS[2][0], SPANS[2][0] + P // 2):
+                step(2, first, P // 2)
         for i in range(4):
             close(2, i)

@@ -306,10 +306,9 @@ def tile_list_spice_substitution_kernel(
         nc.scalar.copy(out=diffs[0][:, 1, 0:1], in_=fade_sb[:, 2:3])
         fade_at = {k: fade_sb[:, k : k + 1] for k in range(8)}
         fade_at[2] = diffs[0][:, 1, 0:1]
-        for half in range(2):
-            held = kept([P, 1], F32, "fade%d" % (4 + half), "woven0%d" % half)
-            nc.scalar.copy(out=held[:], in_=fade_sb[:, 4 + half : 5 + half])
-            fade_at[4 + half] = held[:]
+        fade4 = kept([P, 1], F32, "fade4", "woven0")
+        nc.scalar.copy(out=fade4[:], in_=fade_sb[:, 4:5])
+        fade_at[4] = fade4[:]
         damps = kept([P, 4, M], F32, "damps")
         prods = [placed([P, M], F32, "prods%d" % i, 4 * M * i) for i in range(3)]
 
@@ -325,26 +324,21 @@ def tile_list_spice_substitution_kernel(
             cols = slice(first, first + width)
             pick_carr(k, first, width, prods[k % 3][:, cols], diffs[k // 4][:, k % 4, cols])
 
-        def upper_weave(s):
-            first, width = SPANS[s]
-            woven = kept([P, 4 * width], BF16, "woven0%d" % s)
-            weave(0, diffs[0][:, :, first : first + width], woven[:])
-            return woven
-
         for q in range(4):
             quarter_passes(q, 0)
         for k in range(2, 4):
             for half in range(2):
                 first_pass(k, half, 0)
-        for q in range(2):
+        finish_quarter(0)
+        for q in range(1, 3):
             finish_quarter(q)
-        finish_h(2, 0, nc.vector.tensor_copy)
-        for q in range(2, 4):
-            finish_quarter(q)
+            finish_h(q + 1, 0, nc.vector.tensor_copy)
+        finish_quarter(3)
         grouped[1, 1] = kept([P, 4 * PASS], BF16, "grouped11")
         for half in range(2):
-            dst = grouped[1, 1][:].rearrange("p (t m i) -> p m i t", t=4, i=4)[:, P // 2 * half : P // 2 * (half + 1)]
-            nc.vector.tensor_copy(out=dst, in_=late_halves[half][:].rearrange("p i (m t) -> p m i t", t=4))
+            dst = grouped[1, 1][:].rearrange("p (t m i) -> p m t i", t=4, i=4)[:, P // 2 * half : P // 2 * (half + 1)]
+            src = late_halves[half][:].rearrange("p i (m t) -> p m t i", t=4)
+            nc.gpsimd.tensor_scalar(out=dst, in0=src, scalar1=1.0, scalar2=0.0, op0=ALU.mult, op1=ALU.add)
         quantise_wk(1, 1)
         for first in (0, HALF):
             tile_damp(0, first, HALF)
@@ -355,31 +349,30 @@ def tile_list_spice_substitution_kernel(
         tile_repl(1, 0, M)
         neg_lift = kept([P, 8], F32, "neg_lift")
         nc.scalar.activation(out=neg_lift[:], in_=lift_sb[:].rearrange("p b t -> p (b t)"), func=ACT.Copy, scale=-1.0)
-        finish_h(2, 1)
+        finish_h(2, 1, nc.vector.tensor_copy)
         tile_damp(2, 0, M)
-        WIDE = SPANS[2][0]
-        tile_repl(2, 0, WIDE)
+        tile_repl(2, 0, M)
         tile_carr(1, 0, M)
-        tile_carr(2, 0, WIDE)
-        make_h(3)
+        tile_carr(2, 0, M)
+        finish_h(3, 1)
         tile_damp(3, 0, M)
         for step in (tile_repl, tile_carr):
-            for first in (0, WIDE // 2):
-                step(3, first, WIDE // 2)
-        for half in range(2):
-            k = 4 + half
+            for first in (0, HALF):
+                step(3, first, HALF)
+        WIDE = SPANS[2][0]
+        make_h(4)
+        tile_damp(4, 0, HALF)
+        tile_repl(4, 0, HALF)
+        woven0 = kept([P, 4 * WIDE], BF16, "woven0")
+        weave(0, diffs[0][:, :, 0:WIDE], woven0[:])
+        tile_carr(4, 0, HALF)
+        quantise_z(0, 0, WIDE, woven0[:])
+        last_prod = kept([P, 3, HALF], F32, "last_prod")
+        last_carr = kept([P, 3, HALF], F32, "last_carr")
+        for k in range(5, 8):
             make_h(k)
             tile_damp(k, 0, HALF)
-            tile_repl(k, 0, HALF)
-            woven = upper_weave(half)
-            tile_carr(k, 0, HALF)
-            quantise_z(0, *SPANS[half], woven[:])
-        last_prod = kept([P, 2, HALF], F32, "last_prod")
-        last_carr = kept([P, 2, HALF], F32, "last_carr")
-        for k in range(6, 8):
-            make_h(k)
-            tile_damp(k, 0, HALF)
-            pick_repl(k, 0, HALF, damps[:, k % 4, 0:HALF], last_prod[:, k - 6, :])
+            pick_repl(k, 0, HALF, damps[:, k % 4, 0:HALF], last_prod[:, k - 5, :])
 
         right_damp = kept([P, 4, HALF], F32, "right_damp")
         part_prod = kept([P, 4, P], F32, "part_prod")
@@ -408,41 +401,33 @@ def tile_list_spice_substitution_kernel(
         for t in range(4):
             make_damp(4 + t, HALF, right_damp[:, t, :], fade_sb[:, 4 + t : 5 + t])
             if t == 1:
-                for k in range(6, 8):
-                    fetch_carr(k, 0, HALF, last_carr[:, k - 6, :])
+                for k in range(5, 8):
+                    fetch_carr(k, 0, HALF, last_carr[:, k - 5, :])
         part_fetch(1)
         turn_w(1, 1, 4)
         all_banks(0, 0)
         all_banks(1, 0)
         part_repl(1, 0)
         part_repl(1, 1)
-        nc.vector.tensor_tensor(diffs[1][:, 2:4, 0:HALF], last_carr[:], last_prod[:], ALU.subtract)
-        lower_weave(0, *SPANS[0])
+        nc.vector.tensor_tensor(diffs[1][:, 1:4, 0:HALF], last_carr[:], last_prod[:], ALU.subtract)
         part_repl(1, 2)
-        lower_quantise(0, *SPANS[0])
+        lower_weave(0, *SPANS[0])
         part_repl(1, 3)
-        for i in range(2):
-            close(0, i)
-        upper_prod = kept([P, 2, P], F32, "upper_prod", "last_prod")
-        for k in range(2, 4):
-            pick_repl(k, WIDE, P, damps[:, k, WIDE:], upper_prod[:, k - 2, :])
-        part_subtract(1, *SPANS[1])
-        for k in range(2, 4):
-            pick_carr(k, WIDE, P, upper_prod[:, k - 2, :], diffs[0][:, k, WIDE:])
-        lower_weave(1, *SPANS[1])
-        quantise_wr(1, 1, kept([P, PASS], U32, "wr11_codes"))
-        lower_quantise(1, *SPANS[1])
+        lower_quantise(0, *SPANS[0])
         part_fetch(2)
-        for i in range(2, 4):
+        part_subtract(1, *SPANS[1])
+        quantise_wr(1, 1, kept([P, PASS], U32, "wr11_codes"))
+        for i in range(4):
             close(0, i)
+        lower_weave(1, *SPANS[1])
+        late_woven = kept([P, 4 * P], BF16, "late_woven", "last_prod")
+        weave(0, diffs[0][:, :, WIDE:], late_woven[:])
+        lower_quantise(1, *SPANS[1])
         for i in range(2):
             close(1, i)
-        for t in range(2):
-            part_repl(2, t)
-        woven = upper_weave(2)
-        quantise_z(0, *SPANS[2], woven[:])
+        quantise_z(0, *SPANS[2], late_woven[:])
         all_banks(2, 0)
-        for t in range(2, 4):
+        for t in range(4):
             part_repl(2, t)
         for step in (part_subtract, lower_weave, lower_quantise):
             for first in (SPANS[2][0], SPANS[2][0] + P // 2):

@@ -302,7 +302,7 @@ def tile_list_spice_substitution_kernel(
             second_passes(s, i, 1)
             finish(s, i)
 
-        diffs = [kept([P, 4, M], F32, "diffs%d" % b) for b in range(2)]
+        diffs = [kept([P, 4, (M, HALF)[b]], F32, "diffs%d" % b) for b in range(2)]
         nc.scalar.copy(out=diffs[0][:, 1, 0:1], in_=fade_sb[:, 2:3])
         fade_at = {k: fade_sb[:, k : k + 1] for k in range(8)}
         fade_at[2] = diffs[0][:, 1, 0:1]
@@ -377,7 +377,9 @@ def tile_list_spice_substitution_kernel(
         right_damp = kept([P, 4, HALF], F32, "right_damp")
         part_prod = kept([P, 4, P], F32, "part_prod")
         part_carr = {s: kept([P, 4, P], F32, "part_carr%d" % s) for s in (1, 2)}
-        woven1 = kept([P, 4 * M], BF16, "woven1")
+
+        def right_exp(t):
+            make_damp(4 + t, HALF, right_damp[:, t, :], fade_sb[:, 4 + t : 5 + t])
 
         def part_repl(s, t):
             first = SPANS[s][0]
@@ -387,50 +389,55 @@ def tile_list_spice_substitution_kernel(
             for t in range(4):
                 fetch_carr(4 + t, SPANS[s][0], P, part_carr[s][:, t, :])
 
-        def part_subtract(s, first, count):
-            at = first - SPANS[s][0]
-            cols = slice(at, at + count)
-            nc.vector.tensor_tensor(diffs[1][:, :, first : first + count], part_carr[s][:, :, cols], part_prod[:, :, cols], ALU.subtract)
+        def subtract(into, carr, prod):
+            nc.vector.tensor_tensor(into, carr, prod, ALU.subtract)
 
-        def lower_weave(s, first, count):
-            weave(1, diffs[1][:, :, first : first + count], woven1[:, 4 * first : 4 * (first + count)])
-
-        def lower_quantise(s, first, count):
-            quantise_z(1, first, count, woven1[:, 4 * first : 4 * (first + count)])
-
-        for t in range(4):
-            make_damp(4 + t, HALF, right_damp[:, t, :], fade_sb[:, 4 + t : 5 + t])
-            if t == 1:
-                for k in range(5, 8):
-                    fetch_carr(k, 0, HALF, last_carr[:, k - 5, :])
+        right_exp(0)
+        for k in range(5, 8):
+            fetch_carr(k, 0, HALF, last_carr[:, k - 5, :])
+        for t in range(1, 3):
+            right_exp(t)
         part_fetch(1)
+        right_exp(3)
         turn_w(1, 1, 4)
         all_banks(0, 0)
         all_banks(1, 0)
         part_repl(1, 0)
-        part_repl(1, 1)
-        nc.vector.tensor_tensor(diffs[1][:, 1:4, 0:HALF], last_carr[:], last_prod[:], ALU.subtract)
-        part_repl(1, 2)
-        lower_weave(0, *SPANS[0])
+        subtract(diffs[1][:, 1:4, :], last_carr[:], last_prod[:])
+        for t in range(1, 3):
+            part_repl(1, t)
+        woven1 = kept([P, 4 * HALF], BF16, "woven1")
+        weave(1, diffs[1][:], woven1[:])
         part_repl(1, 3)
-        lower_quantise(0, *SPANS[0])
-        part_fetch(2)
-        part_subtract(1, *SPANS[1])
-        quantise_wr(1, 1, kept([P, PASS], U32, "wr11_codes"))
-        for i in range(4):
+        quantise_z(1, *SPANS[0], woven1[:])
+        for i in range(2):
             close(0, i)
-        lower_weave(1, *SPANS[1])
-        late_woven = kept([P, 4 * P], BF16, "late_woven", "last_prod")
+        part_fetch(2)
+        late_woven = kept([P, 4 * P], BF16, "late_woven", "diffs1")
         weave(0, diffs[0][:, :, WIDE:], late_woven[:])
-        lower_quantise(1, *SPANS[1])
+        middle_diffs = kept([P, 4, P], F32, "middle_diffs", "woven1")
+        subtract(middle_diffs[:], part_carr[1][:], part_prod[:])
+        quantise_z(0, *SPANS[2], late_woven[:])
+        quantise_wr(1, 1, kept([P, PASS], U32, "wr11_codes"))
+        for i in range(2, 4):
+            close(0, i)
+        middle_woven = kept([P, 4 * P], BF16, "middle_woven")
+        weave(1, middle_diffs[:], middle_woven[:])
+        quantise_z(1, *SPANS[1], middle_woven[:])
         for i in range(2):
             close(1, i)
-        quantise_z(0, *SPANS[2], late_woven[:])
         all_banks(2, 0)
         for t in range(4):
             part_repl(2, t)
-        for step in (part_subtract, lower_weave, lower_quantise):
-            for first in (SPANS[2][0], SPANS[2][0] + P // 2):
-                step(2, first, P // 2)
+        last_diffs = kept([P, 4, P], F32, "last_diffs")
+        last_woven = kept([P, 4 * P], BF16, "last_woven")
+        halves = [slice(at, at + P // 2) for at in (0, P // 2)]
+        subtract(last_diffs[:, 0:2, :], part_carr[2][:, 0:2, :], part_prod[:, 0:2, :])
+        for cols in halves:
+            subtract(last_diffs[:, 2:4, cols], part_carr[2][:, 2:4, cols], part_prod[:, 2:4, cols])
+        for cols in halves:
+            weave(1, last_diffs[:, :, cols], last_woven[:, 4 * cols.start : 4 * cols.stop])
+        for cols in halves:
+            quantise_z(1, WIDE + cols.start, P // 2, last_woven[:, 4 * cols.start : 4 * cols.stop])
         for i in range(4):
             close(2, i)

@@ -306,9 +306,6 @@ def tile_list_spice_substitution_kernel(
         nc.scalar.copy(out=diffs[0][:, 1, 0:1], in_=fade_sb[:, 2:3])
         fade_at = {k: fade_sb[:, k : k + 1] for k in range(8)}
         fade_at[2] = diffs[0][:, 1, 0:1]
-        fade4 = kept([P, 1], F32, "fade4", "woven0")
-        nc.scalar.copy(out=fade4[:], in_=fade_sb[:, 4:5])
-        fade_at[4] = fade4[:]
         damps = kept([P, 4, M], F32, "damps")
         prods = [placed([P, M], F32, "prods%d" % i, 4 * M * i) for i in range(3)]
 
@@ -334,6 +331,8 @@ def tile_list_spice_substitution_kernel(
             finish_quarter(q)
             finish_h(q + 1, 0, nc.vector.tensor_copy)
         finish_quarter(3)
+        for k in range(2, 4):
+            finish_h(k, 1, nc.vector.tensor_copy)
         grouped[1, 1] = kept([P, 4 * PASS], BF16, "grouped11")
         for half in range(2):
             dst = grouped[1, 1][:].rearrange("p (t m i) -> p m t i", t=4, i=4)[:, P // 2 * half : P // 2 * (half + 1)]
@@ -349,34 +348,35 @@ def tile_list_spice_substitution_kernel(
         tile_repl(1, 0, M)
         neg_lift = kept([P, 8], F32, "neg_lift")
         nc.scalar.activation(out=neg_lift[:], in_=lift_sb[:].rearrange("p b t -> p (b t)"), func=ACT.Copy, scale=-1.0)
-        finish_h(2, 1, nc.vector.tensor_copy)
         tile_damp(2, 0, M)
         tile_repl(2, 0, M)
         tile_carr(1, 0, M)
         tile_carr(2, 0, M)
-        finish_h(3, 1)
         tile_damp(3, 0, M)
         for step in (tile_repl, tile_carr):
             for first in (0, HALF):
                 step(3, first, HALF)
         WIDE = SPANS[2][0]
-        make_h(4)
-        tile_damp(4, 0, HALF)
-        tile_repl(4, 0, HALF)
-        woven0 = kept([P, 4 * WIDE], BF16, "woven0")
-        weave(0, diffs[0][:, :, 0:WIDE], woven0[:])
-        tile_carr(4, 0, HALF)
-        quantise_z(0, 0, WIDE, woven0[:])
-        last_prod = kept([P, 3, HALF], F32, "last_prod")
-        last_carr = kept([P, 3, HALF], F32, "last_carr")
-        for k in range(5, 8):
+        last_prod = kept([P, 4, HALF], F32, "last_prod")
+        last_carr = kept([P, 4, HALF], F32, "last_carr")
+
+        def lower_tile(k):
             make_h(k)
             tile_damp(k, 0, HALF)
-            pick_repl(k, 0, HALF, damps[:, k % 4, 0:HALF], last_prod[:, k - 5, :])
+            pick_repl(k, 0, HALF, damps[:, k % 4, 0:HALF], last_prod[:, k - 4, :])
+
+        for s in range(2):
+            first, width = SPANS[s]
+            woven = kept([P, 4 * width], BF16, "woven0%d" % s)
+            weave(0, diffs[0][:, :, first : first + width], woven[:])
+            lower_tile(4 + s)
+            quantise_z(0, first, width, woven[:])
+        for k in range(6, 8):
+            lower_tile(k)
 
         right_damp = kept([P, 4, HALF], F32, "right_damp")
         part_prod = kept([P, 4, P], F32, "part_prod")
-        part_carr = {s: kept([P, 4, P], F32, "part_carr%d" % s) for s in (1, 2)}
+        middle_carr = kept([P, 4, P], F32, "middle_carr")
 
         def right_exp(t):
             make_damp(4 + t, HALF, right_damp[:, t, :], fade_sb[:, 4 + t : 5 + t])
@@ -385,38 +385,41 @@ def tile_list_spice_substitution_kernel(
             first = SPANS[s][0]
             pick_repl(4 + t, first, P, right_damp[:, t, first - HALF : first - HALF + P], part_prod[:, t, :])
 
-        def part_fetch(s):
-            for t in range(4):
-                fetch_carr(4 + t, SPANS[s][0], P, part_carr[s][:, t, :])
+        def part_fetch(s, tiles, into):
+            for n, t in enumerate(tiles):
+                fetch_carr(4 + t, SPANS[s][0], P, into[:, n, :])
 
         def subtract(into, carr, prod):
             nc.vector.tensor_tensor(into, carr, prod, ALU.subtract)
 
         right_exp(0)
-        for k in range(5, 8):
-            fetch_carr(k, 0, HALF, last_carr[:, k - 5, :])
+        for k in range(4, 8):
+            fetch_carr(k, 0, HALF, last_carr[:, k - 4, :])
         for t in range(1, 3):
             right_exp(t)
-        part_fetch(1)
+        part_fetch(1, range(4), middle_carr)
         right_exp(3)
         turn_w(1, 1, 4)
         all_banks(0, 0)
         all_banks(1, 0)
         part_repl(1, 0)
-        subtract(diffs[1][:, 1:4, :], last_carr[:], last_prod[:])
+        subtract(diffs[1][:], last_carr[:], last_prod[:])
         for t in range(1, 3):
             part_repl(1, t)
         woven1 = kept([P, 4 * HALF], BF16, "woven1")
         weave(1, diffs[1][:], woven1[:])
         part_repl(1, 3)
         quantise_z(1, *SPANS[0], woven1[:])
+        pair_carr = kept([P, 2, P], F32, "pair_carr")
+        part_fetch(2, range(2), pair_carr)
         for i in range(2):
             close(0, i)
-        part_fetch(2)
         late_woven = kept([P, 4 * P], BF16, "late_woven", "diffs1")
         weave(0, diffs[0][:, :, WIDE:], late_woven[:])
         middle_diffs = kept([P, 4, P], F32, "middle_diffs", "woven1")
-        subtract(middle_diffs[:], part_carr[1][:], part_prod[:])
+        subtract(middle_diffs[:], middle_carr[:], part_prod[:])
+        end_carr = kept([P, 2, P], F32, "end_carr", "middle_carr")
+        part_fetch(2, range(2, 4), end_carr)
         quantise_z(0, *SPANS[2], late_woven[:])
         quantise_wr(1, 1, kept([P, PASS], U32, "wr11_codes"))
         for i in range(2, 4):
@@ -432,9 +435,9 @@ def tile_list_spice_substitution_kernel(
         last_diffs = kept([P, 4, P], F32, "last_diffs")
         last_woven = kept([P, 4 * P], BF16, "last_woven")
         halves = [slice(at, at + P // 2) for at in (0, P // 2)]
-        subtract(last_diffs[:, 0:2, :], part_carr[2][:, 0:2, :], part_prod[:, 0:2, :])
+        subtract(last_diffs[:, 0:2, :], pair_carr[:], part_prod[:, 0:2, :])
         for cols in halves:
-            subtract(last_diffs[:, 2:4, cols], part_carr[2][:, 2:4, cols], part_prod[:, 2:4, cols])
+            subtract(last_diffs[:, 2:4, cols], end_carr[:, :, cols], part_prod[:, 2:4, cols])
         for cols in halves:
             weave(1, last_diffs[:, :, cols], last_woven[:, 4 * cols.start : 4 * cols.stop])
         for cols in halves:

from contextlib import ExitStack

import concourse.mybir as mybir

K, H, T, S, M = 1024, 1024, 4096, 1024, 512
FLOPS = 2 * K * H * S + 2 * 2 * H * K * M

F32 = mybir.dt.float32
BF16 = mybir.dt.bfloat16
I32 = mybir.dt.int32
U32 = mybir.dt.uint32
U16 = mybir.dt.uint16
U8 = mybir.dt.uint8
FP8X4 = mybir.dt.float8_e4m3fn_x4
FP4X4 = mybir.dt.float4_e2m1fn_x4
ALU = mybir.AluOpType
ACT = mybir.ActivationFunctionType

P = 128
PASS = 512
BANK = 512
SPANS = ((0, 256), (256, 128), (384, 128))
SPAN_BANKS = (
    ((0, 0, 2), (1, 2, 2), (2, 4, 2), (3, 6, 2)),
    ((6, 0, 4), (7, 4, 4)),
    ((4, 0, 2), (5, 2, 2), (0, 4, 2), (1, 6, 2)),
)
HALF = M // 2
TAB0, TAB1, AFTER = 2 * T, 6 * T, 10 * T + 64


def tile_list_spice_substitution_kernel(
    tc, tab_words, tab_scales, w, c4_words, c4_scales, fade, lift, back, offs, pos1, pos2, pos3, out
):
    nc = tc.nc
    with ExitStack() as ctx:
        keep = ctx.enter_context(tc.tile_pool(name="keep", bufs=1))
        shared = ctx.enter_context(tc.tile_pool(name="shared", bufs=1))
        psum = ctx.enter_context(tc.psum_pool(name="psum", bufs=1))

        def bank(i):
            return psum.tile([P, BANK], F32, name="bank%d" % i, tag="bank%d" % i)

        def kept(shape, dtype, name, tag=None):
            return keep.tile(shape, dtype, name=name, tag=tag or name, align_bytes=64)

        def placed(shape, dtype, name, offset):
            return shared.tile(shape, dtype, name=name, align_bytes=64, offset=offset)

        tab_sc = placed([P, T], U8, "tab_sc", TAB1 + 4 * T - T // 2)
        nc.vector.memset(tab_sc[:].bitcast(I32), 0)
        nc.sync.dma_start(out=tab_sc[0:P:4, :].bitcast(I32), in_=tab_scales.rearrange("a q t -> (a q) t").bitcast(I32))
        fade_in = shared.tile([P, 2, 8], F32, name="fade_in", offset=TAB0 - 32)
        nc.sync.dma_start(out=fade_in[:, :, 0:4], in_=fade.rearrange("(b p t) -> p b t", b=2, t=4))
        fade_sb = kept([P, 8], F32, "fade_sb")
        nc.scalar.copy(out=fade_sb[:].rearrange("p (b t) -> p b t", b=2), in_=fade_in[:, :, 0:4])

        w_raw, tab = {}, {}

        def load_w(a, first, count, tile):
            rows = w[PASS * a : PASS * (a + 1), PASS * first : PASS * (first + count)]
            nc.sync.dma_start(out=tile[:], in_=rows.rearrange("(p i) r -> p i r", i=4))
            for b in range(count):
                w_raw[a, first + b] = tile[:, :, PASS * b : PASS * (b + 1)]

        def load_tab(a, offset):
            tab[a] = placed([P, T], I32, "tab%d" % a, offset)
            nc.sync.dma_start(out=tab[a][:], in_=tab_words[a].rearrange("p t i -> p (t i)").bitcast(I32))

        load_w(0, 0, 2, kept([P, 4, 2 * PASS], F32, "w_upper"))
        offs_sb = keep.tile([P, S // 16], U16, name="offs_sb")
        nc.sync.dma_start(offs_sb[:], offs)
        lists = []
        for i, pos in enumerate((pos1, pos2, pos3)):
            pos_sb = keep.tile([P, M // 16], U16, name="pos_sb%d" % i)
            nc.sync.dma_start(pos_sb[:], pos)
            lists.append(pos_sb)
        zeros = kept([P, P], F32, "zeros")
        nc.gpsimd.memset(zeros[:], 0.0)
        ident = kept([P, P], F32, "ident")
        nc.gpsimd.affine_select(
            out=ident[:], in_=zeros[:], compare_op=ALU.not_equal, fill=1.0, base=0, pattern=[[-1, P]], channel_multiplier=1
        )
        load_w(1, 0, 1, placed([P, 4, PASS], F32, "w_raw10", 0))
        load_tab(0, TAB0)

        wk_codes, wk_sc, wr_codes, wr_sc, grouped, turned = {}, {}, {}, {}, {}, {}

        def group_w(a, b, copy):
            grouped[a, b] = kept([P, 4 * PASS], BF16, "grouped%d%d" % (a, b))
            dst = grouped[a, b][:].rearrange("p (t m i) -> p m i t", t=4, i=4)
            copy(out=dst, in_=w_raw[a, b].rearrange("p i (m t) -> p m i t", t=4))

        def cast_on_scalar(out, in_):
            nc.scalar.activation(out=out, in_=in_, func=ACT.Copy)

        def quantise_wk(a, b):
            wk_codes[a, b] = kept([P, PASS], U32, "wk%d%d_codes" % (a, b))
            wk_sc[a, b] = kept([P, PASS], U8, "wk%d%d_sc" % (a, b))
            nc.vector.quantize_mx(out=wk_codes[a, b][:].bitcast(FP8X4), scales=wk_sc[a, b][:], in_=grouped[a, b][:])

        def turn_w(a, b, first_bank):
            words = grouped[a, b][:].bitcast(F32).rearrange("p (t m u) -> p t m u", t=4, u=2)
            turned[a, b] = kept([P, 4 * PASS], BF16, "turned%d%d" % (a, b))
            for u in range(2):
                ps = bank(first_bank + u)
                for t in range(4):
                    nc.tensor.transpose(ps[:, P * t : P * (t + 1)], words[:, t, :, u], ident[:])
                nc.scalar.copy(
                    out=turned[a, b][:].rearrange("m (p u e t) -> m u p e t", u=2, e=2, t=4)[:, u],
                    in_=ps[:].bitcast(BF16).rearrange("m (t p e) -> m p e t", t=4, e=2),
                )

        def quantise_wr(a, b, codes):
            wr_codes[a, b] = codes
            wr_sc[a, b] = kept([P, PASS], U8, "wr%d%d_sc" % (a, b))
            nc.vector.quantize_mx(out=codes[:].bitcast(FP8X4), scales=wr_sc[a, b][:], in_=turned[a, b][:])

        v_codes = {}
        v_sc = [kept([P, S], U8, "v_sc%d" % a) for a in range(2)]

        def gather_words(a, half):
            v_codes[a, half] = kept([P, BANK], U32, "v%d%d" % (a, half))
            count = BANK // 2 if a == 1 else BANK
            for first in range(0, BANK, count):
                at = (BANK * half + first) // 16
                cols = offs_sb[:, at : at + count // 16]
                nc.vector.tensor_copy(out=v_codes[a, half][:, first : first + count], in_=tab[a][:].bitcast(U32).indirect(cols))

        def place_scales(a):
            for q in range(4):
                first = 4 * (16 * a + 4 * q)
                nc.sync.dma_start(
                    out=v_sc[a][32 * q : 32 * q + 4, :].bitcast(I32),
                    in_=picked_sc[first : first + 16 : 4, :].bitcast(I32),
                )

        early = ((0, 0), (0, 1), (1, 0))
        picked_sc = kept([P, S], U8, "picked_sc")
        nc.vector.tensor_copy(out=picked_sc[:], in_=tab_sc[:].indirect(offs_sb[:]))
        for n, (a, b) in enumerate(early):
            group_w(a, b, cast_on_scalar if n == 0 else nc.vector.tensor_copy)
        for a, b in early:
            quantise_wk(a, b)
        for n, (a, b) in enumerate(early):
            turn_w(a, b, 2 * n)
        place_scales(0)
        load_tab(1, TAB1)
        place_scales(1)
        late_halves = [placed([P, 4, PASS // 2], F32, "w_late%d" % half, (AFTER, 0)[half]) for half in range(2)]
        for half in range(2):
            rows = w[PASS:, PASS + PASS // 2 * half : PASS + PASS // 2 * (half + 1)]
            nc.sync.dma_start(out=late_halves[half][:], in_=rows.rearrange("(p i) r -> p i r", i=4))
        for a in range(2):
            for half in range(2):
                gather_words(a, half)
        for n, (a, b) in enumerate(early):
            quantise_wr(a, b, placed([P, PASS], U32, "wr%d%d_codes" % (a, b), TAB0 + T + 4 * PASS * n))

        lift_sb = placed([P, 2, 4], F32, "lift_sb", TAB1)
        nc.sync.dma_start(out=lift_sb[:], in_=lift.rearrange("(b p t) -> p b t", b=2, t=4))
        c4 = placed([P, 2, 2 * K], U8, "c4", TAB1 + T)
        nc.sync.dma_start(out=c4[:].bitcast(I32), in_=c4_words.rearrange("b p c -> p b c").bitcast(I32))
        c4_sc = placed([P, 2, K], U8, "c4_sc", TAB1 + 2 * T)
        for q in range(4):
            nc.sync.dma_start(
                out=c4_sc[32 * q : 32 * q + 4, :, :].bitcast(I32),
                in_=c4_scales[:, 4 * q : 4 * q + 4, :].rearrange("b r n -> r b n").bitcast(I32),
            )
        back_sb = placed([P, 8], F32, "back_sb", TAB1 + 3 * T)
        with nc.allow_non_contiguous_dma(reason="one factor for each output row"):
            nc.sync.dma_start(out=back_sb[:], in_=back.rearrange("(j p) -> p j", p=P))

        h, h_banks = {}, {}

        def first_pass(k, half, a):
            b, t = divmod(k, 4)
            if a == 0:
                h_banks[k, half] = bank(2 * (k % 4) + half)
            cols = slice(P * t, P * (t + 1))
            nc.tensor.matmul_mx(
                out=h_banks[k, half][:],
                lhsT=wk_codes[a, b][:, cols].bitcast(FP8X4),
                lhsT_scale=wk_sc[a, b][:, cols],
                rhs=v_codes[a, half][:].bitcast(FP8X4),
                rhs_scale=v_sc[a][:, BANK * half : BANK * (half + 1)],
                start=(a == 0),
                stop=(a == 1),
            )

        def quarter_passes(q, a):
            if a == 0:
                h_banks["quarter", q] = bank(q)
            cols = slice(2 * P * q, 2 * P * (q + 1))
            within = slice(2 * P * (q % 2), 2 * P * (q % 2 + 1))
            for k in range(2):
                nc.tensor.matmul_mx(
                    out=h_banks["quarter", q][:, 2 * P * k : 2 * P * (k + 1)],
                    lhsT=wk_codes[a, 0][:, P * k : P * (k + 1)].bitcast(FP8X4),
                    lhsT_scale=wk_sc[a, 0][:, P * k : P * (k + 1)],
                    rhs=v_codes[a, q // 2][:, within].bitcast(FP8X4),
                    rhs_scale=v_sc[a][:, cols],
                    start=(a == 0 and k == 0),
                    stop=(a == 1 and k == 1),
                )

        def finish_quarter(q):
            quarter_passes(q, 1)
            for k in range(2):
                if q == 0:
                    h[k] = kept([P, S], F32, "h%d" % k)
                nc.scalar.copy(out=h[k][:, 2 * P * q : 2 * P * (q + 1)], in_=h_banks["quarter", q][:, 2 * P * k : 2 * P * (k + 1)])

        def finish_h(k, half, copy=nc.scalar.copy):
            first_pass(k, half, 1)
            if half == 0:
                h[k] = kept([P, S], F32, "h%d" % k)
            copy(out=h[k][:, BANK * half : BANK * (half + 1)], in_=h_banks[k, half][:])

        def make_h(k):
            for half in range(2):
                if k >= 4:
                    first_pass(k, half, 0)
                finish_h(k, half)

        def picked(k, which, first, width):
            return h[k][:].indirect(lists[which][:, first // 16 : (first + width) // 16])

        def make_damp(k, first, into, factor):
            nc.scalar.activation(out=into, in_=picked(k, 0, first, HALF), func=ACT.Exp, scale=factor)

        def pick_repl(k, first, width, damp, into):
            nc.vector.tensor_tensor(into, picked(k, 1, first, width), damp, ALU.mult)

        def pick_carr(k, first, width, prod, into):
            nc.vector.tensor_tensor(into, picked(k, 2, first, width), prod, ALU.subtract)

        def fetch_carr(k, first, width, into):
            nc.scalar.activation(out=into, in_=picked(k, 2, first, width), func=ACT.Copy)

        z_codes = [kept([P, M], U32, "z_codes%d" % b) for b in range(2)]
        z_sc = [kept([P, M], U8, "z_sc%d" % b) for b in range(2)]

        def weave(b, diffs, into):
            src = diffs.rearrange("p t (c i) -> p c t i", i=2)
            factor = neg_lift[:, 4 * b : 4 * b + 4].unsqueeze(1).unsqueeze(3).to_broadcast([P, diffs.shape[2] // 2, 4, 2])
            nc.vector.tensor_tensor(into.rearrange("p (c i t) -> p c t i", i=2, t=4), src, factor, ALU.mult)

        def quantise_z(b, first, count, woven):
            cols = slice(first, first + count)
            nc.vector.quantize_mx(out=z_codes[b][:, cols].bitcast(FP8X4), scales=z_sc[b][:, cols], in_=woven)

        sums = {}

        def second_passes(s, i, b):
            first, width = SPANS[s]
            which, j0, per_bank = SPAN_BANKS[s][i]
            if b == 0:
                sums[s, i] = bank(which)
            passes = []
            for e in range(per_bank):
                j = j0 + e
                a, jj = divmod(j, 4)
                n_cols = slice(P * jj, P * (jj + 1))
                passes.append((c4[:, b, 2 * P * j : 2 * P * (j + 1)].bitcast(FP4X4), c4_sc[:, b, P * j : P * (j + 1)], e))
                passes.append((wr_codes[a, b][:, n_cols].bitcast(FP8X4), wr_sc[a, b][:, n_cols], e))
            for n, (codes, scales, e) in enumerate(passes):
                nc.tensor.matmul_mx(
                    out=sums[s, i][:, width * e : width * (e + 1)],
                    lhsT=codes,
                    lhsT_scale=scales,
                    rhs=z_codes[b][:, first : first + width].bitcast(FP8X4),
                    rhs_scale=z_sc[b][:, first : first + width],
                    start=(b == 0 and n == 0),
                    stop=(b == 1 and n == len(passes) - 1),
                )

        def finish(s, i):
            first, width = SPANS[s]
            j0, per_bank = SPAN_BANKS[s][i][1:]
            res = kept([P, per_bank, width], F32, "res%d_%d" % (s, i))
            if s == 2 and i % 2 == 0:
                factor = back_sb[:, j0 : j0 + per_bank].unsqueeze(2).to_broadcast([P, per_bank, width])
                src = sums[s, i][:, 0 : per_bank * width].rearrange("p (e m) -> p e m", e=per_bank)
                nc.vector.tensor_tensor(res[:], src, factor, ALU.mult)
            else:
                for e in range(per_bank):
                    nc.scalar.activation(
                        out=res[:, e, :],
                        in_=sums[s, i][:, width * e : width * (e + 1)],
                        func=ACT.Copy,
                        scale=back_sb[:, j0 + e : j0 + e + 1],
                    )
            rows = out[P * j0 : P * (j0 + per_bank), first : first + width]
            nc.sync.dma_start(out=rows.rearrange("(e p) m -> p e m", p=P), in_=res[:])

        def all_banks(s, b):
            for i in range(len(SPAN_BANKS[s])):
                second_passes(s, i, b)

        def close(s, i):
            second_passes(s, i, 1)
            finish(s, i)

        diffs = [kept([P, 4, (M, HALF)[b]], F32, "diffs%d" % b) for b in range(2)]
        nc.scalar.copy(out=diffs[0][:, 1, 0:1], in_=fade_sb[:, 2:3])
        fade_at = {k: fade_sb[:, k : k + 1] for k in range(8)}
        fade_at[2] = diffs[0][:, 1, 0:1]
        damps = kept([P, 4, M], F32, "damps")
        prods = [placed([P, M], F32, "prods%d" % i, 4 * M * i) for i in range(3)]

        def tile_damp(k, first, width):
            into = damps[:, k % 4, first : first + width]
            nc.scalar.activation(out=into, in_=picked(k, 0, first, width), func=ACT.Exp, scale=fade_at[k])

        def tile_repl(k, first, width):
            cols = slice(first, first + width)
            pick_repl(k, first, width, damps[:, k % 4, cols], prods[k % 3][:, cols])

        def tile_carr(k, first, width):
            cols = slice(first, first + width)
            pick_carr(k, first, width, prods[k % 3][:, cols], diffs[k // 4][:, k % 4, cols])

        for q in range(4):
            quarter_passes(q, 0)
        for k in range(2, 4):
            for half in range(2):
                first_pass(k, half, 0)
        finish_quarter(0)
        for q in range(1, 3):
            finish_quarter(q)
            finish_h(q + 1, 0, nc.vector.tensor_copy)
        finish_quarter(3)
        for k in range(2, 4):
            finish_h(k, 1, nc.vector.tensor_copy)
        grouped[1, 1] = kept([P, 4 * PASS], BF16, "grouped11")
        for half in range(2):
            dst = grouped[1, 1][:].rearrange("p (t m i) -> p m t i", t=4, i=4)[:, P // 2 * half : P // 2 * (half + 1)]
            src = late_halves[half][:].rearrange("p i (m t) -> p m t i", t=4)
            nc.gpsimd.tensor_scalar(out=dst, in0=src, scalar1=1.0, scalar2=0.0, op0=ALU.mult, op1=ALU.add)
        quantise_wk(1, 1)
        for first in (0, HALF):
            tile_damp(0, first, HALF)
            tile_repl(0, first, HALF)
        for first in (0, HALF):
            tile_carr(0, first, HALF)
        tile_damp(1, 0, M)
        tile_repl(1, 0, M)
        neg_lift = kept([P, 8], F32, "neg_lift")
        nc.scalar.activation(out=neg_lift[:], in_=lift_sb[:].rearrange("p b t -> p (b t)"), func=ACT.Copy, scale=-1.0)
        tile_damp(2, 0, M)
        tile_repl(2, 0, M)
        tile_carr(1, 0, M)
        tile_carr(2, 0, M)
        tile_damp(3, 0, M)
        for step in (tile_repl, tile_carr):
            for first in (0, HALF):
                step(3, first, HALF)
        WIDE = SPANS[2][0]
        last_prod = kept([P, 4, HALF], F32, "last_prod")
        last_carr = kept([P, 4, HALF], F32, "last_carr")

        def lower_tile(k):
            make_h(k)
            tile_damp(k, 0, HALF)
            pick_repl(k, 0, HALF, damps[:, k % 4, 0:HALF], last_prod[:, k - 4, :])

        for s in range(2):
            first, width = SPANS[s]
            woven = kept([P, 4 * width], BF16, "woven0%d" % s)
            weave(0, diffs[0][:, :, first : first + width], woven[:])
            lower_tile(4 + s)
            quantise_z(0, first, width, woven[:])
        for k in range(6, 8):
            lower_tile(k)

        right_damp = kept([P, 4, HALF], F32, "right_damp")
        part_prod = kept([P, 4, P], F32, "part_prod")
        middle_carr = kept([P, 4, P], F32, "middle_carr")

        def right_exp(t):
            make_damp(4 + t, HALF, right_damp[:, t, :], fade_sb[:, 4 + t : 5 + t])

        def part_repl(s, t):
            first = SPANS[s][0]
            pick_repl(4 + t, first, P, right_damp[:, t, first - HALF : first - HALF + P], part_prod[:, t, :])

        def part_fetch(s, tiles, into):
            for n, t in enumerate(tiles):
                fetch_carr(4 + t, SPANS[s][0], P, into[:, n, :])

        def subtract(into, carr, prod):
            nc.vector.tensor_tensor(into, carr, prod, ALU.subtract)

        right_exp(0)
        for k in range(4, 8):
            fetch_carr(k, 0, HALF, last_carr[:, k - 4, :])
        for t in range(1, 3):
            right_exp(t)
        part_fetch(1, range(4), middle_carr)
        right_exp(3)
        turn_w(1, 1, 4)
        all_banks(0, 0)
        all_banks(1, 0)
        part_repl(1, 0)
        subtract(diffs[1][:], last_carr[:], last_prod[:])
        for t in range(1, 3):
            part_repl(1, t)
        woven1 = kept([P, 4 * HALF], BF16, "woven1")
        weave(1, diffs[1][:], woven1[:])
        part_repl(1, 3)
        quantise_z(1, *SPANS[0], woven1[:])
        pair_carr = kept([P, 2, P], F32, "pair_carr")
        part_fetch(2, range(2), pair_carr)
        for i in range(2):
            close(0, i)
        late_woven = kept([P, 4 * P], BF16, "late_woven", "diffs1")
        weave(0, diffs[0][:, :, WIDE:], late_woven[:])
        middle_diffs = kept([P, 4, P], F32, "middle_diffs", "woven1")
        subtract(middle_diffs[:], middle_carr[:], part_prod[:])
        end_carr = kept([P, 2, P], F32, "end_carr", "middle_carr")
        part_fetch(2, range(2, 4), end_carr)
        quantise_z(0, *SPANS[2], late_woven[:])
        quantise_wr(1, 1, kept([P, PASS], U32, "wr11_codes"))
        for i in range(2, 4):
            close(0, i)
        middle_woven = kept([P, 4 * P], BF16, "middle_woven")
        weave(1, middle_diffs[:], middle_woven[:])
        quantise_z(1, *SPANS[1], middle_woven[:])
        for i in range(2):
            close(1, i)
        all_banks(2, 0)
        for t in range(4):
            part_repl(2, t)
        last_diffs = kept([P, 4, P], F32, "last_diffs")
        last_woven = kept([P, 4 * P], BF16, "last_woven")
        halves = [slice(at, at + P // 2) for at in (0, P // 2)]
        subtract(last_diffs[:, 0:2, :], pair_carr[:], part_prod[:, 0:2, :])
        for cols in halves:
            subtract(last_diffs[:, 2:4, cols], end_carr[:, :, cols], part_prod[:, 2:4, cols])
        for cols in halves:
            weave(1, last_diffs[:, :, cols], last_woven[:, 4 * cols.start : 4 * cols.stop])
        for cols in halves:
            quantise_z(1, WIDE + cols.start, P // 2, last_woven[:, 4 * cols.start : 4 * cols.stop])
        for i in range(4):
            close(2, i)
